import numpy as np, ml_dtypes
CORES = [16,18,20,22]
N = 4
import mx_ref
BF = ml_dtypes.bfloat16
def entries(a):
    return np.ascontiguousarray(a.T).reshape(-1)
def table(e):
    return np.ascontiguousarray(np.reshape(e, (-1, 16)).T).astype(np.int32)
def pick(q, e):
    c = np.concatenate([q[0].reshape(128, -1, 4), np.zeros((128, 1, 4), np.uint8)], axis=1); s = np.concatenate([q[1], np.ones((16, 1), np.uint8)], axis=1)
    return (np.ascontiguousarray(c[:, e].reshape(128, -1)), np.ascontiguousarray(s[:, e]))
def join(*qs):
    return (np.concatenate([q[0] for q in qs], axis=1), np.concatenate([q[1] for q in qs], axis=1))
def put(q, e, v):
    c, s = q[0].reshape(128, -1, 4).copy(), q[1].copy(); c[:, e] = v[0].reshape(128, -1, 4); s[:, e] = v[1]
    return (c.reshape(128, -1), s)
def pk(c, s):
    return (np.ascontiguousarray(c), mx_ref.live(s))
def emit(q):
    return q[0], q[1]
def decode(q):
    o = []
    for b in range(4):
        e = np.zeros((128, 128, 4), np.float32); e[np.arange(128), np.arange(128), b] = 1
        o.append(mx_ref.matmul(mx_ref.quantize(e.reshape(128, 512).astype(BF)), q))
    return np.stack(o, axis=2).reshape(128, -1)
def cut(t, i, w=512):
    return t[:, w * i:w * i + w]
def f(rng, *shape):
    return mx_ref.flush((rng.standard_normal(shape, dtype=np.float32) * np.exp2(rng.integers(-2, 3, shape[:-1] + (1,)))).astype(BF))
def wide(rng, *shape, cols=0):
    v = rng.standard_normal(shape, dtype=np.float32) * np.exp2(rng.integers(-12, 13, shape)).astype(np.float32)
    if cols: v *= np.repeat(np.exp2(rng.integers(-cols, cols + 1, shape[:-2] + (1, shape[-1] // 4))) * (rng.random(shape[:-2] + (1, shape[-1] // 4)) > 0.0625), 4, axis=-1).astype(np.float32)
    return mx_ref.flush(v.astype(BF))
P, M, A, CAPP, R = 512, 128, 64, 32, 3
def big(v):
    v = v.astype(np.float32)
    v[np.abs(v) < np.float32(2.0 ** -16)] = 0
    return v.astype(BF)
def listed(e):
    return np.stack([table(v) for v in e])
def setup_inputs(rng):
    return {"ky": big(f(rng, N, 128, 4 * P)), "nx": listed(rng.integers(0, N * M, (N, P))), "x": big(f(rng, N, 128, 4 * A)), "st": listed(rng.integers(0, N * M, (N, A))), "w": f(rng, N, 128, 512)}
def setup_inputs_spread(rng):
    d = setup_inputs(rng)
    d["ky"] = big(wide(rng, N, 128, 4 * P, cols=6))
    d["x"] = big(wide(rng, N, 128, 4 * A, cols=4))
    return d
def setup_inputs_ties(rng):
    d = setup_inputs(rng)
    o = np.argsort(rng.random((N, M, 4)), axis=2) % 2
    v = d["ky"].reshape(N, 128, M, 4, 4)
    v = np.ascontiguousarray(np.stack([np.take_along_axis(v[r], np.broadcast_to(o[r][None, :, :, None], (128, M, 4, 4)), axis=2) for r in range(N)]))
    for r in range(N): v[r][:, rng.permutation(M)[:M // 8]] = 0
    d["ky"] = v.reshape(N, 128, 4 * P)
    to = np.argsort(rng.random((N, M, N)), axis=2)[:, :, :4]
    d["nx"] = listed((to * M + rng.integers(0, M, (N, M, 4))).reshape(N, P))
    return d
def setup_inputs_crowd(rng):
    d = setup_inputs(rng)
    o, st = rng.permutation(N), np.zeros((N, A), int)
    for i in range(N):
        s, to = o[i], o[(i + 1) % N]
        here = rng.permutation(A) < (CAPP if i % 2 == 0 else A - CAPP // 4)
        near = to * M + (rng.integers(0, M, A) if i % 2 == 0 else np.full(A, int(rng.integers(0, M))))
        far = (to + rng.integers(1, N, A)) % N * M + rng.integers(0, M, A)
        st[s] = np.where(here, near, far)
    d["st"] = listed(st)
    return d
def kept(rng, *shape):
    return 4 * rng.integers(0, M // 4, shape) + rng.integers(0, 3, shape)
def setup_inputs_stay(rng):
    d = setup_inputs(rng)
    o = rng.permutation(N)
    z, z2 = int(o[0]), int(o[1])
    v = np.arange(M)[None, :, None]
    to = np.arange(N)[:, None, None] * M + np.where(v % 2 == 0, v, kept(rng, N, M, 4))
    to[z, 3::4] = o[rng.integers(2, N, (M // 4, 4))] * M + rng.integers(0, M, (M // 4, 4))
    to[z2] = z * M + kept(rng, M, 4)
    d["nx"] = listed(to.reshape(N, P))
    leave = np.zeros((N, A), bool)
    leave[:, :CAPP] = np.argsort(rng.random((N, CAPP)), axis=1) < CAPP // 4
    st = z * M + np.where(leave, 4 * rng.integers(0, M // 4, (N, A)) + 3, kept(rng, N, A))
    n = CAPP + CAPP // 2
    st[:, n:] = z2 * M + rng.integers(0, M, (N, A - n))
    low = rng.permutation(N) < N // 2
    st[low] = np.roll(st[low], A - n, axis=1)
    d["st"] = listed(st)
    return d
def setup_inputs_turn(rng):
    d = setup_inputs(rng)
    sign = rng.choice([-1.0, 1.0], (128, 4))
    top = np.arange(128) < 64
    o = np.argsort(rng.random((N, M, 4)), axis=2).reshape(N, P)
    g = np.where(top[None, :, None], np.exp2(-2.0 * o)[:, None, :], np.exp2(2.0 * o + 2)[:, None, :])
    d["ky"] = big(((1 + rng.random((N, 128, P, 4))) * g[..., None] * sign[None, :, None, :]).reshape(N, 128, 4 * P))
    d["x"] = big(((1 + rng.random((N, 128, A, 4))) * top[None, :, None, None] * sign[None, :, None, :]).reshape(N, 128, 4 * A))
    return d
def check_inputs(d):
    b = []
    for k, lo, hi in (("ky", -16, 24), ("x", -16, 24), ("w", -30, 30)):
        v = np.abs(d[k].astype(np.float32))
        if not (np.isfinite(v).all() and ((v == 0) | (v >= 2.0 ** lo) & (v <= 2.0 ** hi)).all()): b.append("a value of " + k)
    for k in ("nx", "st"):
        if d[k].min() < 0 or d[k].max() >= N * M: b.append("an entry of " + k)
    return b
def served(node):
    ok = np.zeros(N * A, bool)
    for s in range(N):
        at = node[A * s:A * s + A] // M
        for d in range(N): ok[A * s + np.flatnonzero(at == d)[:CAPP]] = True
    return np.flatnonzero(ok)
def reference(ky, nx, x, st, w):
    pieces = [mx_ref.quantize(np.ascontiguousarray(cut(ky[d], i))) for d in range(N) for i in range(P // 128)]
    dk = decode(join(*pieces)).reshape(128, N * P, 4)
    leads = np.concatenate([entries(nx[d]) for d in range(N)])
    q = join(*[mx_ref.quantize(np.ascontiguousarray(x[s])) for s in range(N)])
    node = np.concatenate([entries(st[s]) for s in range(N)])
    e = np.arange(N * A)
    way = [node]
    for t in range(R):
        go = served(node)
        z = np.concatenate([mx_ref.matmul(p, q) for p in pieces])
        four = 4 * node[:, None] + np.arange(4)
        k = 4 * node + np.argmax(z[four, e[:, None]] + np.float32(0), axis=1)
        v = decode(q).reshape(128, N * A, 4) * np.float32(0.5) + dk[:, k] * np.float32(0.5)
        new = mx_ref.quantize(np.ascontiguousarray(v.reshape(128, -1).astype(BF)))
        q = put(q, go, pick(new, go))
        node = node.copy()
        node[go] = leads[k[go]]
        way.append(node)
    oc, osc = np.zeros((N, 128, 4 * A), np.uint8), np.zeros((N, 16, A), np.uint8)
    nd, y = np.zeros((N, R + 1, A), np.float32), np.zeros((N, 128, A), np.float32)
    for s in range(N):
        own = pick(q, np.arange(A * s, A * s + A))
        oc[s], osc[s] = emit(own)
        nd[s] = np.stack(way)[:, A * s:A * s + A]
        y[s] = mx_ref.matmul(mx_ref.quantize(np.ascontiguousarray(w[s])), own)
    return {"oc": oc, "osc": osc, "nd": nd, "y": y}

@@ -1,0 +1,330 @@
+from concourse.bass import DstId, RemoteDMATransfer
+from concourse.mybir import dt, AluOpType as A, AxisListType, ActivationFunctionType as F
+
+NR, PK, NQ, CAP, HOPS = 4, 512, 64, 32, 3
+BIG = 1e29
+
+SCRATCH = {
+    "STW": ("sbuf", [128, 4], "int32"), "STU": ("sbuf", [128, 4], "uint16"),
+    "NXW": ("sbuf", [128, 32], "int32"), "NXU": ("sbuf", [128, 32], "uint16"), "NXF": ("sbuf", [128, 512], "float32"),
+    "NODEP": ("sbuf", [128, 512], "int32"), "JP": ("sbuf", [128, 128], "int32"), "JPA": ("sbuf", [128, 128], "int32"),
+    "PI": ("sbuf", [128, 8], "int32"), "PJ": ("sbuf", [128, 8], "int32"), "THR": ("sbuf", [128, 8], "float32"),
+    "KP": ("sbuf", [128, 8], "int32"), "KP2": ("sbuf", [128, 8], "int32"), "M8": ("sbuf", [128, 8], "float32"), "NMK": ("sbuf", [128, 8], "float32"),
+    "IO4": ("sbuf", [128, 8], "int32"), "K16": ("sbuf", [128, 8], "int32"), "AW": ("sbuf", [128, 4], "float32"), "IDL": ("sbuf", [128, 2], "uint16"),
+    "NA": ("sbuf", [128, 64], "float32"), "D16": ("sbuf", [128, 128], "float32"), "NM64": ("sbuf", [128, 64], "float32"),
+    "RS64": ("sbuf", [128, 512], "bfloat16"), "RS16": ("sbuf", [128, 128], "float32"),
+    "AL": ("sbuf", [128, 24], "uint16"),
+    "VS": ("sbuf", [128, 24], "uint16"),
+    "VL": ("sbuf", [128, 24], "uint16"),
+    "Z4": ("sbuf", [128, 24], "uint16"),
+    "OU": ("sbuf", [128, 24], "uint16"),
+    "CS": ("sbuf", [128, 24], "uint16"),
+    "CL": ("sbuf", [128, 24], "uint16"),
+    "SL": ("sbuf", [128, 24], "uint16"),
+    "BT": ("sbuf", [128, 64], "int32"), "MK": ("sbuf", [128, 256], "bfloat16"), "PX": ("sbuf", [128, 256], "bfloat16"),
+    "CN": ("sbuf", [128, 512], "bfloat16"), "SC": ("sbuf", [128, 512], "bfloat16"),
+    "VT": ("sbuf", [128, 64], "int32"), "VD": ("sbuf", [128, 128], "float32"), "VE": ("sbuf", [128, 128], "float32"),
+    "UU": ("sbuf", [128, 256], "bfloat16"), "U2": ("sbuf", [128, 128], "bfloat16"), "PP": ("sbuf", [128, 64], "float32"), "SV": ("sbuf", [128, 64], "float32"),
+    "Q1": ("sbuf", [128, 64], "float32"), "Q2": ("sbuf", [128, 64], "float32"), "Q3": ("sbuf", [128, 64], "float32"), "Q4": ("sbuf", [128, 64], "float32"),
+    "Q5": ("sbuf", [128, 64], "float32"), "Q6": ("sbuf", [128, 64], "float32"), "Q7": ("sbuf", [128, 4], "float32"),
+    "ND": ("sbuf", [128, 256], "float32"),
+    "V4": ("sbuf", [128, 48], "float32"), "T8": ("sbuf", [128, 8], "float32"), "ZS": ("sbuf", [128, 512], "float32"),
+    "T64": ("sbuf", [128, 64], "float32"), "RM": ("sbuf", [128, 64], "float32"),
+    "XS": ("sbuf", [128, 512], "bfloat16"), "OF": ("sbuf", [128, 8], "float32"), "LD": ("sbuf", [128, 128], "float32"), "LE": ("sbuf", [128, 128], "float32"),
+    "HT": ("sbuf", [128, 512], "bfloat16"),
+    "XT": ("sbuf", [128, 512], "bfloat16"), "KT": ("sbuf", [128, 2048], "bfloat16"), "WT": ("sbuf", [128, 512], "bfloat16"),
+    "ET": ("sbuf", [128, 2048], "bfloat16"), "ST": ("sbuf", [128, 512], "bfloat16"), "YS": ("sbuf", [128, 64], "float32"),
+    "pv": ("psum", [128, 2048], "float32"), "pz": ("psum", [128, 1024], "float32"), "px": ("psum", [128, 512], "float32"), "py": ("psum", [128, 512], "float32"),
+}
+
+
+def _codes(name, n):
+    SCRATCH["c" + name] = ("sbuf", [128, n], "float8_e4m3fn_x4")
+    SCRATCH["s" + name] = ("sbuf", [128, n], "uint8")
+
+
+for _n, _w in (("KQ", 512), ("EQ", 512), ("SQ", 128), ("WQ", 128), ("XQ", 128), ("HQ3", 128)):
+    _codes(_n, _w)
+for _t in range(HOPS):
+    for _n, _w in (("HQ", 128), ("SD", 96), ("LA", 128), ("KC", 128), ("NW", 128), ("RW", 192)):
+        _codes(_n + str(_t), _w)
+for _t in range(HOPS + 1):
+    SCRATCH["NN%d" % _t] = ("sbuf", [128, 192], "int32")
+SEMAPHORES = ["cv", "cs", "ct", "cg", "ls", "dst", "dx", "dnx", "dky", "dw", "dh3", "dout"]
+for _t in range(HOPS):
+    SEMAPHORES += ["aq%d" % _t, "av%d" % _t, "rq%d" % _t, "rc%d" % _t, "dh%d" % _t]
+
+
+def rank_program(g, core, T, topo):
+    me = T.rank_of(core)
+    if me is None:
+        return
+    cores = list(T.cores)
+    eng = {"v": g.vector, "s": g.scalar, "t": g.tensor, "g": g, "y": g.sync}
+    count = {}
+    known = {q: {} for q in eng}
+    seen = {}
+
+    def need(q, deps):
+        for d in deps:
+            if d is None:
+                continue
+            sem, val = d
+            if known[q].get(sem, 0) >= val:
+                continue
+            eng[q].wait_ge(T.sem[sem], int(val))
+            known[q][sem] = val
+            for k, w in seen.get(d, {}).items():
+                if known[q].get(k, 0) < w:
+                    known[q][k] = w
+
+    def done(q, ins, sem, n):
+        count[sem] = count.get(sem, 0) + n
+        ins.then_inc(T.sem[sem], n)
+        tok = (sem, count[sem])
+        seen[tok] = dict(known[q])
+        return tok
+
+    v = g.vector
+    getv = {"copy": v.tensor_copy, "tt": v.tensor_tensor, "ts": v.tensor_scalar, "red": v.tensor_reduce, "scan": v.tensor_tensor_scan,
+            "set": v.memset, "q": v.quantize_mx}
+
+    def V(name, deps, *args):
+        need("v", deps)
+        return done("v", getv[name](*args), "cv", 1)
+
+    def S(out, in_, deps):
+        need("s", deps)
+        return done("s", g.scalar.activation(out, in_, F.Copy), "cs", 1)
+
+    def MM(out, lc, ls, rc, rs, start, stop, deps):
+        need("t", deps)
+        return done("t", g.tensor.matmul_mx(out, lc, ls, rc, rs, start, stop), "ct", 1)
+
+    def DMA(q, sem, out, in_, deps=()):
+        need(q, deps)
+        return done(q, eng[q].dma_start(out, in_), sem, 16)
+
+    def IOTA(out, pattern, base, cm, f32=False):
+        if f32:
+            return done("g", g.iota(out, pattern, base, cm, allow_small_or_imprecise_dtypes=True), "cg", 1)
+        return done("g", g.iota(out, pattern, base, cm), "cg", 1)
+
+    peers = [(me + 1 + b) % NR for b in range(NR - 1)]
+
+    def send(remote_sem, views, deps):
+        need("g", deps)
+        tr, total = [], 0
+        for b, r in enumerate(peers):
+            dst = cores[r]
+            e = topo.engines(core, dst)
+            k = len(e) // 4
+            use = e[k * b:k * b + k]
+            m = 0
+            for i in use:
+                m |= 1 << i
+            rid, pid, _ = topo.addr(dst)
+            o, i = views(b, (me - r - 1) % NR)
+            tr.append(RemoteDMATransfer(dst_ids=[DstId(rid=rid, pnc=pid)], dma_engine_mask=m, remote_sem=T.sem[remote_sem], src=i, dst=o))
+            total += len(use)
+        g.remote_dma_fused(tr, local_sem=T.sem.ls)
+        count["ls"] = count.get("ls", 0) + total
+
+    SENT = sum(len(topo.engines(core, cores[r])) // 4 for r in peers)
+
+    def by(x, a, b):
+        return x[:, a:b].bitcast(dt.uint8)
+
+    def wd(x, a, b):
+        return x[:, a:b].bitcast(dt.uint32)
+
+    def L(name, t, a, b, step=1):
+        return T[name][:, 8 * t + a:8 * t + b:step]
+
+    off = 128 * (NR - 1 - me)
+
+    for k in range(8):
+        d_st = DMA("y" if k % 2 == 0 else "s", "dst", T.STW[16 * k:16 * k + 16, 0:4], T.st[:, :])
+    d_x = DMA("y", "dx", T.XT[:, 0:256], T.x[:, :])
+    d_ky = DMA("s", "dky", T.KT[:, 0:1024], T.ky[:, 0:1024])
+    d_ky = DMA("y", "dky", T.KT[:, 1024:2048], T.ky[:, 1024:2048])
+    for k in range(8):
+        d_nx = DMA("y", "dnx", T.NXW[16 * k:16 * k + 16, 0:32], T.nx[:, :])
+    d_w = DMA("y", "dw", T.WT[:, :], T.w[:, :])
+
+    i_pi = IOTA(T.PI[:, 0:1], [[0, 1]], 0, 1)
+    i_jp = IOTA(T.JP[:, :], [[1, 128]], 0, -1)
+    i_np = IOTA(T.NODEP[:, :], [[1, 512]], off, 0)
+    i_kp = IOTA(T.KP[:, :], [[-16, 8]], 0, 1)
+    i_k16 = IOTA(T.K16[:, 0:4], [[16, 4]], 0, 0)
+    i_io4 = IOTA(T.IO4[:, 0:4], [[1, 4]], 0, 0)
+    i_na = IOTA(T.NA[:, :], [[-1, 64]], -129, 0, True)
+
+    m_rs = V("set", [], T.RS64[:, :], 1.0)
+    m_r16 = V("set", [], T.RS16[:, :], 1.0)
+    m_e = V("set", [], T.ET[:, :], 0.0)
+    m_rs = V("set", [m_rs], T.RS64[:, 0:512:64], 0.0)
+    m_r16 = V("set", [m_r16], T.RS16[:, 0:128:16], 0.0)
+    m_xs = V("set", [], T.XS[:, :], 0.0)
+    m_xt = V("set", [], T.XT[:, 256:512], 0.0)
+    k_pj = V("ts", [i_pi], T.PJ[:, 0:1], T.PI[:, 0:1], 15, None, A.bitwise_and)
+    k_jpa = V("ts", [i_jp], T.JPA[:, :], T.JP[:, :], 15, None, A.bitwise_and)
+    k_t0 = V("ts", [k_pj], T.THR[:, 0:1], T.PJ[:, 0:1], 0.0, None, A.add)
+    k_t1 = V("ts", [k_pj], T.THR[:, 1:2], T.PJ[:, 0:1], 16.0, None, A.add)
+    k_d16 = V("ts", [k_jpa], T.D16[:, :], T.JPA[:, :], 0.0, None, A.is_equal)
+    for b in range(4):
+        k_e = V("ts", [m_e, i_jp], T.ET[:, 512 * b + b:512 * b + 512:4], T.JP[:, :], 0.0, 0.5, A.is_equal, A.mult)
+    for b in range(4):
+        k_s = V("ts", [k_jpa], T.ST[:, b:512:4], T.JPA[:, :], 0.0, None, A.is_equal)
+
+    k_st = V("copy", [d_st], T.STU[:, :], T.STW[:, :])
+    node = V("copy", [k_st, i_np], T.NN0[:, 128:192], T.NODEP[:, 0:512].indirect(T.STU[:, 0:4]))
+
+    def lists(t, node):
+        bt = V("ts", [node], T.BT[:, :], T["NN%d" % t][:, 128:192], 7, 3, A.logical_shift_right, A.bitwise_and)
+        for b in range(4):
+            mk = V("ts", [bt], T.MK[:, 64 * b:64 * b + 64], T.BT[:, :], float(b), None, A.is_equal)
+        px = V("scan", [mk, m_rs], T.PX[:, :], T.RS64[:, 0:256], T.MK[:, :], 0.0, A.mult, A.add)
+        cn = V("ts", [px, k_t0], T.CN[:, 0:256], T.PX[:, :], T.THR[:, 0:1], None, A.is_le)
+        cn = V("ts", [px, k_t1], T.CN[:, 256:512], T.PX[:, :], T.THR[:, 1:2], None, A.is_le)
+        sc = V("scan", [cn], T.SC[:, :], T.RS64[:, :], T.CN[:, :], 0.0, A.mult, A.add)
+        for h in range(2):
+            al = V("ts", [sc], L("AL", t, h, 8, 2), T.SC[:, 256 * h + 63:256 * h + 256:64], 63.0, None, A.min)
+        return al
+
+    def sendpicks(t, al, hq):
+        c, s = T["cHQ%d" % t], T["sHQ%d" % t]
+        p1 = V("copy", [al] + hq, wd(T["cSD%d" % t], 0, 96), wd(c, 0, 64).indirect(L("AL", t, 0, 6)))
+        p2 = S(T["sSD%d" % t][:, 0:96], s[:, 0:64].indirect(L("AL", t, 0, 6)), [al] + hq)
+        send("aq%d" % t, lambda b, b2: (by(T["cLA%d" % t], 32 * b2, 32 * b2 + 32), by(T["cSD%d" % t], 32 * b, 32 * b + 32)), [p1])
+        send("aq%d" % t, lambda b, b2: (T["sLA%d" % t][:, 32 * b2:32 * b2 + 32], T["sSD%d" % t][:, 32 * b:32 * b + 32]), [p2])
+        o1 = V("copy", [al] + hq, wd(T["cLA%d" % t], 96, 128), wd(c, 0, 64).indirect(L("AL", t, 6, 8)))
+        o2 = S(T["sLA%d" % t][:, 96:128], s[:, 0:64].indirect(L("AL", t, 6, 8)), [al] + hq)
+        DMA("y", "dh%d" % t, by(T["cRW%d" % t], 128, 192), by(c, 0, 64), hq)
+        dh = DMA("y", "dh%d" % t, T["sRW%d" % t][:, 128:192], s[:, 0:64], hq)
+        return [o1, o2], dh
+
+    def nodelist(t, al, node):
+        vt = V("ts", [node], T.VT[:, :], T["NN%d" % t][:, 128:192], 127, None, A.bitwise_and)
+        vd = V("tt", [vt, al, k_d16], T.VD[:, :], T.VT[:, 0:64].indirect(L("AL", t, 0, 8)), T.D16[:, :], A.mult)
+        ve = V("scan", [vd, m_r16], T.VE[:, :], T.RS16[:, :], T.VD[:, :], 0.0, A.mult, A.add)
+        vs = V("copy", [ve], L("VS", t, 0, 8), T.VE[:, 15:128:16])
+        send("av%d" % t, lambda b, b2: (L("VL", t, 2 * b2, 2 * b2 + 2), L("VS", t, 2 * b, 2 * b + 2)), [vs])
+        return vs
+
+    def server(t, own, vs, prev):
+        KQ, sKQ = T.cKQ, T.sKQ
+        LA, sLA = T["cLA%d" % t], T["sLA%d" % t]
+        land = [("aq%d" % t, 2 * SENT)] + own
+        z0 = MM(T.pz[:, 0:256], LA[:, 0:128], sLA[:, 0:128], KQ[:, 0:256], sKQ[:, 0:256], True, True, land + [K["kq"]] + prev["z"])
+        z1 = MM(T.pz[:, 512:768], LA[:, 0:128], sLA[:, 0:128], KQ[:, 256:512], sKQ[:, 256:512], True, True, [])
+        for b in range(4):
+            MM(T.pv[:, 512 * b:512 * b + 128], T.cEQ[:, 128 * b:128 * b + 128], T.sEQ[:, 128 * b:128 * b + 128],
+               LA[:, 0:128], sLA[:, 0:128], True, False, [K["eq"]] + prev["pv"])
+        w = 16 * t
+        a = V("ts", [vs], T.V4[:, w + 6:w + 8], L("VS", t, 6, 8), 4.0, None, A.mult)
+        a2 = V("ts", [("av%d" % t, SENT)], T.V4[:, w:w + 6], L("VL", t, 0, 6), 4.0, None, A.mult)
+        b8 = V("tt", [a, a2, K["m8"]], T.T8[:, :], T.V4[:, w:w + 8], T.M8[:, :], A.mult)
+        vp = V("red", [b8], T.V4[:, w + 8:w + 9], T.T8[:, :], AxisListType.X, A.add)
+        z4 = V("ts", [vp, i_io4], L("Z4", t, 0, 4), T.IO4[:, 0:4], T.V4[:, w + 8:w + 9], None, A.add)
+        c1 = S(T.ZS[:, 256:512], T.pz[:, 512:768], [z1] + prev["zs"])
+        c0 = V("copy", [z0], T.ZS[:, 0:256], T.pz[:, 0:256])
+        t64 = V("tt", [c0, c1, z4, K["nm"]], T.T64[:, :], T.ZS[:, 0:512].indirect(L("Z4", t, 0, 4)), T.NM64[:, :], A.add)
+        rm = V("scan", [t64], T.RM[:, :], T.T64[:, :], T.T64[:, :], -BIG, A.max, A.max)
+        for u in range(3):
+            xs = V("ts", [rm, m_xs, K["m8"]], T.XS[:, u:32:4], T.NMK[:, :], T.RM[:, 16 * u + 15:16 * u + 16], T.RM[:, 63:64], A.add, A.is_lt)
+        xq = V("q", [xs, prev["xm"]], T.cXQ[:, 0:128], T.sXQ[:, 0:128], T.XS[:, :])
+        xm = MM(T.px[:, 0:128], T.cSQ[:, 0:128], T.sSQ[:, 0:128], T.cXQ[:, 0:128], T.sXQ[:, 0:128], True, True, [xq, K["sq"], prev["of"]])
+        of = V("tt", [xm, a, a2], T.OF[:, :], T.px[:, 0:8], T.V4[:, w:w + 8], A.add)
+        ou = V("copy", [of], L("OU", t, 0, 8), T.OF[:, :])
+        kc = V("copy", [ou, K["kq"]], wd(T["cKC%d" % t], 0, 128), wd(KQ, 0, 512).indirect(L("OU", t, 0, 8)))
+        ks = S(T["sKC%d" % t][:, 0:128], sKQ[:, 0:512].indirect(L("OU", t, 0, 8)), [ou, K["kq"]])
+        km = [MM(T.pv[:, 512 * b:512 * b + 128], T.cEQ[:, 128 * b:128 * b + 128], T.sEQ[:, 128 * b:128 * b + 128],
+                 T["cKC%d" % t][:, 0:128], T["sKC%d" % t][:, 0:128], False, True, [kc, ks]) for b in range(4)]
+        ld = V("tt", [ou, K["nx"], k_d16], T.LD[:, :], T.NXF[:, 0:512].indirect(L("OU", t, 0, 8)), T.D16[:, :], A.mult)
+        le = V("scan", [ld, m_r16], T.LE[:, :], T.RS16[:, :], T.LD[:, :], 0.0, A.mult, A.add)
+        cs = V("copy", [le], L("CS", t, 0, 8), T.LE[:, 15:128:16])
+        send("rc%d" % t, lambda b, b2: (L("CL", t, 2 * b2, 2 * b2 + 2), L("CS", t, 2 * b, 2 * b + 2)), [cs])
+        h = []
+        for b in (1, 3):
+            h.append(S(T.HT[:, b:512:4], T.pv[:, 512 * b:512 * b + 128], [km[b], prev["nq"]]))
+        for b in (0, 2):
+            h.append(V("copy", [km[b], prev["nq"]], T.HT[:, b:512:4], T.pv[:, 512 * b:512 * b + 128]))
+        C, P = T["cNW%d" % t], T["sNW%d" % t]
+        nq = V("q", h, C[:, 0:128], P[:, 0:128], T.HT[:, :])
+        send("rq%d" % t, lambda b, b2: (by(T["cRW%d" % t], 32 * b2, 32 * b2 + 32), by(C, 32 * b, 32 * b + 32)), [nq])
+        send("rq%d" % t, lambda b, b2: (T["sRW%d" % t][:, 32 * b2:32 * b2 + 32], P[:, 32 * b:32 * b + 32]), [])
+        w1 = V("copy", [nq, K["id"]], wd(T["cRW%d" % t], 96, 128), wd(C, 96, 128).indirect(T.IDL[:, 0:2]))
+        w2 = S(T["sRW%d" % t][:, 96:128], P[:, 96:128].indirect(T.IDL[:, 0:2]), [nq, K["id"]])
+        prev.update({"z": [c0, c1], "pv": h, "zs": [t64], "xm": xm, "of": of, "nq": nq})
+        return [w1, w2], cs
+
+    def where(t):
+        u = V("tt", [], T.UU[:, :], T.PX[:, :], T.MK[:, :], A.mult)
+        q1 = V("ts", [], T.Q1[:, :], T.BT[:, :], 32.0, None, A.mult)
+        u = V("tt", [u], T.U2[:, :], T.UU[:, 0:128], T.UU[:, 128:256], A.add)
+        q2 = V("tt", [q1, i_na], T.Q2[:, :], T.Q1[:, :], T.NA[:, :], A.add)
+        p = V("tt", [u], T.PP[:, :], T.U2[:, 0:64], T.U2[:, 64:128], A.add)
+        sv = V("ts", [p], T.SV[:, :], T.PP[:, :], float(CAP), None, A.is_le)
+        q3 = V("tt", [q2, p], T.Q3[:, :], T.Q2[:, :], T.PP[:, :], A.add)
+        q4 = V("tt", [sv], T.Q4[:, :], T.SV[:, :], T.D16[:, 0:64], A.mult)
+        q5 = V("tt", [q3, q4], T.Q5[:, :], T.Q3[:, :], T.Q4[:, :], A.mult)
+        q6 = V("scan", [q5], T.Q6[:, :], T.RS16[:, 0:64], T.Q5[:, :], 0.0, A.mult, A.add)
+        q7 = V("tt", [q6, K["aw"]], T.Q7[:, :], T.Q6[:, 15:64:16], T.AW[:, :], A.add)
+        return V("copy", [q7], L("SL", t, 0, 4), T.Q7[:, :])
+
+    def walk(t, cs, sl, node):
+        n = T["NN%d" % t]
+        g1 = V("copy", [cs], n[:, 96:128], T.NODEP[:, 0:512].indirect(L("CS", t, 6, 8)))
+        g2 = V("copy", [("rc%d" % t, SENT)], n[:, 0:96], T.NODEP[:, 0:512].indirect(L("CL", t, 0, 6)))
+        return V("copy", [g1, g2, sl, node], T["NN%d" % (t + 1)][:, 128:192], n[:, 0:192].indirect(L("SL", t, 0, 4)))
+
+    def order(t, sl, own, dh):
+        deps = own + [sl, dh, ("rq%d" % t, 2 * SENT)]
+        c, s = T["cHQ%d" % (t + 1)], T["sHQ%d" % (t + 1)]
+        h2 = S(s[:, 0:64], T["sRW%d" % t][:, 0:192].indirect(L("SL", t, 0, 4)), deps)
+        h1 = V("copy", deps, wd(c, 0, 64), wd(T["cRW%d" % t], 0, 192).indirect(L("SL", t, 0, 4)))
+        return [h1, h2]
+
+    K = {}
+    prev = {"z": [], "pv": [], "zs": [], "xm": None, "of": None, "nq": None}
+    al = lists(0, node)
+    hq0 = hq = [V("q", [d_x, m_xt], T.cHQ0[:, 0:128], T.sHQ0[:, 0:128], T.XT[:, :])]
+    for t in range(HOPS):
+        own, dh = sendpicks(t, al, hq)
+        vs = nodelist(t, al, node)
+        if t == 0:
+            k_kp = V("ts", [i_kp], T.KP2[:, :], T.KP[:, :], 4, None, A.arith_shift_right)
+            K["nm"] = V("ts", [k_d16], T.NM64[:, :], T.D16[:, 0:64], -1.0, BIG, A.add, A.mult)
+            V("ts", [k_kp], T.M8[:, :], T.KP2[:, :], 0.0, None, A.is_equal)
+            K["m8"] = V("ts", [k_kp], T.NMK[:, :], T.KP2[:, :], 0.0, BIG, A.not_equal, A.mult)
+            K["sq"] = V("q", [k_s], T.cSQ[:, 0:128], T.sSQ[:, 0:128], T.ST[:, :])
+            K["eq"] = V("q", [k_e], T.cEQ[:, 0:512], T.sEQ[:, 0:512], T.ET[:, :])
+            K["kq"] = V("q", [d_ky], T.cKQ[:, 0:512], T.sKQ[:, 0:512], T.KT[:, :])
+            k_nu = V("copy", [d_nx], T.NXU[:, :], T.NXW[:, :])
+            K["nx"] = V("ts", [k_nu, i_np], T.NXF[:, :], T.NODEP[:, 0:512].indirect(T.NXU[:, 0:32]), float(-off), None, A.add)
+            K["id"] = V("ts", [k_t0, i_k16], T.IDL[:, :], T.K16[:, 0:2], T.THR[:, 0:1], None, A.add)
+            K["aw"] = V("ts", [k_t0, i_k16], T.AW[:, :], T.K16[:, 0:4], T.THR[:, 0:1], 128.0, A.add, A.add)
+            DMA("y", "dh3", by(T.cHQ3, 64, 128), by(T.cHQ0, 64, 128), hq0)
+            d_h3 = DMA("y", "dh3", T.sHQ3[:, 64:128], T.sHQ0[:, 64:128], hq0)
+        own, cs = server(t, own, vs, prev)
+        sl = where(t)
+        if t == 0:
+            K["wq"] = V("q", [d_w], T.cWQ[:, 0:128], T.sWQ[:, 0:128], T.WT[:, :])
+        V("ts", [node], T.ND[:, 64 * t:64 * t + 64], T["NN%d" % t][:, 128:192], float(-off), None, A.add)
+        node = walk(t, cs, sl, node)
+        if t + 1 < HOPS:
+            al = lists(t + 1, node)
+        else:
+            nd = V("ts", [node], T.ND[:, 64 * HOPS:64 * HOPS + 64], T["NN%d" % HOPS][:, 128:192], float(-off), None, A.add)
+            DMA("y", "dout", T.nd[:, :], T.ND[0:1, 0:256], [nd])
+        hq = order(t, sl, own, dh)
+
+    DMA("y", "dout", T.oc[:, :], by(T.cHQ3, 0, 64), [hq[0]])
+    for k in range(4):
+        DMA("s" if k < 2 else "y", "dout", T.osc[4 * k:4 * k + 4, 0:64], T.sHQ3[32 * k:32 * k + 4, 0:64], [hq[1]])
+    ym = MM(T.py[:, 0:128], T.cWQ[:, 0:128], T.sWQ[:, 0:128], T.cHQ3[:, 0:128], T.sHQ3[:, 0:128], True, True, hq + [K["wq"], d_h3])
+    yc = V("copy", [ym], T.YS[:, :], T.py[:, 0:64])
+    DMA("y", "dout", T.y[:, :], T.YS[:, :], [yc])
+    for sem in ("dout", "ls", "cv", "cs", "ct", "cg", "dst", "dx", "dky", "dnx", "dw", "dh3", "dh0", "dh1", "dh2"):
+        need("g", [(sem, count[sem])])

@@ -1,24 +1,25 @@
 from concourse.bass import DstId, RemoteDMATransfer
 from concourse.mybir import dt, AluOpType as A, AxisListType, ActivationFunctionType as F
 
-NR, PK, NQ, CAP, HOPS = 4, 512, 64, 32, 3
+NR, CAP, HOPS = 4, 32, 3
 BIG = 1e29
+SINGLE = True
 
 SCRATCH = {
     "STW": ("sbuf", [128, 4], "int32"), "STU": ("sbuf", [128, 4], "uint16"),
-    "NXW": ("sbuf", [128, 32], "int32"), "NXU": ("sbuf", [128, 32], "uint16"), "NXF": ("sbuf", [128, 512], "float32"),
-    "NODEP": ("sbuf", [128, 512], "int32"), "JP": ("sbuf", [128, 128], "int32"), "JPA": ("sbuf", [128, 128], "int32"),
+    "NXD": ("dram", [128, 4], "int32"), "NXR0": ("dram", [128, 4], "int32"), "NXR1": ("dram", [128, 4], "int32"), "NXR2": ("dram", [128, 4], "int32"),
+    "NXW": ("sbuf", [128, 128], "int32"), "NXU": ("sbuf", [128, 128], "uint16"), "NXA": ("sbuf", [128, 2048], "float32"),
+    "NODF": ("sbuf", [128, 512], "float32"), "JP": ("sbuf", [128, 128], "int32"), "JPA": ("sbuf", [128, 128], "int32"),
     "PI": ("sbuf", [128, 8], "int32"), "PJ": ("sbuf", [128, 8], "int32"), "THR": ("sbuf", [128, 8], "float32"),
     "KP": ("sbuf", [128, 8], "int32"), "KP2": ("sbuf", [128, 8], "int32"), "M8": ("sbuf", [128, 8], "float32"), "NMK": ("sbuf", [128, 8], "float32"),
     "IO4": ("sbuf", [128, 8], "int32"), "K16": ("sbuf", [128, 8], "int32"), "AW": ("sbuf", [128, 4], "float32"), "IDL": ("sbuf", [128, 2], "uint16"),
     "NA": ("sbuf", [128, 64], "float32"), "D16": ("sbuf", [128, 128], "float32"), "NM64": ("sbuf", [128, 64], "float32"),
     "RS64": ("sbuf", [128, 512], "bfloat16"), "RS16": ("sbuf", [128, 128], "float32"),
     "AL": ("sbuf", [128, 24], "uint16"),
-    "VS": ("sbuf", [128, 24], "uint16"),
-    "VL": ("sbuf", [128, 24], "uint16"),
+    "VS": ("sbuf", [128, 24], "int32"),
+    "VL": ("sbuf", [128, 24], "int32"),
     "Z4": ("sbuf", [128, 24], "uint16"),
     "OU": ("sbuf", [128, 24], "uint16"),
-    "CS": ("sbuf", [128, 24], "uint16"),
     "CL": ("sbuf", [128, 24], "uint16"),
     "SL": ("sbuf", [128, 24], "uint16"),
     "BT": ("sbuf", [128, 64], "int32"), "MK": ("sbuf", [128, 256], "bfloat16"), "PX": ("sbuf", [128, 256], "bfloat16"),
@@ -28,10 +29,9 @@ SCRATCH = {
     "Q1": ("sbuf", [128, 64], "float32"), "Q2": ("sbuf", [128, 64], "float32"), "Q3": ("sbuf", [128, 64], "float32"), "Q4": ("sbuf", [128, 64], "float32"),
     "Q5": ("sbuf", [128, 64], "float32"), "Q6": ("sbuf", [128, 64], "float32"), "Q7": ("sbuf", [128, 4], "float32"),
     "ND": ("sbuf", [128, 256], "float32"),
-    "V4": ("sbuf", [128, 48], "float32"), "T8": ("sbuf", [128, 8], "float32"), "ZS": ("sbuf", [128, 512], "float32"),
+    "VP": ("sbuf", [128, 8], "float32"), "T8": ("sbuf", [128, 8], "float32"), "ZS": ("sbuf", [128, 512], "float32"),
     "T64": ("sbuf", [128, 64], "float32"), "RM": ("sbuf", [128, 64], "float32"),
-    "XS": ("sbuf", [128, 512], "bfloat16"), "OF": ("sbuf", [128, 8], "float32"), "LD": ("sbuf", [128, 128], "float32"), "LE": ("sbuf", [128, 128], "float32"),
-    "HT": ("sbuf", [128, 512], "bfloat16"),
+    "XS": ("sbuf", [128, 512], "bfloat16"), "OF": ("sbuf", [128, 8], "float32"), "HT": ("sbuf", [128, 512], "bfloat16"),
     "XT": ("sbuf", [128, 512], "bfloat16"), "KT": ("sbuf", [128, 2048], "bfloat16"), "WT": ("sbuf", [128, 512], "bfloat16"),
     "ET": ("sbuf", [128, 2048], "bfloat16"), "ST": ("sbuf", [128, 512], "bfloat16"), "YS": ("sbuf", [128, 64], "float32"),
     "pv": ("psum", [128, 2048], "float32"), "pz": ("psum", [128, 1024], "float32"), "px": ("psum", [128, 512], "float32"), "py": ("psum", [128, 512], "float32"),
@@ -50,7 +50,7 @@ for _t in range(HOPS):
         _codes(_n + str(_t), _w)
 for _t in range(HOPS + 1):
     SCRATCH["NN%d" % _t] = ("sbuf", [128, 192], "int32")
-SEMAPHORES = ["cv", "cs", "ct", "cg", "ls", "dst", "dx", "dnx", "dky", "dw", "dh3", "dout"]
+SEMAPHORES = ["cv", "cs", "ct", "cg", "ls", "dst", "dx", "dnx", "dnd", "nxr", "dky", "dw", "dh3", "dout"]
 for _t in range(HOPS):
     SEMAPHORES += ["aq%d" % _t, "av%d" % _t, "rq%d" % _t, "rc%d" % _t, "dh%d" % _t]
 
@@ -112,28 +112,58 @@ def rank_program(g, core, T, topo):
 
     peers = [(me + 1 + b) % NR for b in range(NR - 1)]
 
-    def send(remote_sem, views, deps):
-        need("g", deps)
-        tr, total = [], 0
-        for b, r in enumerate(peers):
-            dst = cores[r]
-            e = topo.engines(core, dst)
-            k = len(e) // 4
-            use = e[k * b:k * b + k]
-            m = 0
-            for i in use:
-                m |= 1 << i
-            rid, pid, _ = topo.addr(dst)
-            o, i = views(b, (me - r - 1) % NR)
-            tr.append(RemoteDMATransfer(dst_ids=[DstId(rid=rid, pnc=pid)], dma_engine_mask=m, remote_sem=T.sem[remote_sem], src=i, dst=o))
-            total += len(use)
-        g.remote_dma_fused(tr, local_sem=T.sem.ls)
-        count["ls"] = count.get("ls", 0) + total
+    def plan(s):
+        others = sorted((r for r in range(NR) if r != s), key=lambda r: (topo.die(cores[r]) != topo.die(cores[s]), (r - s) % NR))
+        e = topo.engines(cores[s], cores[others[0]])
+        q = len(e) // 4
+        return {others[0]: (e[:q], e[:2 * q]), others[1]: (e[q:2 * q], e[3 * q:]), others[2]: (e[2 * q:], e[2 * q:3 * q])}
 
-    SENT = sum(len(topo.engines(core, cores[r])) // 4 for r in peers)
+    def bits(es):
+        m = 0
+        for i in es:
+            m |= 1 << i
+        return m
+
+    def coreid(r):
+        rid, pid, _ = topo.addr(cores[r])
+        return DstId(rid=rid, pnc=pid)
+
+    mine = plan(me)
+    IN = [sum(len(plan(r)[me][i]) for r in peers) for i in range(2)]
+    BOTH = 15 if SINGLE else sum(IN)
+
+    def fused(tr):
+        g.remote_dma_fused(tr, local_sem=T.sem.ls)
+
+    def one(r, m, sem, src, dst):
+        return RemoteDMATransfer(dst_ids=[coreid(r)], dma_engine_mask=m, remote_sem=T.sem[sem], src=src, dst=dst)
+
+    def send(sem, dst, src, deps, second=0):
+        need("g", deps)
+        tr = [one(r, bits(mine[r][second]), sem, src(b), dst((me - r - 1) % NR)) for b, r in enumerate(peers)]
+        fused(tr)
+        count["ls"] = count.get("ls", 0) + sum(len(mine[r][second]) for r in peers)
 
     def by(x, a, b):
         return x[:, a:b].bitcast(dt.uint8)
+
+    def sendcols(sem, dst, src, dc, ds):
+        C, P, DC, DP = T["c" + src], T["s" + src], T["c" + dst], T["s" + dst]
+        if not SINGLE:
+            send(sem, lambda b: by(DC, 32 * b, 32 * b + 32), lambda b: by(C, 32 * b, 32 * b + 32), [dc])
+            send(sem, lambda b: DP[:, 32 * b:32 * b + 32], lambda b: P[:, 32 * b:32 * b + 32], [ds], 1)
+            return
+        need("g", [dc, ds])
+        tr = []
+        for b, r in enumerate(peers):
+            e = topo.engines(core, cores[r])[5 * b:5 * b + 5]
+            o = 32 * ((me - r - 1) % NR)
+            i = 32 * b
+            for k in range(4):
+                tr.append(one(r, 1 << e[k], sem, by(C, i + 8 * k, i + 8 * k + 8), by(DC, o + 8 * k, o + 8 * k + 8)))
+            tr.append(one(r, 1 << e[4], sem, P[:, i:i + 32], DP[:, o:o + 32]))
+        fused(tr)
+        count["ls"] = count.get("ls", 0) + 15
 
     def wd(x, a, b):
         return x[:, a:b].bitcast(dt.uint32)
@@ -146,118 +176,108 @@ def rank_program(g, core, T, topo):
     for k in range(8):
         d_st = DMA("y" if k % 2 == 0 else "s", "dst", T.STW[16 * k:16 * k + 16, 0:4], T.st[:, :])
     d_x = DMA("y", "dx", T.XT[:, 0:256], T.x[:, :])
+    d_nd = DMA("s", "dnd", T.NXD[:, :], T.nx[:, :])
     d_ky = DMA("s", "dky", T.KT[:, 0:1024], T.ky[:, 0:1024])
     d_ky = DMA("y", "dky", T.KT[:, 1024:2048], T.ky[:, 1024:2048])
     for k in range(8):
-        d_nx = DMA("y", "dnx", T.NXW[16 * k:16 * k + 16, 0:32], T.nx[:, :])
+        d_nx = DMA("y", "dnx", T.NXW[16 * k:16 * k + 16, 96:128], T.nx[:, :])
     d_w = DMA("y", "dw", T.WT[:, :], T.w[:, :])
 
     i_pi = IOTA(T.PI[:, 0:1], [[0, 1]], 0, 1)
+    i_np = IOTA(T.NODF[:, :], [[1, 512]], off, 0, True)
     i_jp = IOTA(T.JP[:, :], [[1, 128]], 0, -1)
-    i_np = IOTA(T.NODEP[:, :], [[1, 512]], off, 0)
     i_kp = IOTA(T.KP[:, :], [[-16, 8]], 0, 1)
     i_k16 = IOTA(T.K16[:, 0:4], [[16, 4]], 0, 0)
     i_io4 = IOTA(T.IO4[:, 0:4], [[1, 4]], 0, 0)
     i_na = IOTA(T.NA[:, :], [[-1, 64]], -129, 0, True)
+    need("g", [d_nd])
+    e16 = topo.engines(core, cores[peers[0]])
+    fused([RemoteDMATransfer(dst_ids=[coreid(r) for r in peers], dma_engine_mask=bits(e16), remote_sem=T.sem.nxr, srcs=[T.NXD[:, :]],
+                             dsts=[T["NXR%d" % ((me - r - 1) % NR)][:, :] for r in peers])])
+    count["ls"] = len(e16)
 
     m_rs = V("set", [], T.RS64[:, :], 1.0)
     m_r16 = V("set", [], T.RS16[:, :], 1.0)
-    m_e = V("set", [], T.ET[:, :], 0.0)
+    m_xt = V("set", [], T.XT[:, 256:512], 0.0)
     m_rs = V("set", [m_rs], T.RS64[:, 0:512:64], 0.0)
     m_r16 = V("set", [m_r16], T.RS16[:, 0:128:16], 0.0)
-    m_xs = V("set", [], T.XS[:, :], 0.0)
-    m_xt = V("set", [], T.XT[:, 256:512], 0.0)
     k_pj = V("ts", [i_pi], T.PJ[:, 0:1], T.PI[:, 0:1], 15, None, A.bitwise_and)
-    k_jpa = V("ts", [i_jp], T.JPA[:, :], T.JP[:, :], 15, None, A.bitwise_and)
+    m_xs = V("set", [], T.XS[:, :], 0.0)
     k_t0 = V("ts", [k_pj], T.THR[:, 0:1], T.PJ[:, 0:1], 0.0, None, A.add)
     k_t1 = V("ts", [k_pj], T.THR[:, 1:2], T.PJ[:, 0:1], 16.0, None, A.add)
-    k_d16 = V("ts", [k_jpa], T.D16[:, :], T.JPA[:, :], 0.0, None, A.is_equal)
-    for b in range(4):
-        k_e = V("ts", [m_e, i_jp], T.ET[:, 512 * b + b:512 * b + 512:4], T.JP[:, :], 0.0, 0.5, A.is_equal, A.mult)
-    for b in range(4):
-        k_s = V("ts", [k_jpa], T.ST[:, b:512:4], T.JPA[:, :], 0.0, None, A.is_equal)
+    V("set", [], T.ET[:, 0:1024], 0.0)
 
     k_st = V("copy", [d_st], T.STU[:, :], T.STW[:, :])
-    node = V("copy", [k_st, i_np], T.NN0[:, 128:192], T.NODEP[:, 0:512].indirect(T.STU[:, 0:4]))
+    node = V("copy", [k_st, i_np], T.NN0[:, 128:192], T.NODF[:, 0:512].indirect(T.STU[:, 0:4]))
 
-    def lists(t, node):
-        bt = V("ts", [node], T.BT[:, :], T["NN%d" % t][:, 128:192], 7, 3, A.logical_shift_right, A.bitwise_and)
+    def lists(t, bt, vt, mid):
         for b in range(4):
             mk = V("ts", [bt], T.MK[:, 64 * b:64 * b + 64], T.BT[:, :], float(b), None, A.is_equal)
+        vt = vt()
         px = V("scan", [mk, m_rs], T.PX[:, :], T.RS64[:, 0:256], T.MK[:, :], 0.0, A.mult, A.add)
         cn = V("ts", [px, k_t0], T.CN[:, 0:256], T.PX[:, :], T.THR[:, 0:1], None, A.is_le)
         cn = V("ts", [px, k_t1], T.CN[:, 256:512], T.PX[:, :], T.THR[:, 1:2], None, A.is_le)
         sc = V("scan", [cn], T.SC[:, :], T.RS64[:, :], T.CN[:, :], 0.0, A.mult, A.add)
+        hq = mid()
         for h in range(2):
             al = V("ts", [sc], L("AL", t, h, 8, 2), T.SC[:, 256 * h + 63:256 * h + 256:64], 63.0, None, A.min)
-        return al
+        return al, vt, hq
 
-    def sendpicks(t, al, hq):
+    def depart(t, al, vt, hq):
         c, s = T["cHQ%d" % t], T["sHQ%d" % t]
-        p1 = V("copy", [al] + hq, wd(T["cSD%d" % t], 0, 96), wd(c, 0, 64).indirect(L("AL", t, 0, 6)))
         p2 = S(T["sSD%d" % t][:, 0:96], s[:, 0:64].indirect(L("AL", t, 0, 6)), [al] + hq)
-        send("aq%d" % t, lambda b, b2: (by(T["cLA%d" % t], 32 * b2, 32 * b2 + 32), by(T["cSD%d" % t], 32 * b, 32 * b + 32)), [p1])
-        send("aq%d" % t, lambda b, b2: (T["sLA%d" % t][:, 32 * b2:32 * b2 + 32], T["sSD%d" % t][:, 32 * b:32 * b + 32]), [p2])
-        o1 = V("copy", [al] + hq, wd(T["cLA%d" % t], 96, 128), wd(c, 0, 64).indirect(L("AL", t, 6, 8)))
         o2 = S(T["sLA%d" % t][:, 96:128], s[:, 0:64].indirect(L("AL", t, 6, 8)), [al] + hq)
+        p1 = V("copy", [al] + hq, wd(T["cSD%d" % t], 0, 96), wd(c, 0, 64).indirect(L("AL", t, 0, 6)))
+        vd = V("tt", [vt, al, K["d16"]], T.VD[:, :], T.VT[:, 0:64].indirect(L("AL", t, 0, 8)), T.D16[:, :], A.mult)
+        o1 = V("copy", [], wd(T["cLA%d" % t], 96, 128), wd(c, 0, 64).indirect(L("AL", t, 6, 8)))
+        ve = V("scan", [vd, m_r16], T.VE[:, :], T.RS16[:, :], T.VD[:, :], 0.0, A.mult, A.add)
+        vs = V("ts", [ve], L("VS", t, 0, 8), T.VE[:, 15:128:16], 4.0, None, A.mult)
+        sendcols("aq%d" % t, "LA%d" % t, "SD%d" % t, p1, p2)
+        send("av%d" % t, lambda b: L("VL", t, 2 * b, 2 * b + 2), lambda b: L("VS", t, 2 * b, 2 * b + 2), [vs])
         DMA("y", "dh%d" % t, by(T["cRW%d" % t], 128, 192), by(c, 0, 64), hq)
         dh = DMA("y", "dh%d" % t, T["sRW%d" % t][:, 128:192], s[:, 0:64], hq)
-        return [o1, o2], dh
-
-    def nodelist(t, al, node):
-        vt = V("ts", [node], T.VT[:, :], T["NN%d" % t][:, 128:192], 127, None, A.bitwise_and)
-        vd = V("tt", [vt, al, k_d16], T.VD[:, :], T.VT[:, 0:64].indirect(L("AL", t, 0, 8)), T.D16[:, :], A.mult)
-        ve = V("scan", [vd, m_r16], T.VE[:, :], T.RS16[:, :], T.VD[:, :], 0.0, A.mult, A.add)
-        vs = V("copy", [ve], L("VS", t, 0, 8), T.VE[:, 15:128:16])
-        send("av%d" % t, lambda b, b2: (L("VL", t, 2 * b2, 2 * b2 + 2), L("VS", t, 2 * b, 2 * b + 2)), [vs])
-        return vs
+        return [o1, o2], vs, dh
 
     def server(t, own, vs, prev):
         KQ, sKQ = T.cKQ, T.sKQ
         LA, sLA = T["cLA%d" % t], T["sLA%d" % t]
-        land = [("aq%d" % t, 2 * SENT)] + own
+        land = [("aq%d" % t, BOTH)] + own
         z0 = MM(T.pz[:, 0:256], LA[:, 0:128], sLA[:, 0:128], KQ[:, 0:256], sKQ[:, 0:256], True, True, land + [K["kq"]] + prev["z"])
         z1 = MM(T.pz[:, 512:768], LA[:, 0:128], sLA[:, 0:128], KQ[:, 256:512], sKQ[:, 256:512], True, True, [])
         for b in range(4):
             MM(T.pv[:, 512 * b:512 * b + 128], T.cEQ[:, 128 * b:128 * b + 128], T.sEQ[:, 128 * b:128 * b + 128],
                LA[:, 0:128], sLA[:, 0:128], True, False, [K["eq"]] + prev["pv"])
-        w = 16 * t
-        a = V("ts", [vs], T.V4[:, w + 6:w + 8], L("VS", t, 6, 8), 4.0, None, A.mult)
-        a2 = V("ts", [("av%d" % t, SENT)], T.V4[:, w:w + 6], L("VL", t, 0, 6), 4.0, None, A.mult)
-        b8 = V("tt", [a, a2, K["m8"]], T.T8[:, :], T.V4[:, w:w + 8], T.M8[:, :], A.mult)
-        vp = V("red", [b8], T.V4[:, w + 8:w + 9], T.T8[:, :], AxisListType.X, A.add)
-        z4 = V("ts", [vp, i_io4], L("Z4", t, 0, 4), T.IO4[:, 0:4], T.V4[:, w + 8:w + 9], None, A.add)
         c1 = S(T.ZS[:, 256:512], T.pz[:, 512:768], [z1] + prev["zs"])
+        V("tt", [vs, K["m8"]], T.T8[:, 6:8], L("VS", t, 6, 8), T.M8[:, 6:8], A.mult)
         c0 = V("copy", [z0], T.ZS[:, 0:256], T.pz[:, 0:256])
+        b8 = V("tt", [("av%d" % t, IN[0])], T.T8[:, 0:6], L("VL", t, 0, 6), T.M8[:, 0:6], A.mult)
+        vp = V("red", [b8], T.VP[:, 0:1], T.T8[:, :], AxisListType.X, A.add)
+        z4 = V("ts", [vp, i_io4], L("Z4", t, 0, 4), T.IO4[:, 0:4], T.VP[:, 0:1], None, A.add)
         t64 = V("tt", [c0, c1, z4, K["nm"]], T.T64[:, :], T.ZS[:, 0:512].indirect(L("Z4", t, 0, 4)), T.NM64[:, :], A.add)
         rm = V("scan", [t64], T.RM[:, :], T.T64[:, :], T.T64[:, :], -BIG, A.max, A.max)
         for u in range(3):
             xs = V("ts", [rm, m_xs, K["m8"]], T.XS[:, u:32:4], T.NMK[:, :], T.RM[:, 16 * u + 15:16 * u + 16], T.RM[:, 63:64], A.add, A.is_lt)
         xq = V("q", [xs, prev["xm"]], T.cXQ[:, 0:128], T.sXQ[:, 0:128], T.XS[:, :])
         xm = MM(T.px[:, 0:128], T.cSQ[:, 0:128], T.sSQ[:, 0:128], T.cXQ[:, 0:128], T.sXQ[:, 0:128], True, True, [xq, K["sq"], prev["of"]])
-        of = V("tt", [xm, a, a2], T.OF[:, :], T.px[:, 0:8], T.V4[:, w:w + 8], A.add)
+        V("tt", [xm], T.OF[:, 0:6], T.px[:, 0:6], L("VL", t, 0, 6), A.add)
+        of = V("tt", [xm], T.OF[:, 6:8], T.px[:, 6:8], L("VS", t, 6, 8), A.add)
         ou = V("copy", [of], L("OU", t, 0, 8), T.OF[:, :])
+        send("rc%d" % t, lambda b: L("CL", t, 2 * b, 2 * b + 2), lambda b: L("OU", t, 2 * b, 2 * b + 2), [ou])
         kc = V("copy", [ou, K["kq"]], wd(T["cKC%d" % t], 0, 128), wd(KQ, 0, 512).indirect(L("OU", t, 0, 8)))
         ks = S(T["sKC%d" % t][:, 0:128], sKQ[:, 0:512].indirect(L("OU", t, 0, 8)), [ou, K["kq"]])
-        km = [MM(T.pv[:, 512 * b:512 * b + 128], T.cEQ[:, 128 * b:128 * b + 128], T.sEQ[:, 128 * b:128 * b + 128],
-                 T["cKC%d" % t][:, 0:128], T["sKC%d" % t][:, 0:128], False, True, [kc, ks]) for b in range(4)]
-        ld = V("tt", [ou, K["nx"], k_d16], T.LD[:, :], T.NXF[:, 0:512].indirect(L("OU", t, 0, 8)), T.D16[:, :], A.mult)
-        le = V("scan", [ld, m_r16], T.LE[:, :], T.RS16[:, :], T.LD[:, :], 0.0, A.mult, A.add)
-        cs = V("copy", [le], L("CS", t, 0, 8), T.LE[:, 15:128:16])
-        send("rc%d" % t, lambda b, b2: (L("CL", t, 2 * b2, 2 * b2 + 2), L("CS", t, 2 * b, 2 * b + 2)), [cs])
         h = []
-        for b in (1, 3):
-            h.append(S(T.HT[:, b:512:4], T.pv[:, 512 * b:512 * b + 128], [km[b], prev["nq"]]))
-        for b in (0, 2):
-            h.append(V("copy", [km[b], prev["nq"]], T.HT[:, b:512:4], T.pv[:, 512 * b:512 * b + 128]))
+        for b in range(4):
+            km = MM(T.pv[:, 512 * b:512 * b + 128], T.cEQ[:, 128 * b:128 * b + 128], T.sEQ[:, 128 * b:128 * b + 128],
+                    T["cKC%d" % t][:, 0:128], T["sKC%d" % t][:, 0:128], False, True, [kc, ks])
+            o, i = T.HT[:, b:512:4], T.pv[:, 512 * b:512 * b + 128]
+            h.append(S(o, i, [km, prev["nq"]]) if b % 2 == 0 else V("copy", [km, prev["nq"]], o, i))
         C, P = T["cNW%d" % t], T["sNW%d" % t]
         nq = V("q", h, C[:, 0:128], P[:, 0:128], T.HT[:, :])
-        send("rq%d" % t, lambda b, b2: (by(T["cRW%d" % t], 32 * b2, 32 * b2 + 32), by(C, 32 * b, 32 * b + 32)), [nq])
-        send("rq%d" % t, lambda b, b2: (T["sRW%d" % t][:, 32 * b2:32 * b2 + 32], P[:, 32 * b:32 * b + 32]), [])
+        sendcols("rq%d" % t, "RW%d" % t, "NW%d" % t, nq, nq)
         w1 = V("copy", [nq, K["id"]], wd(T["cRW%d" % t], 96, 128), wd(C, 96, 128).indirect(T.IDL[:, 0:2]))
         w2 = S(T["sRW%d" % t][:, 96:128], P[:, 96:128].indirect(T.IDL[:, 0:2]), [nq, K["id"]])
         prev.update({"z": [c0, c1], "pv": h, "zs": [t64], "xm": xm, "of": of, "nq": nq})
-        return [w1, w2], cs
+        return [w1, w2], ou
 
     def where(t):
         u = V("tt", [], T.UU[:, :], T.PX[:, :], T.MK[:, :], A.mult)
@@ -273,14 +293,8 @@ def rank_program(g, core, T, topo):
         q7 = V("tt", [q6, K["aw"]], T.Q7[:, :], T.Q6[:, 15:64:16], T.AW[:, :], A.add)
         return V("copy", [q7], L("SL", t, 0, 4), T.Q7[:, :])
 
-    def walk(t, cs, sl, node):
-        n = T["NN%d" % t]
-        g1 = V("copy", [cs], n[:, 96:128], T.NODEP[:, 0:512].indirect(L("CS", t, 6, 8)))
-        g2 = V("copy", [("rc%d" % t, SENT)], n[:, 0:96], T.NODEP[:, 0:512].indirect(L("CL", t, 0, 6)))
-        return V("copy", [g1, g2, sl, node], T["NN%d" % (t + 1)][:, 128:192], n[:, 0:192].indirect(L("SL", t, 0, 4)))
-
     def order(t, sl, own, dh):
-        deps = own + [sl, dh, ("rq%d" % t, 2 * SENT)]
+        deps = own + [sl, dh, ("rq%d" % t, BOTH)]
         c, s = T["cHQ%d" % (t + 1)], T["sHQ%d" % (t + 1)]
         h2 = S(s[:, 0:64], T["sRW%d" % t][:, 0:192].indirect(L("SL", t, 0, 4)), deps)
         h1 = V("copy", deps, wd(c, 0, 64), wd(T["cRW%d" % t], 0, 192).indirect(L("SL", t, 0, 4)))
@@ -288,37 +302,69 @@ def rank_program(g, core, T, topo):
 
     K = {}
     prev = {"z": [], "pv": [], "zs": [], "xm": None, "of": None, "nq": None}
-    al = lists(0, node)
-    hq0 = hq = [V("q", [d_x, m_xt], T.cHQ0[:, 0:128], T.sHQ0[:, 0:128], T.XT[:, :])]
+    bt = V("ts", [node], T.BT[:, :], T.NN0[:, 128:192], 7, 3, A.logical_shift_right, A.bitwise_and)
+    hq0 = []
+
+    def vt0():
+        return V("ts", [node], T.VT[:, :], T.NN0[:, 128:192], 127, None, A.bitwise_and)
+
+    def mid0():
+        K["jpa"] = V("ts", [i_jp], T.JPA[:, :], T.JP[:, :], 15, None, A.bitwise_and)
+        hq0.append(V("q", [d_x, m_xt], T.cHQ0[:, 0:128], T.sHQ0[:, 0:128], T.XT[:, :]))
+        K["d16"] = V("ts", [K["jpa"]], T.D16[:, :], T.JPA[:, :], 0.0, None, A.is_equal)
+        return hq0
+
+    al, vt, hq = lists(0, bt, vt0, mid0)
     for t in range(HOPS):
-        own, dh = sendpicks(t, al, hq)
-        vs = nodelist(t, al, node)
+        own, vs, dh = depart(t, al, vt, hq)
         if t == 0:
             k_kp = V("ts", [i_kp], T.KP2[:, :], T.KP[:, :], 4, None, A.arith_shift_right)
-            K["nm"] = V("ts", [k_d16], T.NM64[:, :], T.D16[:, 0:64], -1.0, BIG, A.add, A.mult)
+            K["nm"] = V("ts", [K["d16"]], T.NM64[:, :], T.D16[:, 0:64], -1.0, BIG, A.add, A.mult)
             V("ts", [k_kp], T.M8[:, :], T.KP2[:, :], 0.0, None, A.is_equal)
             K["m8"] = V("ts", [k_kp], T.NMK[:, :], T.KP2[:, :], 0.0, BIG, A.not_equal, A.mult)
-            K["sq"] = V("q", [k_s], T.cSQ[:, 0:128], T.sSQ[:, 0:128], T.ST[:, :])
-            K["eq"] = V("q", [k_e], T.cEQ[:, 0:512], T.sEQ[:, 0:512], T.ET[:, :])
+            m_e = V("set", [], T.ET[:, 1024:2048], 0.0)
             K["kq"] = V("q", [d_ky], T.cKQ[:, 0:512], T.sKQ[:, 0:512], T.KT[:, :])
-            k_nu = V("copy", [d_nx], T.NXU[:, :], T.NXW[:, :])
-            K["nx"] = V("ts", [k_nu, i_np], T.NXF[:, :], T.NODEP[:, 0:512].indirect(T.NXU[:, 0:32]), float(-off), None, A.add)
+            for b in range(4):
+                k_e = V("ts", [m_e, i_jp], T.ET[:, 512 * b + b:512 * b + 512:4], T.JP[:, :], 0.0, 0.5, A.is_equal, A.mult)
+            for b in range(4):
+                k_s = V("ts", [K["jpa"]], T.ST[:, b:512:4], T.JPA[:, :], 0.0, None, A.is_equal)
+            K["eq"] = V("q", [k_e], T.cEQ[:, 0:512], T.sEQ[:, 0:512], T.ET[:, :])
+            K["sq"] = V("q", [k_s], T.cSQ[:, 0:128], T.sSQ[:, 0:128], T.ST[:, :])
             K["id"] = V("ts", [k_t0, i_k16], T.IDL[:, :], T.K16[:, 0:2], T.THR[:, 0:1], None, A.add)
             K["aw"] = V("ts", [k_t0, i_k16], T.AW[:, :], T.K16[:, 0:4], T.THR[:, 0:1], 128.0, A.add, A.add)
             DMA("y", "dh3", by(T.cHQ3, 64, 128), by(T.cHQ0, 64, 128), hq0)
             d_h3 = DMA("y", "dh3", T.sHQ3[:, 64:128], T.sHQ0[:, 64:128], hq0)
-        own, cs = server(t, own, vs, prev)
-        sl = where(t)
-        if t == 0:
+            for b in range(3):
+                for k in range(8):
+                    d_nx = DMA("y", "dnx", T.NXW[16 * k:16 * k + 16, 32 * b:32 * b + 32], T["NXR%d" % b][:, :], [("nxr", 3 * len(e16))])
+        if t == 1:
             K["wq"] = V("q", [d_w], T.cWQ[:, 0:128], T.sWQ[:, 0:128], T.WT[:, :])
+        sl = where(t)
+        own, ou = server(t, own, vs, prev)
+        if t == 0:
+            k_nu = V("copy", [d_nx], T.NXU[:, :], T.NXW[:, :])
+            K["nxo"] = V("copy", [k_nu, i_np], T.NXA[:, 1536:2048], T.NODF[:, 0:512].indirect(T.NXU[:, 96:128]))
+            for b in range(3):
+                K["nxa"] = S(T.NXA[:, 512 * b:512 * b + 512], T.NODF[:, 0:512].indirect(T.NXU[:, 32 * b:32 * b + 32]), [k_nu, i_np])
         V("ts", [node], T.ND[:, 64 * t:64 * t + 64], T["NN%d" % t][:, 128:192], float(-off), None, A.add)
-        node = walk(t, cs, sl, node)
+        n = T["NN%d" % t]
+        V("copy", [ou, K["nxo"]], n[:, 96:128], T.NXA[:, 1536:2048].indirect(L("OU", t, 6, 8)))
+        for b in range(3):
+            g1 = V("copy", [("rc%d" % t, IN[0]), K["nxa"]], n[:, 32 * b:32 * b + 32], T.NXA[:, 512 * b:512 * b + 512].indirect(L("CL", t, 2 * b, 2 * b + 2)))
+        byq = n[:, 0:192].indirect(L("SL", t, 0, 4))
+
+        def nodes():
+            return V("copy", [g1, sl, node], T["NN%d" % (t + 1)][:, 128:192], byq)
+
         if t + 1 < HOPS:
-            al = lists(t + 1, node)
+            bt = V("ts", [g1, sl, node], T.BT[:, :], byq, 7, 3, A.logical_shift_right, A.bitwise_and)
+            al, vt, hq = lists(t + 1, bt, lambda: V("ts", [g1, sl, node], T.VT[:, :], byq, 127, None, A.bitwise_and), lambda: order(t, sl, own, dh))
+            node = nodes()
         else:
+            node = nodes()
             nd = V("ts", [node], T.ND[:, 64 * HOPS:64 * HOPS + 64], T["NN%d" % HOPS][:, 128:192], float(-off), None, A.add)
             DMA("y", "dout", T.nd[:, :], T.ND[0:1, 0:256], [nd])
-        hq = order(t, sl, own, dh)
+            hq = order(t, sl, own, dh)
 
     DMA("y", "dout", T.oc[:, :], by(T.cHQ3, 0, 64), [hq[0]])
     for k in range(4):
@@ -326,5 +372,5 @@ def rank_program(g, core, T, topo):
     ym = MM(T.py[:, 0:128], T.cWQ[:, 0:128], T.sWQ[:, 0:128], T.cHQ3[:, 0:128], T.sHQ3[:, 0:128], True, True, hq + [K["wq"], d_h3])
     yc = V("copy", [ym], T.YS[:, :], T.py[:, 0:64])
     DMA("y", "dout", T.y[:, :], T.YS[:, :], [yc])
-    for sem in ("dout", "ls", "cv", "cs", "ct", "cg", "dst", "dx", "dky", "dnx", "dw", "dh3", "dh0", "dh1", "dh2"):
+    for sem in ("dout", "ls", "cv", "cs", "ct", "cg", "dst", "dx", "dky", "dnx", "dnd", "dw", "dh3", "dh0", "dh1", "dh2"):
         need("g", [(sem, count[sem])])

@@ -3,13 +3,13 @@ from concourse.mybir import dt, AluOpType as A, AxisListType, ActivationFunction
 
 NR, CAP, HOPS = 4, 32, 3
 BIG = 1e29
-SINGLE = True
+CUT = 320
 
 SCRATCH = {
     "STW": ("sbuf", [128, 4], "int32"), "STU": ("sbuf", [128, 4], "uint16"),
     "NXD": ("dram", [128, 4], "int32"), "NXR0": ("dram", [128, 4], "int32"), "NXR1": ("dram", [128, 4], "int32"), "NXR2": ("dram", [128, 4], "int32"),
     "NXW": ("sbuf", [128, 128], "int32"), "NXU": ("sbuf", [128, 128], "uint16"), "NXA": ("sbuf", [128, 2048], "float32"),
-    "NODF": ("sbuf", [128, 512], "float32"), "JP": ("sbuf", [128, 128], "int32"), "JPA": ("sbuf", [128, 128], "int32"),
+    "NODF": ("sbuf", [128, 512], "float32"), "JP": ("sbuf", [128, 128], "int32"), "JPA": ("sbuf", [128, 128], "int32"), "ID": ("sbuf", [128, 128], "bfloat16"),
     "PI": ("sbuf", [128, 8], "int32"), "PJ": ("sbuf", [128, 8], "int32"), "THR": ("sbuf", [128, 8], "float32"),
     "KP": ("sbuf", [128, 8], "int32"), "KP2": ("sbuf", [128, 8], "int32"), "M8": ("sbuf", [128, 8], "float32"), "NMK": ("sbuf", [128, 8], "float32"),
     "IO4": ("sbuf", [128, 8], "int32"), "K16": ("sbuf", [128, 8], "int32"), "AW": ("sbuf", [128, 4], "float32"), "IDL": ("sbuf", [128, 2], "uint16"),
@@ -112,11 +112,11 @@ def rank_program(g, core, T, topo):
 
     peers = [(me + 1 + b) % NR for b in range(NR - 1)]
 
-    def plan(s):
-        others = sorted((r for r in range(NR) if r != s), key=lambda r: (topo.die(cores[r]) != topo.die(cores[s]), (r - s) % NR))
-        e = topo.engines(cores[s], cores[others[0]])
+    def part(s, r):
+        others = sorted((o for o in range(NR) if o != s), key=lambda o: (topo.die(cores[o]) != topo.die(cores[s]), (o - s) % NR))
+        e = topo.engines(cores[s], cores[r])
         q = len(e) // 4
-        return {others[0]: (e[:q], e[:2 * q]), others[1]: (e[q:2 * q], e[3 * q:]), others[2]: (e[2 * q:], e[2 * q:3 * q])}
+        return (e[:q], e[q:2 * q], e[2 * q:])[others.index(r)]
 
     def bits(es):
         m = 0
@@ -128,9 +128,8 @@ def rank_program(g, core, T, topo):
         rid, pid, _ = topo.addr(cores[r])
         return DstId(rid=rid, pnc=pid)
 
-    mine = plan(me)
-    IN = [sum(len(plan(r)[me][i]) for r in peers) for i in range(2)]
-    BOTH = 15 if SINGLE else sum(IN)
+    LIST = sum(len(part(r, me)) for r in peers)
+    COLS = 15
 
     def fused(tr):
         g.remote_dma_fused(tr, local_sem=T.sem.ls)
@@ -138,22 +137,17 @@ def rank_program(g, core, T, topo):
     def one(r, m, sem, src, dst):
         return RemoteDMATransfer(dst_ids=[coreid(r)], dma_engine_mask=m, remote_sem=T.sem[sem], src=src, dst=dst)
 
-    def send(sem, dst, src, deps, second=0):
+    def send(sem, dst, src, deps):
         need("g", deps)
-        tr = [one(r, bits(mine[r][second]), sem, src(b), dst((me - r - 1) % NR)) for b, r in enumerate(peers)]
-        fused(tr)
-        count["ls"] = count.get("ls", 0) + sum(len(mine[r][second]) for r in peers)
+        fused([one(r, bits(part(me, r)), sem, src(b), dst((me - r - 1) % NR)) for b, r in enumerate(peers)])
+        count["ls"] = count.get("ls", 0) + sum(len(part(me, r)) for r in peers)
 
     def by(x, a, b):
         return x[:, a:b].bitcast(dt.uint8)
 
-    def sendcols(sem, dst, src, dc, ds):
+    def sendcols(sem, dst, src, deps):
         C, P, DC, DP = T["c" + src], T["s" + src], T["c" + dst], T["s" + dst]
-        if not SINGLE:
-            send(sem, lambda b: by(DC, 32 * b, 32 * b + 32), lambda b: by(C, 32 * b, 32 * b + 32), [dc])
-            send(sem, lambda b: DP[:, 32 * b:32 * b + 32], lambda b: P[:, 32 * b:32 * b + 32], [ds], 1)
-            return
-        need("g", [dc, ds])
+        need("g", deps)
         tr = []
         for b, r in enumerate(peers):
             e = topo.engines(core, cores[r])[5 * b:5 * b + 5]
@@ -172,6 +166,7 @@ def rank_program(g, core, T, topo):
         return T[name][:, 8 * t + a:8 * t + b:step]
 
     off = 128 * (NR - 1 - me)
+    K = {}
 
     for k in range(8):
         d_st = DMA("y" if k % 2 == 0 else "s", "dst", T.STW[16 * k:16 * k + 16, 0:4], T.st[:, :])
@@ -184,8 +179,8 @@ def rank_program(g, core, T, topo):
     d_w = DMA("y", "dw", T.WT[:, :], T.w[:, :])
 
     i_pi = IOTA(T.PI[:, 0:1], [[0, 1]], 0, 1)
-    i_np = IOTA(T.NODF[:, :], [[1, 512]], off, 0, True)
     i_jp = IOTA(T.JP[:, :], [[1, 128]], 0, -1)
+    i_np = IOTA(T.NODF[:, :], [[1, 512]], off, 0, True)
     i_kp = IOTA(T.KP[:, :], [[-16, 8]], 0, 1)
     i_k16 = IOTA(T.K16[:, 0:4], [[16, 4]], 0, 0)
     i_io4 = IOTA(T.IO4[:, 0:4], [[1, 4]], 0, 0)
@@ -205,7 +200,16 @@ def rank_program(g, core, T, topo):
     m_xs = V("set", [], T.XS[:, :], 0.0)
     k_t0 = V("ts", [k_pj], T.THR[:, 0:1], T.PJ[:, 0:1], 0.0, None, A.add)
     k_t1 = V("ts", [k_pj], T.THR[:, 1:2], T.PJ[:, 0:1], 16.0, None, A.add)
-    V("set", [], T.ET[:, 0:1024], 0.0)
+    k_jpa = V("ts", [i_jp], T.JPA[:, :], T.JP[:, :], 15, None, A.bitwise_and)
+    k_id = V("ts", [i_jp], T.ID[:, :], T.JP[:, :], 0.0, 0.5, A.is_equal, A.mult)
+    K["d16"] = V("ts", [k_jpa], T.D16[:, :], T.JPA[:, :], 0.0, None, A.is_equal)
+    for b in range(4):
+        need("s", [m_rs])
+        m_e = done("s", g.scalar.activation(T.ET[:, 512 * b:512 * b + 512], T.RS64[:, :], F.Copy, 0.0, 0.0), "cs", 1)
+    for b in range(4):
+        k_e = S(T.ET[:, 512 * b + b:512 * b + 512:4], T.ID[:, :], [m_e, k_id])
+    for b in range(4):
+        k_s = S(T.ST[:, b:512:4], T.D16[:, :], [K["d16"]])
 
     k_st = V("copy", [d_st], T.STU[:, :], T.STW[:, :])
     node = V("copy", [k_st, i_np], T.NN0[:, 128:192], T.NODF[:, 0:512].indirect(T.STU[:, 0:4]))
@@ -232,25 +236,25 @@ def rank_program(g, core, T, topo):
         o1 = V("copy", [], wd(T["cLA%d" % t], 96, 128), wd(c, 0, 64).indirect(L("AL", t, 6, 8)))
         ve = V("scan", [vd, m_r16], T.VE[:, :], T.RS16[:, :], T.VD[:, :], 0.0, A.mult, A.add)
         vs = V("ts", [ve], L("VS", t, 0, 8), T.VE[:, 15:128:16], 4.0, None, A.mult)
-        sendcols("aq%d" % t, "LA%d" % t, "SD%d" % t, p1, p2)
+        sendcols("aq%d" % t, "LA%d" % t, "SD%d" % t, [p1, p2])
         send("av%d" % t, lambda b: L("VL", t, 2 * b, 2 * b + 2), lambda b: L("VS", t, 2 * b, 2 * b + 2), [vs])
         DMA("y", "dh%d" % t, by(T["cRW%d" % t], 128, 192), by(c, 0, 64), hq)
         dh = DMA("y", "dh%d" % t, T["sRW%d" % t][:, 128:192], s[:, 0:64], hq)
         return [o1, o2], vs, dh
 
-    def server(t, own, vs, prev):
+    def server(t, own, vs, prev, aside):
         KQ, sKQ = T.cKQ, T.sKQ
         LA, sLA = T["cLA%d" % t], T["sLA%d" % t]
-        land = [("aq%d" % t, BOTH)] + own
-        z0 = MM(T.pz[:, 0:256], LA[:, 0:128], sLA[:, 0:128], KQ[:, 0:256], sKQ[:, 0:256], True, True, land + [K["kq"]] + prev["z"])
-        z1 = MM(T.pz[:, 512:768], LA[:, 0:128], sLA[:, 0:128], KQ[:, 256:512], sKQ[:, 256:512], True, True, [])
+        land = [("aq%d" % t, COLS)] + own
+        z0 = MM(T.pz[:, 0:CUT], LA[:, 0:128], sLA[:, 0:128], KQ[:, 0:CUT], sKQ[:, 0:CUT], True, True, land + [K["kq"]] + prev["z"])
+        z1 = MM(T.pz[:, 512:1024 - CUT], LA[:, 0:128], sLA[:, 0:128], KQ[:, CUT:512], sKQ[:, CUT:512], True, True, [])
         for b in range(4):
             MM(T.pv[:, 512 * b:512 * b + 128], T.cEQ[:, 128 * b:128 * b + 128], T.sEQ[:, 128 * b:128 * b + 128],
                LA[:, 0:128], sLA[:, 0:128], True, False, [K["eq"]] + prev["pv"])
-        c1 = S(T.ZS[:, 256:512], T.pz[:, 512:768], [z1] + prev["zs"])
+        c1 = S(T.ZS[:, CUT:512], T.pz[:, 512:1024 - CUT], [z1] + prev["zs"])
         V("tt", [vs, K["m8"]], T.T8[:, 6:8], L("VS", t, 6, 8), T.M8[:, 6:8], A.mult)
-        c0 = V("copy", [z0], T.ZS[:, 0:256], T.pz[:, 0:256])
-        b8 = V("tt", [("av%d" % t, IN[0])], T.T8[:, 0:6], L("VL", t, 0, 6), T.M8[:, 0:6], A.mult)
+        b8 = V("tt", [("av%d" % t, LIST)], T.T8[:, 0:6], L("VL", t, 0, 6), T.M8[:, 0:6], A.mult)
+        c0 = V("copy", [z0], T.ZS[:, 0:CUT], T.pz[:, 0:CUT])
         vp = V("red", [b8], T.VP[:, 0:1], T.T8[:, :], AxisListType.X, A.add)
         z4 = V("ts", [vp, i_io4], L("Z4", t, 0, 4), T.IO4[:, 0:4], T.VP[:, 0:1], None, A.add)
         t64 = V("tt", [c0, c1, z4, K["nm"]], T.T64[:, :], T.ZS[:, 0:512].indirect(L("Z4", t, 0, 4)), T.NM64[:, :], A.add)
@@ -265,22 +269,25 @@ def rank_program(g, core, T, topo):
         send("rc%d" % t, lambda b: L("CL", t, 2 * b, 2 * b + 2), lambda b: L("OU", t, 2 * b, 2 * b + 2), [ou])
         kc = V("copy", [ou, K["kq"]], wd(T["cKC%d" % t], 0, 128), wd(KQ, 0, 512).indirect(L("OU", t, 0, 8)))
         ks = S(T["sKC%d" % t][:, 0:128], sKQ[:, 0:512].indirect(L("OU", t, 0, 8)), [ou, K["kq"]])
+        aside(0)
         h = []
         for b in range(4):
             km = MM(T.pv[:, 512 * b:512 * b + 128], T.cEQ[:, 128 * b:128 * b + 128], T.sEQ[:, 128 * b:128 * b + 128],
                     T["cKC%d" % t][:, 0:128], T["sKC%d" % t][:, 0:128], False, True, [kc, ks])
             o, i = T.HT[:, b:512:4], T.pv[:, 512 * b:512 * b + 128]
             h.append(S(o, i, [km, prev["nq"]]) if b % 2 == 0 else V("copy", [km, prev["nq"]], o, i))
+        aside(1)
         C, P = T["cNW%d" % t], T["sNW%d" % t]
         nq = V("q", h, C[:, 0:128], P[:, 0:128], T.HT[:, :])
-        sendcols("rq%d" % t, "RW%d" % t, "NW%d" % t, nq, nq)
+        sendcols("rq%d" % t, "RW%d" % t, "NW%d" % t, [nq])
         w1 = V("copy", [nq, K["id"]], wd(T["cRW%d" % t], 96, 128), wd(C, 96, 128).indirect(T.IDL[:, 0:2]))
         w2 = S(T["sRW%d" % t][:, 96:128], P[:, 96:128].indirect(T.IDL[:, 0:2]), [nq, K["id"]])
         prev.update({"z": [c0, c1], "pv": h, "zs": [t64], "xm": xm, "of": of, "nq": nq})
         return [w1, w2], ou
 
-    def where(t):
+    def where(t, fill):
         u = V("tt", [], T.UU[:, :], T.PX[:, :], T.MK[:, :], A.mult)
+        fill(0)
         q1 = V("ts", [], T.Q1[:, :], T.BT[:, :], 32.0, None, A.mult)
         u = V("tt", [u], T.U2[:, :], T.UU[:, 0:128], T.UU[:, 128:256], A.add)
         q2 = V("tt", [q1, i_na], T.Q2[:, :], T.Q1[:, :], T.NA[:, :], A.add)
@@ -288,19 +295,23 @@ def rank_program(g, core, T, topo):
         sv = V("ts", [p], T.SV[:, :], T.PP[:, :], float(CAP), None, A.is_le)
         q3 = V("tt", [q2, p], T.Q3[:, :], T.Q2[:, :], T.PP[:, :], A.add)
         q4 = V("tt", [sv], T.Q4[:, :], T.SV[:, :], T.D16[:, 0:64], A.mult)
+        fill(1)
         q5 = V("tt", [q3, q4], T.Q5[:, :], T.Q3[:, :], T.Q4[:, :], A.mult)
+        fill(2)
         q6 = V("scan", [q5], T.Q6[:, :], T.RS16[:, 0:64], T.Q5[:, :], 0.0, A.mult, A.add)
         q7 = V("tt", [q6, K["aw"]], T.Q7[:, :], T.Q6[:, 15:64:16], T.AW[:, :], A.add)
         return V("copy", [q7], L("SL", t, 0, 4), T.Q7[:, :])
 
     def order(t, sl, own, dh):
-        deps = own + [sl, dh, ("rq%d" % t, BOTH)]
+        deps = own + [sl, dh, ("rq%d" % t, COLS)]
         c, s = T["cHQ%d" % (t + 1)], T["sHQ%d" % (t + 1)]
         h2 = S(s[:, 0:64], T["sRW%d" % t][:, 0:192].indirect(L("SL", t, 0, 4)), deps)
         h1 = V("copy", deps, wd(c, 0, 64), wd(T["cRW%d" % t], 0, 192).indirect(L("SL", t, 0, 4)))
         return [h1, h2]
 
-    K = {}
+    def table(b):
+        return T.NXA[:, 512 * b:512 * b + 512], T.NODF[:, 0:512].indirect(T.NXU[:, 32 * b:32 * b + 32])
+
     prev = {"z": [], "pv": [], "zs": [], "xm": None, "of": None, "nq": None}
     bt = V("ts", [node], T.BT[:, :], T.NN0[:, 128:192], 7, 3, A.logical_shift_right, A.bitwise_and)
     hq0 = []
@@ -309,9 +320,7 @@ def rank_program(g, core, T, topo):
         return V("ts", [node], T.VT[:, :], T.NN0[:, 128:192], 127, None, A.bitwise_and)
 
     def mid0():
-        K["jpa"] = V("ts", [i_jp], T.JPA[:, :], T.JP[:, :], 15, None, A.bitwise_and)
         hq0.append(V("q", [d_x, m_xt], T.cHQ0[:, 0:128], T.sHQ0[:, 0:128], T.XT[:, :]))
-        K["d16"] = V("ts", [K["jpa"]], T.D16[:, :], T.JPA[:, :], 0.0, None, A.is_equal)
         return hq0
 
     al, vt, hq = lists(0, bt, vt0, mid0)
@@ -322,14 +331,6 @@ def rank_program(g, core, T, topo):
             K["nm"] = V("ts", [K["d16"]], T.NM64[:, :], T.D16[:, 0:64], -1.0, BIG, A.add, A.mult)
             V("ts", [k_kp], T.M8[:, :], T.KP2[:, :], 0.0, None, A.is_equal)
             K["m8"] = V("ts", [k_kp], T.NMK[:, :], T.KP2[:, :], 0.0, BIG, A.not_equal, A.mult)
-            m_e = V("set", [], T.ET[:, 1024:2048], 0.0)
-            K["kq"] = V("q", [d_ky], T.cKQ[:, 0:512], T.sKQ[:, 0:512], T.KT[:, :])
-            for b in range(4):
-                k_e = V("ts", [m_e, i_jp], T.ET[:, 512 * b + b:512 * b + 512:4], T.JP[:, :], 0.0, 0.5, A.is_equal, A.mult)
-            for b in range(4):
-                k_s = V("ts", [K["jpa"]], T.ST[:, b:512:4], T.JPA[:, :], 0.0, None, A.is_equal)
-            K["eq"] = V("q", [k_e], T.cEQ[:, 0:512], T.sEQ[:, 0:512], T.ET[:, :])
-            K["sq"] = V("q", [k_s], T.cSQ[:, 0:128], T.sSQ[:, 0:128], T.ST[:, :])
             K["id"] = V("ts", [k_t0, i_k16], T.IDL[:, :], T.K16[:, 0:2], T.THR[:, 0:1], None, A.add)
             K["aw"] = V("ts", [k_t0, i_k16], T.AW[:, :], T.K16[:, 0:4], T.THR[:, 0:1], 128.0, A.add, A.add)
             DMA("y", "dh3", by(T.cHQ3, 64, 128), by(T.cHQ0, 64, 128), hq0)
@@ -339,18 +340,34 @@ def rank_program(g, core, T, topo):
                     d_nx = DMA("y", "dnx", T.NXW[16 * k:16 * k + 16, 32 * b:32 * b + 32], T["NXR%d" % b][:, :], [("nxr", 3 * len(e16))])
         if t == 1:
             K["wq"] = V("q", [d_w], T.cWQ[:, 0:128], T.sWQ[:, 0:128], T.WT[:, :])
-        sl = where(t)
-        own, ou = server(t, own, vs, prev)
+
+        def fill(k):
+            if t == 0 and k == 0:
+                K["kq"] = V("q", [d_ky], T.cKQ[:, 0:512], T.sKQ[:, 0:512], T.KT[:, :])
+            if t == 0 and k == 1:
+                K["sq"] = V("q", [k_s], T.cSQ[:, 0:128], T.sSQ[:, 0:128], T.ST[:, :])
+            if t == 0 and k == 2:
+                K["eq"] = V("q", [k_e], T.cEQ[:, 0:512], T.sEQ[:, 0:512], T.ET[:, :])
+
+        def aside(k):
+            if t == 0 and k == 0:
+                K["nu"] = V("copy", [d_nx], T.NXU[:, :], T.NXW[:, :])
+            if t == 0 and k == 1:
+                for b in (1, 2):
+                    o, i = table(b)
+                    K["nxa"] = S(o, i, [K["nu"], i_np])
+
+        sl = where(t, fill)
+        own, ou = server(t, own, vs, prev, aside)
         if t == 0:
-            k_nu = V("copy", [d_nx], T.NXU[:, :], T.NXW[:, :])
-            K["nxo"] = V("copy", [k_nu, i_np], T.NXA[:, 1536:2048], T.NODF[:, 0:512].indirect(T.NXU[:, 96:128]))
-            for b in range(3):
-                K["nxa"] = S(T.NXA[:, 512 * b:512 * b + 512], T.NODF[:, 0:512].indirect(T.NXU[:, 32 * b:32 * b + 32]), [k_nu, i_np])
+            for b in (3, 0):
+                o, i = table(b)
+                K["nxo"] = V("copy", [K["nu"], i_np], o, i)
         V("ts", [node], T.ND[:, 64 * t:64 * t + 64], T["NN%d" % t][:, 128:192], float(-off), None, A.add)
         n = T["NN%d" % t]
         V("copy", [ou, K["nxo"]], n[:, 96:128], T.NXA[:, 1536:2048].indirect(L("OU", t, 6, 8)))
         for b in range(3):
-            g1 = V("copy", [("rc%d" % t, IN[0]), K["nxa"]], n[:, 32 * b:32 * b + 32], T.NXA[:, 512 * b:512 * b + 512].indirect(L("CL", t, 2 * b, 2 * b + 2)))
+            g1 = V("copy", [("rc%d" % t, LIST), K["nxa"]], n[:, 32 * b:32 * b + 32], T.NXA[:, 512 * b:512 * b + 512].indirect(L("CL", t, 2 * b, 2 * b + 2)))
         byq = n[:, 0:192].indirect(L("SL", t, 0, 4))
 
         def nodes():

@@ -3,16 +3,18 @@ from concourse.mybir import dt, AluOpType as A, AxisListType, ActivationFunction
 
 NR, CAP, HOPS = 4, 32, 3
 BIG = 1e29
-CUT = 320
+CUTS = (0, 208, 384, 512)
 
 SCRATCH = {
     "STW": ("sbuf", [128, 4], "int32"), "STU": ("sbuf", [128, 4], "uint16"),
     "NXD": ("dram", [128, 4], "int32"), "NXR0": ("dram", [128, 4], "int32"), "NXR1": ("dram", [128, 4], "int32"), "NXR2": ("dram", [128, 4], "int32"),
-    "NXW": ("sbuf", [128, 128], "int32"), "NXU": ("sbuf", [128, 128], "uint16"), "NXA": ("sbuf", [128, 2048], "float32"),
-    "NODF": ("sbuf", [128, 512], "float32"), "JP": ("sbuf", [128, 128], "int32"), "JPA": ("sbuf", [128, 128], "int32"), "ID": ("sbuf", [128, 128], "bfloat16"),
+    "NXW": ("sbuf", [128, 96], "int32"), "NXV": ("sbuf", [128, 32], "int32"), "NXU": ("sbuf", [128, 128], "uint16"), "NXA": ("sbuf", [128, 2048], "float32"),
+    "NODF": ("sbuf", [128, 512], "float32"), "NODI": ("sbuf", [128, 512], "int32"),
+    "JP": ("sbuf", [128, 128], "int32"), "JPA": ("sbuf", [128, 128], "int32"), "ID": ("sbuf", [128, 128], "bfloat16"),
     "PI": ("sbuf", [128, 8], "int32"), "PJ": ("sbuf", [128, 8], "int32"), "THR": ("sbuf", [128, 8], "float32"),
     "KP": ("sbuf", [128, 8], "int32"), "KP2": ("sbuf", [128, 8], "int32"), "M8": ("sbuf", [128, 8], "float32"), "NMK": ("sbuf", [128, 8], "float32"),
     "IO4": ("sbuf", [128, 8], "int32"), "K16": ("sbuf", [128, 8], "int32"), "AW": ("sbuf", [128, 4], "float32"), "IDL": ("sbuf", [128, 2], "uint16"),
+    "TB": ("sbuf", [128, 8], "float32"),
     "NA": ("sbuf", [128, 64], "float32"), "D16": ("sbuf", [128, 128], "float32"), "NM64": ("sbuf", [128, 64], "float32"),
     "RS64": ("sbuf", [128, 512], "bfloat16"), "RS16": ("sbuf", [128, 128], "float32"),
     "AL": ("sbuf", [128, 24], "uint16"),
@@ -20,21 +22,21 @@ SCRATCH = {
     "VL": ("sbuf", [128, 24], "int32"),
     "Z4": ("sbuf", [128, 24], "uint16"),
     "OU": ("sbuf", [128, 24], "uint16"),
+    "OR": ("sbuf", [128, 24], "uint16"),
     "CL": ("sbuf", [128, 24], "uint16"),
     "SL": ("sbuf", [128, 24], "uint16"),
-    "BT": ("sbuf", [128, 64], "int32"), "MK": ("sbuf", [128, 256], "bfloat16"), "PX": ("sbuf", [128, 256], "bfloat16"),
-    "CN": ("sbuf", [128, 512], "bfloat16"), "SC": ("sbuf", [128, 512], "bfloat16"),
-    "VT": ("sbuf", [128, 64], "int32"), "VD": ("sbuf", [128, 128], "float32"), "VE": ("sbuf", [128, 128], "float32"),
+    "BT": ("sbuf", [128, 64], "int32"), "VT": ("sbuf", [128, 64], "int32"), "MK": ("sbuf", [128, 256], "bfloat16"), "PX": ("sbuf", [128, 256], "bfloat16"),
+    "CN": ("sbuf", [128, 512], "bfloat16"), "SC": ("sbuf", [128, 512], "bfloat16"), "VD": ("sbuf", [128, 128], "float32"), "VE": ("sbuf", [128, 128], "float32"),
     "UU": ("sbuf", [128, 256], "bfloat16"), "U2": ("sbuf", [128, 128], "bfloat16"), "PP": ("sbuf", [128, 64], "float32"), "SV": ("sbuf", [128, 64], "float32"),
     "Q1": ("sbuf", [128, 64], "float32"), "Q2": ("sbuf", [128, 64], "float32"), "Q3": ("sbuf", [128, 64], "float32"), "Q4": ("sbuf", [128, 64], "float32"),
-    "Q5": ("sbuf", [128, 64], "float32"), "Q6": ("sbuf", [128, 64], "float32"), "Q7": ("sbuf", [128, 4], "float32"),
-    "ND": ("sbuf", [128, 256], "float32"),
-    "VP": ("sbuf", [128, 8], "float32"), "T8": ("sbuf", [128, 8], "float32"), "ZS": ("sbuf", [128, 512], "float32"),
-    "T64": ("sbuf", [128, 64], "float32"), "RM": ("sbuf", [128, 64], "float32"),
-    "XS": ("sbuf", [128, 512], "bfloat16"), "OF": ("sbuf", [128, 8], "float32"), "HT": ("sbuf", [128, 512], "bfloat16"),
+    "Q5": ("sbuf", [128, 64], "float32"), "Q6": ("sbuf", [128, 64], "float32"), "Q7": ("sbuf", [128, 4], "float32"), "ND": ("sbuf", [128, 256], "float32"),
+    "VA": ("sbuf", [128, 8], "float32"), "VR": ("sbuf", [128, 8], "float32"), "VP": ("sbuf", [128, 8], "float32"), "T8": ("sbuf", [128, 8], "float32"),
+    "ZS": ("sbuf", [128, 512], "float32"), "T64": ("sbuf", [128, 64], "float32"), "RM": ("sbuf", [128, 64], "float32"),
+    "XS": ("sbuf", [128, 512], "bfloat16"), "OF": ("sbuf", [128, 8], "float32"), "OG": ("sbuf", [128, 8], "float32"), "HT": ("sbuf", [128, 512], "bfloat16"),
+    "DK": ("sbuf", [128, 2048], "float32"), "DQ": ("sbuf", [128, 256], "float32"), "GK": ("sbuf", [128, 256], "float32"),
     "XT": ("sbuf", [128, 512], "bfloat16"), "KT": ("sbuf", [128, 2048], "bfloat16"), "WT": ("sbuf", [128, 512], "bfloat16"),
     "ET": ("sbuf", [128, 2048], "bfloat16"), "ST": ("sbuf", [128, 512], "bfloat16"), "YS": ("sbuf", [128, 64], "float32"),
-    "pv": ("psum", [128, 2048], "float32"), "pz": ("psum", [128, 1024], "float32"), "px": ("psum", [128, 512], "float32"), "py": ("psum", [128, 512], "float32"),
+    "pv": ("psum", [128, 2048], "float32"), "pz": ("psum", [128, 1536], "float32"), "px": ("psum", [128, 512], "float32"),
 }
 
 
@@ -43,16 +45,16 @@ def _codes(name, n):
     SCRATCH["s" + name] = ("sbuf", [128, n], "uint8")
 
 
-for _n, _w in (("KQ", 512), ("EQ", 512), ("SQ", 128), ("WQ", 128), ("XQ", 128), ("HQ3", 128)):
+for _n, _w in (("KQ", 512), ("EQ", 512), ("SQ", 128), ("WQ", 128), ("XQ", 128), ("HQ3", 128), ("KC", 128)):
     _codes(_n, _w)
 for _t in range(HOPS):
-    for _n, _w in (("HQ", 128), ("SD", 96), ("LA", 128), ("KC", 128), ("NW", 128), ("RW", 192)):
+    for _n, _w in (("SD", 96), ("LA", 128), ("NW", 128), ("RW", 192 if _t else 256)):
         _codes(_n + str(_t), _w)
 for _t in range(HOPS + 1):
     SCRATCH["NN%d" % _t] = ("sbuf", [128, 192], "int32")
-SEMAPHORES = ["cv", "cs", "ct", "cg", "ls", "dst", "dx", "dnx", "dnd", "nxr", "dky", "dw", "dh3", "dout"]
+SEMAPHORES = ["cv", "cs", "ct", "cg", "ls", "dst", "dx", "dno", "dnx", "dnd", "nxr", "dky", "dw", "dh3", "dout"]
 for _t in range(HOPS):
-    SEMAPHORES += ["aq%d" % _t, "av%d" % _t, "rq%d" % _t, "rc%d" % _t, "dh%d" % _t]
+    SEMAPHORES += ["aq%d" % _t, "av%d" % _t, "rq%d" % _t, "rc%d" % _t]
 
 
 def rank_program(g, core, T, topo):
@@ -93,9 +95,9 @@ def rank_program(g, core, T, topo):
         need("v", deps)
         return done("v", getv[name](*args), "cv", 1)
 
-    def S(out, in_, deps):
+    def S(out, in_, deps, *scale):
         need("s", deps)
-        return done("s", g.scalar.activation(out, in_, F.Copy), "cs", 1)
+        return done("s", g.scalar.activation(out, in_, F.Copy, *scale), "cs", 1)
 
     def MM(out, lc, ls, rc, rs, start, stop, deps):
         need("t", deps)
@@ -137,9 +139,10 @@ def rank_program(g, core, T, topo):
     def one(r, m, sem, src, dst):
         return RemoteDMATransfer(dst_ids=[coreid(r)], dma_engine_mask=m, remote_sem=T.sem[sem], src=src, dst=dst)
 
-    def send(sem, dst, src, deps):
+    def send(sem, t, dst, src, deps):
         need("g", deps)
-        fused([one(r, bits(part(me, r)), sem, src(b), dst((me - r - 1) % NR)) for b, r in enumerate(peers)])
+        fused([one(r, bits(part(me, r)), sem + str(t), L(src, t, 2 * b, 2 * b + 2), L(dst, t, 2 * ((me - r - 1) % NR), 2 * ((me - r - 1) % NR) + 2))
+               for b, r in enumerate(peers)])
         count["ls"] = count.get("ls", 0) + sum(len(part(me, r)) for r in peers)
 
     def by(x, a, b):
@@ -170,21 +173,19 @@ def rank_program(g, core, T, topo):
 
     for k in range(8):
         d_st = DMA("y" if k % 2 == 0 else "s", "dst", T.STW[16 * k:16 * k + 16, 0:4], T.st[:, :])
-    d_x = DMA("y", "dx", T.XT[:, 0:256], T.x[:, :])
     d_nd = DMA("s", "dnd", T.NXD[:, :], T.nx[:, :])
+    d_x = DMA("y", "dx", T.XT[:, 0:256], T.x[:, :])
     d_ky = DMA("s", "dky", T.KT[:, 0:1024], T.ky[:, 0:1024])
     d_ky = DMA("y", "dky", T.KT[:, 1024:2048], T.ky[:, 1024:2048])
     for k in range(8):
-        d_nx = DMA("y", "dnx", T.NXW[16 * k:16 * k + 16, 96:128], T.nx[:, :])
+        d_no = DMA("y", "dno", T.NXV[16 * k:16 * k + 16, 0:32], T.nx[:, :])
     d_w = DMA("y", "dw", T.WT[:, :], T.w[:, :])
 
     i_pi = IOTA(T.PI[:, 0:1], [[0, 1]], 0, 1)
     i_jp = IOTA(T.JP[:, :], [[1, 128]], 0, -1)
-    i_np = IOTA(T.NODF[:, :], [[1, 512]], off, 0, True)
+    i_ni = IOTA(T.NODI[:, :], [[1, 512]], off, 0)
     i_kp = IOTA(T.KP[:, :], [[-16, 8]], 0, 1)
-    i_k16 = IOTA(T.K16[:, 0:4], [[16, 4]], 0, 0)
     i_io4 = IOTA(T.IO4[:, 0:4], [[1, 4]], 0, 0)
-    i_na = IOTA(T.NA[:, :], [[-1, 64]], -129, 0, True)
     need("g", [d_nd])
     e16 = topo.engines(core, cores[peers[0]])
     fused([RemoteDMATransfer(dst_ids=[coreid(r) for r in peers], dma_engine_mask=bits(e16), remote_sem=T.sem.nxr, srcs=[T.NXD[:, :]],
@@ -192,202 +193,295 @@ def rank_program(g, core, T, topo):
     count["ls"] = len(e16)
 
     m_rs = V("set", [], T.RS64[:, :], 1.0)
-    m_r16 = V("set", [], T.RS16[:, :], 1.0)
-    m_xt = V("set", [], T.XT[:, 256:512], 0.0)
-    m_rs = V("set", [m_rs], T.RS64[:, 0:512:64], 0.0)
-    m_r16 = V("set", [m_r16], T.RS16[:, 0:128:16], 0.0)
     k_pj = V("ts", [i_pi], T.PJ[:, 0:1], T.PI[:, 0:1], 15, None, A.bitwise_and)
-    m_xs = V("set", [], T.XS[:, :], 0.0)
+    m_rs = V("set", [m_rs], T.RS64[:, 0:512:64], 0.0)
     k_t0 = V("ts", [k_pj], T.THR[:, 0:1], T.PJ[:, 0:1], 0.0, None, A.add)
     k_t1 = V("ts", [k_pj], T.THR[:, 1:2], T.PJ[:, 0:1], 16.0, None, A.add)
-    k_jpa = V("ts", [i_jp], T.JPA[:, :], T.JP[:, :], 15, None, A.bitwise_and)
     k_id = V("ts", [i_jp], T.ID[:, :], T.JP[:, :], 0.0, 0.5, A.is_equal, A.mult)
+    k_jpa = V("ts", [i_jp], T.JPA[:, :], T.JP[:, :], 15, None, A.bitwise_and)
+    m_xt = V("set", [], T.XT[:, 256:512], 0.0)
+    m_r16 = V("set", [], T.RS16[:, :], 1.0)
     K["d16"] = V("ts", [k_jpa], T.D16[:, :], T.JPA[:, :], 0.0, None, A.is_equal)
     for b in range(4):
-        need("s", [m_rs])
-        m_e = done("s", g.scalar.activation(T.ET[:, 512 * b:512 * b + 512], T.RS64[:, :], F.Copy, 0.0, 0.0), "cs", 1)
-    for b in range(4):
-        k_e = S(T.ET[:, 512 * b + b:512 * b + 512:4], T.ID[:, :], [m_e, k_id])
-    for b in range(4):
-        k_s = S(T.ST[:, b:512:4], T.D16[:, :], [K["d16"]])
+        m_e = S(T.ET[:, 512 * b:512 * b + 512], T.RS64[:, :], [m_rs], 0.0, 0.0)
+    for b in range(2):
+        S(T.ET[:, 512 * b + b:512 * b + 512:4], T.ID[:, :], [m_e, k_id])
 
-    k_st = V("copy", [d_st], T.STU[:, :], T.STW[:, :])
-    node = V("copy", [k_st, i_np], T.NN0[:, 128:192], T.NODF[:, 0:512].indirect(T.STU[:, 0:4]))
-
-    def lists(t, bt, vt, mid):
+    def lists(t, bt, gap):
+        gap(0)
         for b in range(4):
             mk = V("ts", [bt], T.MK[:, 64 * b:64 * b + 64], T.BT[:, :], float(b), None, A.is_equal)
-        vt = vt()
+        gap(1)
         px = V("scan", [mk, m_rs], T.PX[:, :], T.RS64[:, 0:256], T.MK[:, :], 0.0, A.mult, A.add)
+        gap(2)
         cn = V("ts", [px, k_t0], T.CN[:, 0:256], T.PX[:, :], T.THR[:, 0:1], None, A.is_le)
         cn = V("ts", [px, k_t1], T.CN[:, 256:512], T.PX[:, :], T.THR[:, 1:2], None, A.is_le)
+        gap(3)
         sc = V("scan", [cn], T.SC[:, :], T.RS64[:, :], T.CN[:, :], 0.0, A.mult, A.add)
-        hq = mid()
+        gap(4)
         for h in range(2):
             al = V("ts", [sc], L("AL", t, h, 8, 2), T.SC[:, 256 * h + 63:256 * h + 256:64], 63.0, None, A.min)
-        return al, vt, hq
+        gap(5)
+        return al
 
-    def depart(t, al, vt, hq):
-        c, s = T["cHQ%d" % t], T["sHQ%d" % t]
-        p2 = S(T["sSD%d" % t][:, 0:96], s[:, 0:64].indirect(L("AL", t, 0, 6)), [al] + hq)
-        o2 = S(T["sLA%d" % t][:, 96:128], s[:, 0:64].indirect(L("AL", t, 6, 8)), [al] + hq)
-        p1 = V("copy", [al] + hq, wd(T["cSD%d" % t], 0, 96), wd(c, 0, 64).indirect(L("AL", t, 0, 6)))
-        vd = V("tt", [vt, al, K["d16"]], T.VD[:, :], T.VT[:, 0:64].indirect(L("AL", t, 0, 8)), T.D16[:, :], A.mult)
-        o1 = V("copy", [], wd(T["cLA%d" % t], 96, 128), wd(c, 0, 64).indirect(L("AL", t, 6, 8)))
-        ve = V("scan", [vd, m_r16], T.VE[:, :], T.RS16[:, :], T.VD[:, :], 0.0, A.mult, A.add)
-        vs = V("ts", [ve], L("VS", t, 0, 8), T.VE[:, 15:128:16], 4.0, None, A.mult)
+    def diag(t, al):
+        return V("tt", [K["vt"], al, K["d16"]], T.VD[:, :], T.VT[:, 0:64].indirect(L("AL", t, 0, 8)), T.D16[:, :], A.mult)
+
+    def depart(t, al, held):
+        c, s = T["cRW%d" % t], T["sRW%d" % t]
+        p2 = S(T["sSD%d" % t][:, 0:96], s[:, 128:192].indirect(L("AL", t, 0, 6)), [al] + held)
+        p1 = V("copy", [al] + held, wd(T["cSD%d" % t], 0, 96), wd(c, 128, 192).indirect(L("AL", t, 0, 6)))
         sendcols("aq%d" % t, "LA%d" % t, "SD%d" % t, [p1, p2])
-        send("av%d" % t, lambda b: L("VL", t, 2 * b, 2 * b + 2), lambda b: L("VS", t, 2 * b, 2 * b + 2), [vs])
-        DMA("y", "dh%d" % t, by(T["cRW%d" % t], 128, 192), by(c, 0, 64), hq)
-        dh = DMA("y", "dh%d" % t, T["sRW%d" % t][:, 128:192], s[:, 0:64], hq)
-        return [o1, o2], vs, dh
+        return S(T["sLA%d" % t][:, 96:128], s[:, 128:192].indirect(L("AL", t, 6, 8)), [al] + held)
 
-    def server(t, own, vs, prev, aside):
+    def tell(t, al, vd, held, o2):
+        o1 = V("copy", [al] + held, wd(T["cLA%d" % t], 96, 128), wd(T["cRW%d" % t], 128, 192).indirect(L("AL", t, 6, 8)))
+        ve = V("scan", [vd, K["r16"]], T.VE[:, :], T.RS16[:, :], T.VD[:, :], 0.0, A.mult, A.add)
+        vs = V("ts", [ve], L("VS", t, 0, 8), T.VE[:, 15:128:16], 4.0, None, A.mult)
+        send("av", t, "VL", "VS", [vs])
+        return [o1, o2], vs
+
+    def eq(b):
+        return T.cEQ[:, 128 * b:128 * b + 128], T.sEQ[:, 128 * b:128 * b + 128]
+
+    def server(t, own, vs, prev, aside, step):
         KQ, sKQ = T.cKQ, T.sKQ
         LA, sLA = T["cLA%d" % t], T["sLA%d" % t]
-        land = [("aq%d" % t, COLS)] + own
-        z0 = MM(T.pz[:, 0:CUT], LA[:, 0:128], sLA[:, 0:128], KQ[:, 0:CUT], sKQ[:, 0:CUT], True, True, land + [K["kq"]] + prev["z"])
-        z1 = MM(T.pz[:, 512:1024 - CUT], LA[:, 0:128], sLA[:, 0:128], KQ[:, CUT:512], sKQ[:, CUT:512], True, True, [])
-        for b in range(4):
-            MM(T.pv[:, 512 * b:512 * b + 128], T.cEQ[:, 128 * b:128 * b + 128], T.sEQ[:, 128 * b:128 * b + 128],
-               LA[:, 0:128], sLA[:, 0:128], True, False, [K["eq"]] + prev["pv"])
-        c1 = S(T.ZS[:, CUT:512], T.pz[:, 512:1024 - CUT], [z1] + prev["zs"])
+        land = [("aq%d" % t, COLS)] + own + [K["kq"]]
+        z = []
+        for i in range(3):
+            a, b = CUTS[i], CUTS[i + 1]
+            z.append(MM(T.pz[:, 512 * i:512 * i + b - a], LA[:, 0:128], sLA[:, 0:128], KQ[:, a:b], sKQ[:, a:b], True, True, land + [prev["z"][i]]))
+
+        def zcopy(i):
+            return T.ZS[:, CUTS[i]:CUTS[i + 1]], T.pz[:, 512 * i:512 * i + CUTS[i + 1] - CUTS[i]]
+
+        def half(b):
+            return MM(T.pv[:, 512 * b:512 * b + 128], *eq(b), LA[:, 0:128], sLA[:, 0:128], True, t > 0, [K["eq"], prev["pv"][b]])
+
+        dq = [half(b) for b in range(2)]
+        c0 = S(*zcopy(0), [z[0], prev["t64"]])
+        if t > 0:
+            d = [S(T.DQ[:, 128 * b:128 * b + 128], T.pv[:, 512 * b:512 * b + 128], [dq[b], prev["ht"]]) for b in range(2)]
+        aside(3)
         V("tt", [vs, K["m8"]], T.T8[:, 6:8], L("VS", t, 6, 8), T.M8[:, 6:8], A.mult)
+        V("copy", [vs], T.VA[:, 6:8], L("VS", t, 6, 8))
         b8 = V("tt", [("av%d" % t, LIST)], T.T8[:, 0:6], L("VL", t, 0, 6), T.M8[:, 0:6], A.mult)
-        c0 = V("copy", [z0], T.ZS[:, 0:CUT], T.pz[:, 0:CUT])
+        va = V("copy", [], T.VA[:, 0:6], L("VL", t, 0, 6))
+        vr = V("tt", [i_tb], T.VR[:, 0:6], L("VL", t, 0, 6), T.TB[:, 0:6], A.add) if t > 0 else None
         vp = V("red", [b8], T.VP[:, 0:1], T.T8[:, :], AxisListType.X, A.add)
+        c1 = V("copy", [z[1]], *zcopy(1))
         z4 = V("ts", [vp, i_io4], L("Z4", t, 0, 4), T.IO4[:, 0:4], T.VP[:, 0:1], None, A.add)
-        t64 = V("tt", [c0, c1, z4, K["nm"]], T.T64[:, :], T.ZS[:, 0:512].indirect(L("Z4", t, 0, 4)), T.NM64[:, :], A.add)
+        c2 = V("copy", [z[2]], *zcopy(2))
+        t64 = V("tt", [c0, c1, c2, z4, K["nm"]], T.T64[:, :], T.ZS[:, 0:512].indirect(L("Z4", t, 0, 4)), T.NM64[:, :], A.add)
+        step()
         rm = V("scan", [t64], T.RM[:, :], T.T64[:, :], T.T64[:, :], -BIG, A.max, A.max)
+        step()
         for u in range(3):
-            xs = V("ts", [rm, m_xs, K["m8"]], T.XS[:, u:32:4], T.NMK[:, :], T.RM[:, 16 * u + 15:16 * u + 16], T.RM[:, 63:64], A.add, A.is_lt)
+            xs = V("ts", [rm, K["xs"], K["nk"]], T.XS[:, u:32:4], T.NMK[:, :], T.RM[:, 16 * u + 15:16 * u + 16], T.RM[:, 63:64], A.add, A.is_lt)
+        step()
         xq = V("q", [xs, prev["xm"]], T.cXQ[:, 0:128], T.sXQ[:, 0:128], T.XS[:, :])
         xm = MM(T.px[:, 0:128], T.cSQ[:, 0:128], T.sSQ[:, 0:128], T.cXQ[:, 0:128], T.sXQ[:, 0:128], True, True, [xq, K["sq"], prev["of"]])
-        V("tt", [xm], T.OF[:, 0:6], T.px[:, 0:6], L("VL", t, 0, 6), A.add)
-        of = V("tt", [xm], T.OF[:, 6:8], T.px[:, 6:8], L("VS", t, 6, 8), A.add)
-        ou = V("copy", [of], L("OU", t, 0, 8), T.OF[:, :])
-        send("rc%d" % t, lambda b: L("CL", t, 2 * b, 2 * b + 2), lambda b: L("OU", t, 2 * b, 2 * b + 2), [ou])
-        kc = V("copy", [ou, K["kq"]], wd(T["cKC%d" % t], 0, 128), wd(KQ, 0, 512).indirect(L("OU", t, 0, 8)))
-        ks = S(T["sKC%d" % t][:, 0:128], sKQ[:, 0:512].indirect(L("OU", t, 0, 8)), [ou, K["kq"]])
+        dq += [half(b) for b in range(2, 4)]
         aside(0)
-        h = []
-        for b in range(4):
-            km = MM(T.pv[:, 512 * b:512 * b + 128], T.cEQ[:, 128 * b:128 * b + 128], T.sEQ[:, 128 * b:128 * b + 128],
-                    T["cKC%d" % t][:, 0:128], T["sKC%d" % t][:, 0:128], False, True, [kc, ks])
-            o, i = T.HT[:, b:512:4], T.pv[:, 512 * b:512 * b + 128]
-            h.append(S(o, i, [km, prev["nq"]]) if b % 2 == 0 else V("copy", [km, prev["nq"]], o, i))
-        aside(1)
+        step()
+        step()
+        if t > 0:
+            og = V("tt", [xm, vr], T.OG[:, 0:6], T.px[:, 0:6], T.VR[:, 0:6], A.add)
+            of = V("tt", [xm, va], T.OF[:, :], T.px[:, 0:8], T.VA[:, :], A.add)
+            told = V("copy", [og], L("OR", t, 0, 6), T.OG[:, 0:6])
+            send("rc", t, "CL", "OR", [told])
+        else:
+            of = V("tt", [xm, va], T.OF[:, :], T.px[:, 0:8], T.VA[:, :], A.add)
+        ou = V("copy", [of], L("OU", t, 0, 8), T.OF[:, :])
+        step()
+        if t == 0:
+            ks = S(T.sKC[:, 0:128], sKQ[:, 0:512].indirect(L("OU", t, 0, 8)), [ou, K["kq"]])
+            nd = V("tt", [ou, K["t3"], K["d16"]], T.VD[:, :], T.NXA[:, 1536:2048].indirect(L("OU", t, 0, 8)), T.D16[:, :], A.mult)
+            kc = V("copy", [ou], wd(T.cKC, 0, 128), wd(KQ, 0, 512).indirect(L("OU", t, 0, 8)))
+            ne = V("scan", [nd], T.VE[:, :], T.RS16[:, :], T.VD[:, :], 0.0, A.mult, A.add)
+            told = V("ts", [ne], L("OR", t, 0, 8), T.VE[:, 15:128:16], float(-off), None, A.add)
+            send("rc", t, "CL", "OR", [told])
+            aside(1)
+            h = []
+            for b in range(4):
+                km = MM(T.pv[:, 512 * b:512 * b + 128], *eq(b), T.cKC[:, 0:128], T.sKC[:, 0:128], False, True, [kc, ks])
+                o, i = T.HT[:, b:512:4], T.pv[:, 512 * b:512 * b + 128]
+                h.append(S(o, i, [km]) if b % 2 == 0 else V("copy", [km], o, i))
+            ready = h
+            ht = None
+        else:
+            def chosen(b):
+                return T.DK[:, 512 * b:512 * b + 512].indirect(L("OU", t, 0, 8))
+
+            gk = [S(T.GK[:, 128 * b:128 * b + 128], chosen(2 + b), [ou, prev["ht"]] + K["dk"]) for b in range(2)]
+            aside(1)
+            for b in range(2):
+                V("tt", [ou, d[b], prev["nq"]] + K["dk"], T.HT[:, b:512:4], chosen(b), T.DQ[:, 128 * b:128 * b + 128], A.add)
+            ready = [V("tt", [dq[2 + b], gk[b]], T.HT[:, 2 + b:512:4], T.pv[:, 512 * (2 + b):512 * (2 + b) + 128], T.GK[:, 128 * b:128 * b + 128], A.add)
+                     for b in range(2)]
+            h = d + ready
+            ht = ready[1]
+        step()
         C, P = T["cNW%d" % t], T["sNW%d" % t]
-        nq = V("q", h, C[:, 0:128], P[:, 0:128], T.HT[:, :])
+        nq = V("q", ready, C[:, 0:128], P[:, 0:128], T.HT[:, :])
         sendcols("rq%d" % t, "RW%d" % t, "NW%d" % t, [nq])
+        prev.update({"z": [c0, c1, c2], "pv": h, "t64": t64, "ht": ht, "xm": xm, "of": of, "nq": nq})
         w1 = V("copy", [nq, K["id"]], wd(T["cRW%d" % t], 96, 128), wd(C, 96, 128).indirect(T.IDL[:, 0:2]))
         w2 = S(T["sRW%d" % t][:, 96:128], P[:, 96:128].indirect(T.IDL[:, 0:2]), [nq, K["id"]])
-        prev.update({"z": [c0, c1], "pv": h, "zs": [t64], "xm": xm, "of": of, "nq": nq})
-        return [w1, w2], ou
+        aside(2)
+        return [w1, w2], ou, told
 
-    def where(t, fill):
+    def where(t):
         u = V("tt", [], T.UU[:, :], T.PX[:, :], T.MK[:, :], A.mult)
-        fill(0)
         q1 = V("ts", [], T.Q1[:, :], T.BT[:, :], 32.0, None, A.mult)
         u = V("tt", [u], T.U2[:, :], T.UU[:, 0:128], T.UU[:, 128:256], A.add)
         q2 = V("tt", [q1, i_na], T.Q2[:, :], T.Q1[:, :], T.NA[:, :], A.add)
         p = V("tt", [u], T.PP[:, :], T.U2[:, 0:64], T.U2[:, 64:128], A.add)
+        yield None
         sv = V("ts", [p], T.SV[:, :], T.PP[:, :], float(CAP), None, A.is_le)
         q3 = V("tt", [q2, p], T.Q3[:, :], T.Q2[:, :], T.PP[:, :], A.add)
+        yield None
         q4 = V("tt", [sv], T.Q4[:, :], T.SV[:, :], T.D16[:, 0:64], A.mult)
-        fill(1)
+        yield None
         q5 = V("tt", [q3, q4], T.Q5[:, :], T.Q3[:, :], T.Q4[:, :], A.mult)
-        fill(2)
+        yield None
         q6 = V("scan", [q5], T.Q6[:, :], T.RS16[:, 0:64], T.Q5[:, :], 0.0, A.mult, A.add)
+        yield None
         q7 = V("tt", [q6, K["aw"]], T.Q7[:, :], T.Q6[:, 15:64:16], T.AW[:, :], A.add)
-        return V("copy", [q7], L("SL", t, 0, 4), T.Q7[:, :])
+        yield None
+        K["sl"] = V("copy", [q7], L("SL", t, 0, 4), T.Q7[:, :])
+        while True:
+            yield None
 
-    def order(t, sl, own, dh):
-        deps = own + [sl, dh, ("rq%d" % t, COLS)]
-        c, s = T["cHQ%d" % (t + 1)], T["sHQ%d" % (t + 1)]
-        h2 = S(s[:, 0:64], T["sRW%d" % t][:, 0:192].indirect(L("SL", t, 0, 4)), deps)
-        h1 = V("copy", deps, wd(c, 0, 64), wd(T["cRW%d" % t], 0, 192).indirect(L("SL", t, 0, 4)))
+    def order(t, deps, c, s, o):
+        h2 = S(s[:, o:o + 64], T["sRW%d" % t][:, 0:192].indirect(L("SL", t, 0, 4)), deps)
+        h1 = V("copy", deps, wd(c, o, o + 64), wd(T["cRW%d" % t], 0, 192).indirect(L("SL", t, 0, 4)))
         return [h1, h2]
 
     def table(b):
-        return T.NXA[:, 512 * b:512 * b + 512], T.NODF[:, 0:512].indirect(T.NXU[:, 32 * b:32 * b + 32])
+        return S(T.NXA[:, 512 * b:512 * b + 512], T.NODF[:, 0:512].indirect(T.NXU[:, 32 * b:32 * b + 32]), [K["no"] if b == 3 else K["nu"], K["nf"]])
 
-    prev = {"z": [], "pv": [], "zs": [], "xm": None, "of": None, "nq": None}
-    bt = V("ts", [node], T.BT[:, :], T.NN0[:, 128:192], 7, 3, A.logical_shift_right, A.bitwise_and)
-    hq0 = []
+    def dkc(b):
+        K["dk"].append(S(T.DK[:, 512 * b:512 * b + 512], T.pv[:, 512 * b:512 * b + 512], [K["um"][b]]))
 
-    def vt0():
-        return V("ts", [node], T.VT[:, :], T.NN0[:, 128:192], 127, None, A.bitwise_and)
+    k_st = V("copy", [d_st], T.STU[:, :], T.STW[:, :])
+    start = T.NODI[:, 0:512].indirect(T.STU[:, 0:4])
+    bt = V("ts", [k_st, i_ni], T.BT[:, :], start, 7, 3, A.logical_shift_right, A.bitwise_and)
 
-    def mid0():
-        hq0.append(V("q", [d_x, m_xt], T.cHQ0[:, 0:128], T.sHQ0[:, 0:128], T.XT[:, :]))
-        return hq0
+    def gap0(k):
+        if k == 0:
+            K["node"] = V("copy", [], T.NN0[:, 128:192], start)
+        if k == 1:
+            K["r16"] = V("set", [m_r16], T.RS16[:, 0:128:16], 0.0)
+        if k == 2:
+            K["vt"] = V("ts", [K["node"]], T.VT[:, :], T.NN0[:, 128:192], 127, None, A.bitwise_and)
+        if k == 3:
+            K["held"] = [V("q", [d_x, m_xt], T.cRW0[:, 128:256], T.sRW0[:, 128:256], T.XT[:, :])]
 
-    al, vt, hq = lists(0, bt, vt0, mid0)
-    for t in range(HOPS):
-        own, vs, dh = depart(t, al, vt, hq)
-        if t == 0:
-            k_kp = V("ts", [i_kp], T.KP2[:, :], T.KP[:, :], 4, None, A.arith_shift_right)
-            K["nm"] = V("ts", [K["d16"]], T.NM64[:, :], T.D16[:, 0:64], -1.0, BIG, A.add, A.mult)
-            V("ts", [k_kp], T.M8[:, :], T.KP2[:, :], 0.0, None, A.is_equal)
-            K["m8"] = V("ts", [k_kp], T.NMK[:, :], T.KP2[:, :], 0.0, BIG, A.not_equal, A.mult)
+    al = lists(0, bt, gap0)
+    held, node = K["held"], K["node"]
+    hq0 = held[0]
+    o2 = depart(0, al, held)
+    vd = diag(0, al)
+    own, vs = tell(0, al, vd, held, o2)
+    i_na = IOTA(T.NA[:, :], [[-1, 64]], -129, 0, True)
+    i_k16 = IOTA(T.K16[:, 0:4], [[16, 4]], 0, 0)
+    i_tb = IOTA(T.TB[:, 0:6], [[-512, 3], [0, 2]], 1024, 0, True)
+    for b in range(2, 4):
+        k_e = S(T.ET[:, 512 * b + b:512 * b + 512:4], T.ID[:, :], [m_e, k_id])
+    for b in range(4):
+        k_s = S(T.ST[:, b:512:4], T.D16[:, :], [K["d16"]])
+    K["kq"] = V("q", [d_ky], T.cKQ[:, 0:512], T.sKQ[:, 0:512], T.KT[:, :])
+    k_kp = V("ts", [i_kp], T.KP2[:, :], T.KP[:, :], 4, None, A.arith_shift_right)
+    K["nm"] = V("ts", [K["d16"]], T.NM64[:, :], T.D16[:, 0:64], -1.0, BIG, A.add, A.mult)
+    K["m8"] = V("ts", [k_kp], T.M8[:, :], T.KP2[:, :], 0.0, None, A.is_equal)
+    K["nk"] = V("ts", [k_kp], T.NMK[:, :], T.KP2[:, :], 0.0, BIG, A.not_equal, A.mult)
+    K["nf"] = V("copy", [i_ni], T.NODF[:, :], T.NODI[:, :])
+    K["no"] = V("copy", [d_no], T.NXU[:, 96:128], T.NXV[:, :])
+    K["xs"] = V("set", [], T.XS[:, :], 0.0)
+    K["eq"] = V("q", [k_e], T.cEQ[:, 0:512], T.sEQ[:, 0:512], T.ET[:, :])
+    K["t3"] = table(3)
+    K["sq"] = V("q", [k_s], T.cSQ[:, 0:128], T.sSQ[:, 0:128], T.ST[:, :])
+    for b in range(3):
+        for k in range(8):
+            d_nx = DMA("y", "dnx", T.NXW[16 * k:16 * k + 16, 32 * b:32 * b + 32], T["NXR%d" % b][:, :], [("nxr", 3 * len(e16))])
+    DMA("y", "dh3", by(T.cHQ3, 64, 128), by(T.cRW0, 192, 256), [hq0])
+    d_h3 = DMA("y", "dh3", T.sHQ3[:, 64:128], T.sRW0[:, 192:256], [hq0])
+    find = where(0)
+    next(find)
+
+    def aside0(k):
+        if k == 0:
             K["id"] = V("ts", [k_t0, i_k16], T.IDL[:, :], T.K16[:, 0:2], T.THR[:, 0:1], None, A.add)
             K["aw"] = V("ts", [k_t0, i_k16], T.AW[:, :], T.K16[:, 0:4], T.THR[:, 0:1], 128.0, A.add, A.add)
-            DMA("y", "dh3", by(T.cHQ3, 64, 128), by(T.cHQ0, 64, 128), hq0)
-            d_h3 = DMA("y", "dh3", T.sHQ3[:, 64:128], T.sHQ0[:, 64:128], hq0)
-            for b in range(3):
-                for k in range(8):
-                    d_nx = DMA("y", "dnx", T.NXW[16 * k:16 * k + 16, 32 * b:32 * b + 32], T["NXR%d" % b][:, :], [("nxr", 3 * len(e16))])
-        if t == 1:
+        if k == 2:
+            K["dk"] = []
+            K["um"] = [MM(T.pv[:, 512 * b:512 * b + 512], *eq(b), T.cKQ[:, 0:512], T.sKQ[:, 0:512], True, True, [prev["pv"][b]]) for b in range(4)]
+            for b in range(2):
+                dkc(b)
+
+    def aside1(k):
+        if k == 3:
+            K["nxa"].append(table(1))
+        if k == 1:
+            K["nxa"].append(table(2))
+        if k == 2:
             K["wq"] = V("q", [d_w], T.cWQ[:, 0:128], T.sWQ[:, 0:128], T.WT[:, :])
 
-        def fill(k):
-            if t == 0 and k == 0:
-                K["kq"] = V("q", [d_ky], T.cKQ[:, 0:512], T.sKQ[:, 0:512], T.KT[:, :])
-            if t == 0 and k == 1:
-                K["sq"] = V("q", [k_s], T.cSQ[:, 0:128], T.sSQ[:, 0:128], T.ST[:, :])
-            if t == 0 and k == 2:
-                K["eq"] = V("q", [k_e], T.cEQ[:, 0:512], T.sEQ[:, 0:512], T.ET[:, :])
-
-        def aside(k):
-            if t == 0 and k == 0:
-                K["nu"] = V("copy", [d_nx], T.NXU[:, :], T.NXW[:, :])
-            if t == 0 and k == 1:
-                for b in (1, 2):
-                    o, i = table(b)
-                    K["nxa"] = S(o, i, [K["nu"], i_np])
-
-        sl = where(t, fill)
-        own, ou = server(t, own, vs, prev, aside)
-        if t == 0:
-            for b in (3, 0):
-                o, i = table(b)
-                K["nxo"] = V("copy", [K["nu"], i_np], o, i)
-        V("ts", [node], T.ND[:, 64 * t:64 * t + 64], T["NN%d" % t][:, 128:192], float(-off), None, A.add)
+    prev = {"z": [None] * 3, "pv": [None] * 4, "t64": None, "ht": None, "xm": None, "of": None, "nq": None}
+    for t in range(HOPS):
         n = T["NN%d" % t]
-        V("copy", [ou, K["nxo"]], n[:, 96:128], T.NXA[:, 1536:2048].indirect(L("OU", t, 6, 8)))
-        for b in range(3):
-            g1 = V("copy", [("rc%d" % t, LIST), K["nxa"]], n[:, 32 * b:32 * b + 32], T.NXA[:, 512 * b:512 * b + 512].indirect(L("CL", t, 2 * b, 2 * b + 2)))
+        if t == 0:
+            back, ou, told = server(0, own, vs, prev, aside0, lambda: next(find))
+            mine, theirs, tabs = T.NODI[:, 0:512].indirect(L("OR", 0, 6, 8)), T.NODI[:, 0:512].indirect(L("CL", 0, 0, 6)), [told]
+        else:
+            find = where(t)
+            next(find)
+            if t == 1:
+                K["nu"] = V("copy", [d_nx], T.NXU[:, 0:96], T.NXW[:, :])
+                for b in range(2, 4):
+                    dkc(b)
+                prev["pv"] = K["dk"]
+                K["nxa"] = [K["t3"], table(0)]
+            back, ou, told = server(t, own, vs, prev, aside1 if t == 1 else lambda k: None, lambda: next(find))
+            mine, theirs, tabs = T.NXA[:, 1536:2048].indirect(L("OU", t, 6, 8)), T.NXA[:, 0:1536].indirect(L("CL", t, 0, 6)), [ou] + K["nxa"]
+        sl = K["sl"]
+        V("copy", tabs, n[:, 96:128], mine)
+        V("ts", [node], T.ND[:, 64 * t:64 * t + 64], n[:, 128:192], float(-off), None, A.add)
+        g1 = V("copy", [("rc%d" % t, LIST)], n[:, 0:96], theirs)
         byq = n[:, 0:192].indirect(L("SL", t, 0, 4))
+        got = held + back + [sl, ("rq%d" % t, COLS)]
 
         def nodes():
             return V("copy", [g1, sl, node], T["NN%d" % (t + 1)][:, 128:192], byq)
 
-        if t + 1 < HOPS:
-            bt = V("ts", [g1, sl, node], T.BT[:, :], byq, 7, 3, A.logical_shift_right, A.bitwise_and)
-            al, vt, hq = lists(t + 1, bt, lambda: V("ts", [g1, sl, node], T.VT[:, :], byq, 127, None, A.bitwise_and), lambda: order(t, sl, own, dh))
-            node = nodes()
-        else:
+        if t + 1 == HOPS:
             node = nodes()
             nd = V("ts", [node], T.ND[:, 64 * HOPS:64 * HOPS + 64], T["NN%d" % HOPS][:, 128:192], float(-off), None, A.add)
             DMA("y", "dout", T.nd[:, :], T.ND[0:1, 0:256], [nd])
-            hq = order(t, sl, own, dh)
+            hq = order(t, got, T.cHQ3, T.sHQ3, 0)
+            break
+        bt = V("ts", [g1, sl, node], T.BT[:, :], byq, 7, 3, A.logical_shift_right, A.bitwise_and)
+
+        def gap(k):
+            if k == 0:
+                K["vt"] = V("ts", [g1, sl, node], T.VT[:, :], byq, 127, None, A.bitwise_and)
+            if k == 1:
+                K["node"] = nodes()
+
+        al = lists(t + 1, bt, gap)
+        node = K["node"]
+        vd = diag(t + 1, al)
+        held = order(t, got, T["cRW%d" % (t + 1)], T["sRW%d" % (t + 1)], 128)
+        o2 = depart(t + 1, al, held)
+        own, vs = tell(t + 1, al, vd, held, o2)
 
     DMA("y", "dout", T.oc[:, :], by(T.cHQ3, 0, 64), [hq[0]])
     for k in range(4):
         DMA("s" if k < 2 else "y", "dout", T.osc[4 * k:4 * k + 4, 0:64], T.sHQ3[32 * k:32 * k + 4, 0:64], [hq[1]])
-    ym = MM(T.py[:, 0:128], T.cWQ[:, 0:128], T.sWQ[:, 0:128], T.cHQ3[:, 0:128], T.sHQ3[:, 0:128], True, True, hq + [K["wq"], d_h3])
-    yc = V("copy", [ym], T.YS[:, :], T.py[:, 0:64])
+    ym = MM(T.px[:, 0:128], T.cWQ[:, 0:128], T.sWQ[:, 0:128], T.cHQ3[:, 0:128], T.sHQ3[:, 0:128], True, True, hq + [K["wq"], d_h3, prev["of"]])
+    yc = V("copy", [ym], T.YS[:, :], T.px[:, 0:64])
     DMA("y", "dout", T.y[:, :], T.YS[:, :], [yc])
-    for sem in ("dout", "ls", "cv", "cs", "ct", "cg", "dst", "dx", "dky", "dnx", "dnd", "dw", "dh3", "dh0", "dh1", "dh2"):
+    for sem in ("dout", "ls", "cv", "cs", "ct", "cg", "dst", "dx", "dky", "dnx", "dno", "dnd", "dw", "dh3"):
         need("g", [(sem, count[sem])])

@@ -3,7 +3,7 @@ from concourse.mybir import dt, AluOpType as A, AxisListType, ActivationFunction
 
 NR, CAP, HOPS = 4, 32, 3
 BIG = 1e29
-CUTS = (0, 208, 384, 512)
+CUTS = (0, 128, 256, 384, 512)
 
 SCRATCH = {
     "STW": ("sbuf", [128, 4], "int32"), "STU": ("sbuf", [128, 4], "uint16"),
@@ -11,12 +11,13 @@ SCRATCH = {
     "NXW": ("sbuf", [128, 96], "int32"), "NXV": ("sbuf", [128, 32], "int32"), "NXU": ("sbuf", [128, 128], "uint16"), "NXA": ("sbuf", [128, 2048], "float32"),
     "NODF": ("sbuf", [128, 512], "float32"), "NODI": ("sbuf", [128, 512], "int32"),
     "JP": ("sbuf", [128, 128], "int32"), "JPA": ("sbuf", [128, 128], "int32"), "ID": ("sbuf", [128, 128], "bfloat16"),
-    "PI": ("sbuf", [128, 8], "int32"), "PJ": ("sbuf", [128, 8], "int32"), "THR": ("sbuf", [128, 8], "float32"),
-    "KP": ("sbuf", [128, 8], "int32"), "KP2": ("sbuf", [128, 8], "int32"), "M8": ("sbuf", [128, 8], "float32"), "NMK": ("sbuf", [128, 8], "float32"),
-    "IO4": ("sbuf", [128, 8], "int32"), "K16": ("sbuf", [128, 8], "int32"), "AW": ("sbuf", [128, 4], "float32"), "IDL": ("sbuf", [128, 2], "uint16"),
-    "TB": ("sbuf", [128, 8], "float32"),
-    "NA": ("sbuf", [128, 64], "float32"), "D16": ("sbuf", [128, 128], "float32"), "NM64": ("sbuf", [128, 64], "float32"),
-    "RS64": ("sbuf", [128, 512], "bfloat16"), "RS16": ("sbuf", [128, 128], "float32"),
+    "PI": ("sbuf", [128, 8], "int32"), "THR": ("sbuf", [128, 8], "float32"),
+    "KP": ("sbuf", [128, 8], "int32"), "KP2": ("sbuf", [128, 8], "int32"), "M8": ("sbuf", [128, 8], "float32"),
+    "XI": ("sbuf", [128, 8], "int32"), "XF": ("sbuf", [128, 8], "float32"), "XL": ("sbuf", [128, 2], "uint16"),
+    "IO4": ("sbuf", [128, 8], "int32"), "AW": ("sbuf", [128, 4], "float32"), "IDL": ("sbuf", [128, 2], "uint16"),
+    "TB": ("sbuf", [128, 8], "float32"), "IO": ("sbuf", [128, 16], "float32"), "C16": ("sbuf", [128, 16], "float32"),
+    "D16": ("sbuf", [128, 128], "float32"), "D16B": ("sbuf", [128, 256], "bfloat16"), "NM64": ("sbuf", [128, 64], "float32"),
+    "RS64": ("sbuf", [128, 512], "bfloat16"), "RS16": ("sbuf", [128, 128], "float32"), "RS16B": ("sbuf", [128, 256], "bfloat16"),
     "AL": ("sbuf", [128, 24], "uint16"),
     "VS": ("sbuf", [128, 24], "int32"),
     "VL": ("sbuf", [128, 24], "int32"),
@@ -27,11 +28,12 @@ SCRATCH = {
     "SL": ("sbuf", [128, 24], "uint16"),
     "BT": ("sbuf", [128, 64], "int32"), "VT": ("sbuf", [128, 64], "int32"), "MK": ("sbuf", [128, 256], "bfloat16"), "PX": ("sbuf", [128, 256], "bfloat16"),
     "CN": ("sbuf", [128, 512], "bfloat16"), "SC": ("sbuf", [128, 512], "bfloat16"), "VD": ("sbuf", [128, 128], "float32"), "VE": ("sbuf", [128, 128], "float32"),
-    "UU": ("sbuf", [128, 256], "bfloat16"), "U2": ("sbuf", [128, 128], "bfloat16"), "PP": ("sbuf", [128, 64], "float32"), "SV": ("sbuf", [128, 64], "float32"),
-    "Q1": ("sbuf", [128, 64], "float32"), "Q2": ("sbuf", [128, 64], "float32"), "Q3": ("sbuf", [128, 64], "float32"), "Q4": ("sbuf", [128, 64], "float32"),
-    "Q5": ("sbuf", [128, 64], "float32"), "Q6": ("sbuf", [128, 64], "float32"), "Q7": ("sbuf", [128, 4], "float32"), "ND": ("sbuf", [128, 256], "float32"),
+    "VDB": ("sbuf", [128, 128], "bfloat16"), "VEB": ("sbuf", [128, 128], "bfloat16"),
+    "MD": ("sbuf", [128, 256], "bfloat16"), "UD": ("sbuf", [128, 256], "bfloat16"), "FF": ("sbuf", [128, 256], "bfloat16"),
+    "WW": ("sbuf", [128, 96], "float32"), "ND": ("sbuf", [128, 256], "float32"),
     "VA": ("sbuf", [128, 8], "float32"), "VR": ("sbuf", [128, 8], "float32"), "VP": ("sbuf", [128, 8], "float32"), "T8": ("sbuf", [128, 8], "float32"),
-    "ZS": ("sbuf", [128, 512], "float32"), "T64": ("sbuf", [128, 64], "float32"), "RM": ("sbuf", [128, 64], "float32"),
+    "ZS": ("sbuf", [128, 512], "float32"), "T64": ("sbuf", [128, 64], "float32"),
+    "RM": ("sbuf", [128, 72], "float32"),
     "XS": ("sbuf", [128, 512], "bfloat16"), "OF": ("sbuf", [128, 8], "float32"), "OG": ("sbuf", [128, 8], "float32"), "HT": ("sbuf", [128, 512], "bfloat16"),
     "DK": ("sbuf", [128, 2048], "float32"), "DQ": ("sbuf", [128, 256], "float32"), "GK": ("sbuf", [128, 256], "float32"),
     "XT": ("sbuf", [128, 512], "bfloat16"), "KT": ("sbuf", [128, 2048], "bfloat16"), "WT": ("sbuf", [128, 512], "bfloat16"),
@@ -182,10 +184,9 @@ def rank_program(g, core, T, topo):
     d_w = DMA("y", "dw", T.WT[:, :], T.w[:, :])
 
     i_pi = IOTA(T.PI[:, 0:1], [[0, 1]], 0, 1)
-    i_jp = IOTA(T.JP[:, :], [[1, 128]], 0, -1)
     i_ni = IOTA(T.NODI[:, :], [[1, 512]], off, 0)
+    i_jp = IOTA(T.JP[:, :], [[1, 128]], 0, -1)
     i_kp = IOTA(T.KP[:, :], [[-16, 8]], 0, 1)
-    i_io4 = IOTA(T.IO4[:, 0:4], [[1, 4]], 0, 0)
     need("g", [d_nd])
     e16 = topo.engines(core, cores[peers[0]])
     fused([RemoteDMATransfer(dst_ids=[coreid(r) for r in peers], dma_engine_mask=bits(e16), remote_sem=T.sem.nxr, srcs=[T.NXD[:, :]],
@@ -193,53 +194,62 @@ def rank_program(g, core, T, topo):
     count["ls"] = len(e16)
 
     m_rs = V("set", [], T.RS64[:, :], 1.0)
-    k_pj = V("ts", [i_pi], T.PJ[:, 0:1], T.PI[:, 0:1], 15, None, A.bitwise_and)
+    k_pj = V("ts", [i_pi], T.XI[:, 4:5], T.PI[:, 0:1], 15, None, A.bitwise_and)
     m_rs = V("set", [m_rs], T.RS64[:, 0:512:64], 0.0)
-    k_t0 = V("ts", [k_pj], T.THR[:, 0:1], T.PJ[:, 0:1], 0.0, None, A.add)
-    k_t1 = V("ts", [k_pj], T.THR[:, 1:2], T.PJ[:, 0:1], 16.0, None, A.add)
-    k_id = V("ts", [i_jp], T.ID[:, :], T.JP[:, :], 0.0, 0.5, A.is_equal, A.mult)
-    k_jpa = V("ts", [i_jp], T.JPA[:, :], T.JP[:, :], 15, None, A.bitwise_and)
+    k_t0 = V("ts", [k_pj], T.THR[:, 0:1], T.XI[:, 4:5], 0.0, None, A.add)
+    k_t1 = V("ts", [k_pj], T.THR[:, 1:2], T.XI[:, 4:5], 16.0, None, A.add)
+    k_th = [k_t0, k_t1]
+    x_a = V("ts", [k_pj], T.XI[:, 0:1], T.XI[:, 4:5], 2, None, A.arith_shift_right)
+    x_u = V("ts", [i_pi], T.XI[:, 3:4], T.PI[:, 0:1], 1.0, None, A.add)
+    x_g = V("ts", [i_pi], T.XI[:, 2:3], T.PI[:, 0:1], 4, None, A.arith_shift_right)
+    x_b = V("ts", [x_a], T.XI[:, 1:2], T.XI[:, 0:1], 4.0, None, A.add)
+    x_u = V("ts", [x_u], T.XI[:, 5:6], T.XI[:, 3:4], 3, None, A.bitwise_and)
+    x_g = V("copy", [x_g], T.XF[:, 0:1], T.XI[:, 2:3])
+    x_m = V("set", [], T.RM[:, 0:8], BIG)
+    x_u = V("ts", [x_u], T.XF[:, 1:2], T.XI[:, 5:6], 16.0, 7.0, A.mult, A.add)
     m_xt = V("set", [], T.XT[:, 256:512], 0.0)
-    m_r16 = V("set", [], T.RS16[:, :], 1.0)
-    K["d16"] = V("ts", [k_jpa], T.D16[:, :], T.JPA[:, :], 0.0, None, A.is_equal)
-    for b in range(4):
-        m_e = S(T.ET[:, 512 * b:512 * b + 512], T.RS64[:, :], [m_rs], 0.0, 0.0)
-    for b in range(2):
-        S(T.ET[:, 512 * b + b:512 * b + 512:4], T.ID[:, :], [m_e, k_id])
+    m_r16 = V("set", [], T.RS16B[:, :], 1.0)
+    m_r16f = V("set", [], T.RS16[:, :], 1.0)
+    x_e = V("ts", [x_b, x_g, x_u], T.XF[:, 2:4], T.XI[:, 0:2], T.XF[:, 0:1], T.XF[:, 1:2], A.is_equal, A.mult)
 
     def lists(t, bt, gap):
         gap(0)
+        mk = []
         for b in range(4):
-            mk = V("ts", [bt], T.MK[:, 64 * b:64 * b + 64], T.BT[:, :], float(b), None, A.is_equal)
+            mk.append(V("ts", [bt], T.MK[:, 64 * b:64 * b + 64], T.BT[:, :], float(b), None, A.is_equal))
         gap(1)
-        px = V("scan", [mk, m_rs], T.PX[:, :], T.RS64[:, 0:256], T.MK[:, :], 0.0, A.mult, A.add)
+        px = [V("scan", [mk[2 * h + 1], m_rs], T.PX[:, 128 * h:128 * h + 128], T.RS64[:, 0:128], T.MK[:, 128 * h:128 * h + 128], 0.0, A.mult, A.add)
+              for h in range(2)]
         gap(2)
-        cn = V("ts", [px, k_t0], T.CN[:, 0:256], T.PX[:, :], T.THR[:, 0:1], None, A.is_le)
-        cn = V("ts", [px, k_t1], T.CN[:, 256:512], T.PX[:, :], T.THR[:, 1:2], None, A.is_le)
+        cn = [V("ts", [px[1], k_th[h]], T.CN[:, 256 * h:256 * h + 256], T.PX[:, :], T.THR[:, h:h + 1], None, A.is_le) for h in range(2)]
         gap(3)
-        sc = V("scan", [cn], T.SC[:, :], T.RS64[:, :], T.CN[:, :], 0.0, A.mult, A.add)
+        sc = [V("scan", [cn[h]], T.SC[:, 256 * h:256 * h + 256], T.RS64[:, 0:256], T.CN[:, 256 * h:256 * h + 256], 0.0, A.mult, A.add) for h in range(2)]
         gap(4)
         for h in range(2):
-            al = V("ts", [sc], L("AL", t, h, 8, 2), T.SC[:, 256 * h + 63:256 * h + 256:64], 63.0, None, A.min)
+            al = V("ts", [sc[h]], L("AL", t, h, 8, 2), T.SC[:, 256 * h + 63:256 * h + 256:64], 63.0, None, A.min)
         gap(5)
         return al
 
     def diag(t, al):
-        return V("tt", [K["vt"], al, K["d16"]], T.VD[:, :], T.VT[:, 0:64].indirect(L("AL", t, 0, 8)), T.D16[:, :], A.mult)
+        return V("tt", [K["vt"], al, K["d16"]], T.VDB[:, :], T.VT[:, 0:64].indirect(L("AL", t, 0, 8)), T.D16B[:, 0:128], A.mult)
+
+    def run(vd):
+        return V("scan", [vd, K["r16"]], T.VEB[:, :], T.RS16B[:, 0:128], T.VDB[:, :], 0.0, A.mult, A.add)
 
     def depart(t, al, held):
         c, s = T["cRW%d" % t], T["sRW%d" % t]
-        p2 = S(T["sSD%d" % t][:, 0:96], s[:, 128:192].indirect(L("AL", t, 0, 6)), [al] + held)
-        p1 = V("copy", [al] + held, wd(T["cSD%d" % t], 0, 96), wd(c, 128, 192).indirect(L("AL", t, 0, 6)))
+        p2 = S(T["sSD%d" % t][:, 0:96], s[:, 128:192].indirect(L("AL", t, 0, 6)), [al, held[-1]])
+        p1 = V("copy", [al, held[0]], wd(T["cSD%d" % t], 0, 96), wd(c, 128, 192).indirect(L("AL", t, 0, 6)))
         sendcols("aq%d" % t, "LA%d" % t, "SD%d" % t, [p1, p2])
-        return S(T["sLA%d" % t][:, 96:128], s[:, 128:192].indirect(L("AL", t, 6, 8)), [al] + held)
+        return S(T["sLA%d" % t][:, 96:128], s[:, 128:192].indirect(L("AL", t, 6, 8)), [al, held[-1]])
 
-    def tell(t, al, vd, held, o2):
-        o1 = V("copy", [al] + held, wd(T["cLA%d" % t], 96, 128), wd(T["cRW%d" % t], 128, 192).indirect(L("AL", t, 6, 8)))
-        ve = V("scan", [vd, K["r16"]], T.VE[:, :], T.RS16[:, :], T.VD[:, :], 0.0, A.mult, A.add)
-        vs = V("ts", [ve], L("VS", t, 0, 8), T.VE[:, 15:128:16], 4.0, None, A.mult)
+    def mine32(t, al, held):
+        return V("copy", [al, held[0]], wd(T["cLA%d" % t], 96, 128), wd(T["cRW%d" % t], 128, 192).indirect(L("AL", t, 6, 8)))
+
+    def tell(t, ve):
+        vs = V("ts", [ve], L("VS", t, 0, 8), T.VEB[:, 15:128:16], 4.0, None, A.mult)
         send("av", t, "VL", "VS", [vs])
-        return [o1, o2], vs
+        return vs
 
     def eq(b):
         return T.cEQ[:, 128 * b:128 * b + 128], T.sEQ[:, 128 * b:128 * b + 128]
@@ -249,18 +259,24 @@ def rank_program(g, core, T, topo):
         LA, sLA = T["cLA%d" % t], T["sLA%d" % t]
         land = [("aq%d" % t, COLS)] + own + [K["kq"]]
         z = []
-        for i in range(3):
+
+        def zout(i):
+            n = CUTS[i + 1] - CUTS[i]
+            return T.pz[:, 512 * i:512 * i + n] if i < 3 else T.px[:, 0:n]
+
+        for i in range(4):
             a, b = CUTS[i], CUTS[i + 1]
-            z.append(MM(T.pz[:, 512 * i:512 * i + b - a], LA[:, 0:128], sLA[:, 0:128], KQ[:, a:b], sKQ[:, a:b], True, True, land + [prev["z"][i]]))
+            z.append(MM(zout(i), LA[:, 0:128], sLA[:, 0:128], KQ[:, a:b], sKQ[:, a:b], True, True, land + [prev["z"][i]]))
 
         def zcopy(i):
-            return T.ZS[:, CUTS[i]:CUTS[i + 1]], T.pz[:, 512 * i:512 * i + CUTS[i + 1] - CUTS[i]]
+            return T.ZS[:, CUTS[i]:CUTS[i + 1]], zout(i)
 
         def half(b):
             return MM(T.pv[:, 512 * b:512 * b + 128], *eq(b), LA[:, 0:128], sLA[:, 0:128], True, t > 0, [K["eq"], prev["pv"][b]])
 
         dq = [half(b) for b in range(2)]
         c0 = S(*zcopy(0), [z[0], prev["t64"]])
+        c2 = S(*zcopy(2), [z[2]])
         if t > 0:
             d = [S(T.DQ[:, 128 * b:128 * b + 128], T.pv[:, 512 * b:512 * b + 128], [dq[b], prev["ht"]]) for b in range(2)]
         aside(3)
@@ -272,16 +288,15 @@ def rank_program(g, core, T, topo):
         vp = V("red", [b8], T.VP[:, 0:1], T.T8[:, :], AxisListType.X, A.add)
         c1 = V("copy", [z[1]], *zcopy(1))
         z4 = V("ts", [vp, i_io4], L("Z4", t, 0, 4), T.IO4[:, 0:4], T.VP[:, 0:1], None, A.add)
-        c2 = V("copy", [z[2]], *zcopy(2))
-        t64 = V("tt", [c0, c1, c2, z4, K["nm"]], T.T64[:, :], T.ZS[:, 0:512].indirect(L("Z4", t, 0, 4)), T.NM64[:, :], A.add)
+        c3 = V("copy", [z[3]], *zcopy(3))
+        t64 = V("tt", [c0, c1, c2, c3, z4, K["nm"]], T.T64[:, :], T.ZS[:, 0:512].indirect(L("Z4", t, 0, 4)), T.NM64[:, :], A.add)
         step()
-        rm = V("scan", [t64], T.RM[:, :], T.T64[:, :], T.T64[:, :], -BIG, A.max, A.max)
+        rm = V("scan", [t64], T.RM[:, 8:72], T.T64[:, :], T.T64[:, :], -BIG, A.max, A.max)
         step()
-        for u in range(3):
-            xs = V("ts", [rm, K["xs"], K["nk"]], T.XS[:, u:32:4], T.NMK[:, :], T.RM[:, 16 * u + 15:16 * u + 16], T.RM[:, 63:64], A.add, A.is_lt)
+        xs = V("ts", [rm, x_m, K["xs"], K["xl"]], T.XS[:, 0:32], T.RM[:, 0:56].indirect(T.XL[:, 0:2]), T.RM[:, 71:72], None, A.is_lt)
         step()
         xq = V("q", [xs, prev["xm"]], T.cXQ[:, 0:128], T.sXQ[:, 0:128], T.XS[:, :])
-        xm = MM(T.px[:, 0:128], T.cSQ[:, 0:128], T.sSQ[:, 0:128], T.cXQ[:, 0:128], T.sXQ[:, 0:128], True, True, [xq, K["sq"], prev["of"]])
+        xm = MM(T.px[:, 0:128], T.cSQ[:, 0:128], T.sSQ[:, 0:128], T.cXQ[:, 0:128], T.sXQ[:, 0:128], True, True, [xq, K["sq"], c3])
         dq += [half(b) for b in range(2, 4)]
         aside(0)
         step()
@@ -297,9 +312,9 @@ def rank_program(g, core, T, topo):
         step()
         if t == 0:
             ks = S(T.sKC[:, 0:128], sKQ[:, 0:512].indirect(L("OU", t, 0, 8)), [ou, K["kq"]])
-            nd = V("tt", [ou, K["t3"], K["d16"]], T.VD[:, :], T.NXA[:, 1536:2048].indirect(L("OU", t, 0, 8)), T.D16[:, :], A.mult)
+            nd = V("tt", [ou, K["t3"], K["db"]], T.VD[:, :], T.NXA[:, 1536:2048].indirect(L("OU", t, 0, 8)), T.D16[:, :], A.mult)
             kc = V("copy", [ou], wd(T.cKC, 0, 128), wd(KQ, 0, 512).indirect(L("OU", t, 0, 8)))
-            ne = V("scan", [nd], T.VE[:, :], T.RS16[:, :], T.VD[:, :], 0.0, A.mult, A.add)
+            ne = V("scan", [nd, K["r16f"]], T.VE[:, :], T.RS16[:, :], T.VD[:, :], 0.0, A.mult, A.add)
             told = V("ts", [ne], L("OR", t, 0, 8), T.VE[:, 15:128:16], float(-off), None, A.add)
             send("rc", t, "CL", "OR", [told])
             aside(1)
@@ -326,37 +341,41 @@ def rank_program(g, core, T, topo):
         C, P = T["cNW%d" % t], T["sNW%d" % t]
         nq = V("q", ready, C[:, 0:128], P[:, 0:128], T.HT[:, :])
         sendcols("rq%d" % t, "RW%d" % t, "NW%d" % t, [nq])
-        prev.update({"z": [c0, c1, c2], "pv": h, "t64": t64, "ht": ht, "xm": xm, "of": of, "nq": nq})
-        w1 = V("copy", [nq, K["id"]], wd(T["cRW%d" % t], 96, 128), wd(C, 96, 128).indirect(T.IDL[:, 0:2]))
-        w2 = S(T["sRW%d" % t][:, 96:128], P[:, 96:128].indirect(T.IDL[:, 0:2]), [nq, K["id"]])
+        prev.update({"z": [c0, c1, c2, of], "pv": h, "t64": t64, "ht": ht, "xm": xm, "of": of, "nq": nq})
+        w1 = V("copy", [nq, K["idl"]], wd(T["cRW%d" % t], 96, 128), wd(C, 96, 128).indirect(T.IDL[:, 0:2]))
+        w2 = S(T["sRW%d" % t][:, 96:128], P[:, 96:128].indirect(T.IDL[:, 0:2]), [nq, K["idl"]])
         aside(2)
         return [w1, w2], ou, told
 
     def where(t):
-        u = V("tt", [], T.UU[:, :], T.PX[:, :], T.MK[:, :], A.mult)
-        q1 = V("ts", [], T.Q1[:, :], T.BT[:, :], 32.0, None, A.mult)
-        u = V("tt", [u], T.U2[:, :], T.UU[:, 0:128], T.UU[:, 128:256], A.add)
-        q2 = V("tt", [q1, i_na], T.Q2[:, :], T.Q1[:, :], T.NA[:, :], A.add)
-        p = V("tt", [u], T.PP[:, :], T.U2[:, 0:64], T.U2[:, 64:128], A.add)
+        md = V("scan", [K["db"]], T.MD[:, :], T.MK[:, :], T.D16B[:, :], 0.0, A.max, A.mult)
         yield None
-        sv = V("ts", [p], T.SV[:, :], T.PP[:, :], float(CAP), None, A.is_le)
-        q3 = V("tt", [q2, p], T.Q3[:, :], T.Q2[:, :], T.PP[:, :], A.add)
+        ud = V("scan", [md], T.UD[:, :], T.PX[:, :], T.MD[:, :], 0.0, A.max, A.mult)
         yield None
-        q4 = V("tt", [sv], T.Q4[:, :], T.SV[:, :], T.D16[:, 0:64], A.mult)
+        ff = V("scan", [ud, K["r16"]], T.FF[:, :], T.RS16B[:, :], T.UD[:, :], 0.0, A.mult, A.add)
         yield None
-        q5 = V("tt", [q3, q4], T.Q5[:, :], T.Q3[:, :], T.Q4[:, :], A.mult)
+        w = T.FF[:, 15:256:16]
+        w1 = V("ts", [ff], T.WW[:, 0:16], w, float(CAP), None, A.is_le)
+        w2 = V("ts", [ff], T.WW[:, 16:32], w, 0.0, None, A.is_gt)
+        w3 = V("tt", [ff, K["c16"]], T.WW[:, 32:48], w, T.C16[:, :], A.add)
         yield None
-        q6 = V("scan", [q5], T.Q6[:, :], T.RS16[:, 0:64], T.Q5[:, :], 0.0, A.mult, A.add)
+        w4 = V("tt", [w1, w2], T.WW[:, 48:64], T.WW[:, 0:16], T.WW[:, 16:32], A.mult)
         yield None
-        q7 = V("tt", [q6, K["aw"]], T.Q7[:, :], T.Q6[:, 15:64:16], T.AW[:, :], A.add)
+        w5 = V("tt", [w4, w3], T.WW[:, 64:80], T.WW[:, 48:64], T.WW[:, 32:48], A.mult)
         yield None
-        K["sl"] = V("copy", [q7], L("SL", t, 0, 4), T.Q7[:, :])
+        w6 = V("tt", [w5], T.WW[:, 80:88], T.WW[:, 64:72], T.WW[:, 72:80], A.add)
+        yield None
+        w7 = V("tt", [w6], T.WW[:, 88:92], T.WW[:, 80:84], T.WW[:, 84:88], A.add)
+        yield None
+        w8 = V("tt", [w7, K["aw"]], T.WW[:, 92:96], T.WW[:, 88:92], T.AW[:, :], A.add)
+        yield None
+        K["sl"] = V("copy", [w8], L("SL", t, 0, 4), T.WW[:, 92:96])
         while True:
             yield None
 
-    def order(t, deps, c, s, o):
-        h2 = S(s[:, o:o + 64], T["sRW%d" % t][:, 0:192].indirect(L("SL", t, 0, 4)), deps)
-        h1 = V("copy", deps, wd(c, o, o + 64), wd(T["cRW%d" % t], 0, 192).indirect(L("SL", t, 0, 4)))
+    def order(t, held, back, deps, c, s, o):
+        h2 = S(s[:, o:o + 64], T["sRW%d" % t][:, 0:192].indirect(L("SL", t, 0, 4)), [held[-1], back[1]] + deps)
+        h1 = V("copy", [held[0], back[0]] + deps, wd(c, o, o + 64), wd(T["cRW%d" % t], 0, 192).indirect(L("SL", t, 0, 4)))
         return [h1, h2]
 
     def table(b):
@@ -364,6 +383,9 @@ def rank_program(g, core, T, topo):
 
     def dkc(b):
         K["dk"].append(S(T.DK[:, 512 * b:512 * b + 512], T.pv[:, 512 * b:512 * b + 512], [K["um"][b]]))
+
+    for b in range(4):
+        m_e = S(T.ET[:, 512 * b:512 * b + 512], T.RS64[:, :], [m_rs], 0.0, 0.0)
 
     k_st = V("copy", [d_st], T.STU[:, :], T.STW[:, :])
     start = T.NODI[:, 0:512].indirect(T.STU[:, 0:4])
@@ -373,63 +395,78 @@ def rank_program(g, core, T, topo):
         if k == 0:
             K["node"] = V("copy", [], T.NN0[:, 128:192], start)
         if k == 1:
-            K["r16"] = V("set", [m_r16], T.RS16[:, 0:128:16], 0.0)
+            K["r16"] = V("set", [m_r16], T.RS16B[:, 0:256:16], 0.0)
+            K["jpa"] = V("ts", [i_jp], T.JPA[:, :], T.JP[:, :], 15, None, A.bitwise_and)
         if k == 2:
+            K["r16f"] = V("set", [m_r16f], T.RS16[:, 0:128:16], 0.0)
             K["vt"] = V("ts", [K["node"]], T.VT[:, :], T.NN0[:, 128:192], 127, None, A.bitwise_and)
         if k == 3:
             K["held"] = [V("q", [d_x, m_xt], T.cRW0[:, 128:256], T.sRW0[:, 128:256], T.XT[:, :])]
+        if k == 4:
+            K["d16"] = V("ts", [K["jpa"]], T.D16B[:, 0:128], T.JPA[:, :], 0.0, None, A.is_equal)
+        if k == 5:
+            K["xl"] = V("copy", [x_e], T.XL[:, 0:2], T.XF[:, 2:4])
+            K["id"] = V("ts", [i_jp], T.ID[:, :], T.JP[:, :], 0.0, 0.5, A.is_equal, A.mult)
 
     al = lists(0, bt, gap0)
     held, node = K["held"], K["node"]
     hq0 = held[0]
     o2 = depart(0, al, held)
     vd = diag(0, al)
-    own, vs = tell(0, al, vd, held, o2)
-    i_na = IOTA(T.NA[:, :], [[-1, 64]], -129, 0, True)
-    i_k16 = IOTA(T.K16[:, 0:4], [[16, 4]], 0, 0)
+    o1 = mine32(0, al, held)
+    vs = tell(0, run(vd))
+    own = [o1, o2]
+    i_io4 = IOTA(T.IO4[:, 0:4], [[1, 4]], 0, 0)
+    i_16 = IOTA(T.IO[:, :], [[32, 4], [-16, 4]], -129, 0, True)
+    i_k16 = IOTA(T.IO4[:, 4:8], [[16, 4]], 0, 0)
     i_tb = IOTA(T.TB[:, 0:6], [[-512, 3], [0, 2]], 1024, 0, True)
-    for b in range(2, 4):
-        k_e = S(T.ET[:, 512 * b + b:512 * b + 512:4], T.ID[:, :], [m_e, k_id])
+    K["xs"] = IOTA(T.XS[:, :], [[0, 512]], 0, 0, True)
+    K["nf"] = IOTA(T.NODF[:, :], [[1, 512]], off, 0, True)
+    S(T.D16[:, :], T.D16B[:, 0:128], [K["d16"]])
+    K["db"] = S(T.D16B[:, 128:256], T.D16B[:, 0:128], [K["d16"]])
     for b in range(4):
-        k_s = S(T.ST[:, b:512:4], T.D16[:, :], [K["d16"]])
+        k_e = S(T.ET[:, 512 * b + b:512 * b + 512:4], T.ID[:, :], [m_e, K["id"]])
+    for b in range(4):
+        k_s = S(T.ST[:, b:512:4], T.D16B[:, 0:128], [K["d16"]])
     K["kq"] = V("q", [d_ky], T.cKQ[:, 0:512], T.sKQ[:, 0:512], T.KT[:, :])
+    find = where(0)
+    next(find)
     k_kp = V("ts", [i_kp], T.KP2[:, :], T.KP[:, :], 4, None, A.arith_shift_right)
-    K["nm"] = V("ts", [K["d16"]], T.NM64[:, :], T.D16[:, 0:64], -1.0, BIG, A.add, A.mult)
+    K["nm"] = V("ts", [K["d16"]], T.NM64[:, :], T.D16B[:, 0:64], -1.0, BIG, A.add, A.mult)
+    next(find)
     K["m8"] = V("ts", [k_kp], T.M8[:, :], T.KP2[:, :], 0.0, None, A.is_equal)
-    K["nk"] = V("ts", [k_kp], T.NMK[:, :], T.KP2[:, :], 0.0, BIG, A.not_equal, A.mult)
-    K["nf"] = V("copy", [i_ni], T.NODF[:, :], T.NODI[:, :])
+    K["c16"] = V("ts", [i_16, k_t0], T.C16[:, :], T.IO[:, :], T.THR[:, 0:1], None, A.subtract)
+    next(find)
     K["no"] = V("copy", [d_no], T.NXU[:, 96:128], T.NXV[:, :])
-    K["xs"] = V("set", [], T.XS[:, :], 0.0)
     K["eq"] = V("q", [k_e], T.cEQ[:, 0:512], T.sEQ[:, 0:512], T.ET[:, :])
-    K["t3"] = table(3)
     K["sq"] = V("q", [k_s], T.cSQ[:, 0:128], T.sSQ[:, 0:128], T.ST[:, :])
     for b in range(3):
         for k in range(8):
             d_nx = DMA("y", "dnx", T.NXW[16 * k:16 * k + 16, 32 * b:32 * b + 32], T["NXR%d" % b][:, :], [("nxr", 3 * len(e16))])
     DMA("y", "dh3", by(T.cHQ3, 64, 128), by(T.cRW0, 192, 256), [hq0])
     d_h3 = DMA("y", "dh3", T.sHQ3[:, 64:128], T.sRW0[:, 192:256], [hq0])
-    find = where(0)
-    next(find)
 
     def aside0(k):
+        if k == 3:
+            K["t3"] = table(3)
         if k == 0:
-            K["id"] = V("ts", [k_t0, i_k16], T.IDL[:, :], T.K16[:, 0:2], T.THR[:, 0:1], None, A.add)
-            K["aw"] = V("ts", [k_t0, i_k16], T.AW[:, :], T.K16[:, 0:4], T.THR[:, 0:1], 128.0, A.add, A.add)
+            K["idl"] = V("ts", [k_t0, i_k16], T.IDL[:, :], T.IO4[:, 4:6], T.THR[:, 0:1], None, A.add)
+            K["aw"] = V("ts", [k_t0, i_k16], T.AW[:, :], T.IO4[:, 4:8], T.THR[:, 0:1], 128.0, A.add, A.add)
         if k == 2:
+            K["nu"] = V("copy", [d_nx], T.NXU[:, 0:96], T.NXW[:, :])
             K["dk"] = []
             K["um"] = [MM(T.pv[:, 512 * b:512 * b + 512], *eq(b), T.cKQ[:, 0:512], T.sKQ[:, 0:512], True, True, [prev["pv"][b]]) for b in range(4)]
             for b in range(2):
                 dkc(b)
+            K["nxa"] = [K["t3"], table(0)]
 
     def aside1(k):
         if k == 3:
-            K["nxa"].append(table(1))
-        if k == 1:
             K["nxa"].append(table(2))
         if k == 2:
             K["wq"] = V("q", [d_w], T.cWQ[:, 0:128], T.sWQ[:, 0:128], T.WT[:, :])
 
-    prev = {"z": [None] * 3, "pv": [None] * 4, "t64": None, "ht": None, "xm": None, "of": None, "nq": None}
+    prev = {"z": [None] * 4, "pv": [None] * 4, "t64": None, "ht": None, "xm": None, "of": None, "nq": None}
     for t in range(HOPS):
         n = T["NN%d" % t]
         if t == 0:
@@ -439,11 +476,12 @@ def rank_program(g, core, T, topo):
             find = where(t)
             next(find)
             if t == 1:
-                K["nu"] = V("copy", [d_nx], T.NXU[:, 0:96], T.NXW[:, :])
-                for b in range(2, 4):
-                    dkc(b)
+                dkc(2)
+                K["dk"].append(V("copy", [K["um"][3]], T.DK[:, 1536:2048], T.pv[:, 1536:2048]))
                 prev["pv"] = K["dk"]
-                K["nxa"] = [K["t3"], table(0)]
+                K["nxa"].append(table(1))
+            next(find)
+            next(find)
             back, ou, told = server(t, own, vs, prev, aside1 if t == 1 else lambda k: None, lambda: next(find))
             mine, theirs, tabs = T.NXA[:, 1536:2048].indirect(L("OU", t, 6, 8)), T.NXA[:, 0:1536].indirect(L("CL", t, 0, 6)), [ou] + K["nxa"]
         sl = K["sl"]
@@ -451,7 +489,7 @@ def rank_program(g, core, T, topo):
         V("ts", [node], T.ND[:, 64 * t:64 * t + 64], n[:, 128:192], float(-off), None, A.add)
         g1 = V("copy", [("rc%d" % t, LIST)], n[:, 0:96], theirs)
         byq = n[:, 0:192].indirect(L("SL", t, 0, 4))
-        got = held + back + [sl, ("rq%d" % t, COLS)]
+        got = [sl, ("rq%d" % t, COLS)]
 
         def nodes():
             return V("copy", [g1, sl, node], T["NN%d" % (t + 1)][:, 128:192], byq)
@@ -460,22 +498,26 @@ def rank_program(g, core, T, topo):
             node = nodes()
             nd = V("ts", [node], T.ND[:, 64 * HOPS:64 * HOPS + 64], T["NN%d" % HOPS][:, 128:192], float(-off), None, A.add)
             DMA("y", "dout", T.nd[:, :], T.ND[0:1, 0:256], [nd])
-            hq = order(t, got, T.cHQ3, T.sHQ3, 0)
+            hq = order(t, held, back, got, T.cHQ3, T.sHQ3, 0)
             break
         bt = V("ts", [g1, sl, node], T.BT[:, :], byq, 7, 3, A.logical_shift_right, A.bitwise_and)
 
         def gap(k):
             if k == 0:
-                K["vt"] = V("ts", [g1, sl, node], T.VT[:, :], byq, 127, None, A.bitwise_and)
-            if k == 1:
                 K["node"] = nodes()
+            if k == 2:
+                K["vt"] = V("ts", [K["node"]], T.VT[:, :], T["NN%d" % (t + 1)][:, 128:192], 127, None, A.bitwise_and)
+            if k == 5:
+                K["held"] = order(t, held, back, got, T["cRW%d" % (t + 1)], T["sRW%d" % (t + 1)], 128)
 
         al = lists(t + 1, bt, gap)
-        node = K["node"]
-        vd = diag(t + 1, al)
-        held = order(t, got, T["cRW%d" % (t + 1)], T["sRW%d" % (t + 1)], 128)
+        held, node = K["held"], K["node"]
         o2 = depart(t + 1, al, held)
-        own, vs = tell(t + 1, al, vd, held, o2)
+        vd = diag(t + 1, al)
+        ve = run(vd)
+        o1 = mine32(t + 1, al, held)
+        vs = tell(t + 1, ve)
+        own = [o1, o2]
 
     DMA("y", "dout", T.oc[:, :], by(T.cHQ3, 0, 64), [hq[0]])
     for k in range(4):

from concourse.bass import DstId, RemoteDMATransfer
from concourse.mybir import dt, AluOpType as A, AxisListType, ActivationFunctionType as F

NR, CAP, HOPS = 4, 32, 3
BIG = 1e29
CUTS = (0, 128, 256, 384, 512)

SCRATCH = {
    "STW": ("sbuf", [128, 4], "int32"), "STU": ("sbuf", [128, 4], "uint16"),
    "NXD": ("dram", [128, 4], "int32"), "NXR0": ("dram", [128, 4], "int32"), "NXR1": ("dram", [128, 4], "int32"), "NXR2": ("dram", [128, 4], "int32"),
    "NXW": ("sbuf", [128, 96], "int32"), "NXV": ("sbuf", [128, 32], "int32"), "NXU": ("sbuf", [128, 128], "uint16"), "NXA": ("sbuf", [128, 2048], "float32"),
    "NODF": ("sbuf", [128, 512], "float32"), "NODI": ("sbuf", [128, 512], "int32"),
    "JP": ("sbuf", [128, 128], "int32"), "JPA": ("sbuf", [128, 128], "int32"), "ID": ("sbuf", [128, 128], "bfloat16"),
    "PI": ("sbuf", [128, 8], "int32"), "THR": ("sbuf", [128, 8], "float32"),
    "KP": ("sbuf", [128, 8], "int32"), "KP2": ("sbuf", [128, 8], "int32"), "M8": ("sbuf", [128, 8], "float32"),
    "XI": ("sbuf", [128, 8], "int32"), "XF": ("sbuf", [128, 8], "float32"), "XL": ("sbuf", [128, 2], "uint16"),
    "IO4": ("sbuf", [128, 8], "int32"), "AW": ("sbuf", [128, 4], "float32"), "IDL": ("sbuf", [128, 2], "uint16"),
    "TB": ("sbuf", [128, 8], "float32"), "IO": ("sbuf", [128, 16], "float32"), "C16": ("sbuf", [128, 16], "float32"),
    "D16": ("sbuf", [128, 128], "float32"), "D16B": ("sbuf", [128, 256], "bfloat16"), "NM64": ("sbuf", [128, 64], "float32"),
    "RS64": ("sbuf", [128, 512], "bfloat16"), "RS16": ("sbuf", [128, 128], "float32"), "RS16B": ("sbuf", [128, 256], "bfloat16"),
    "AL": ("sbuf", [128, 24], "uint16"),
    "VS": ("sbuf", [128, 24], "int32"),
    "VL": ("sbuf", [128, 24], "int32"),
    "Z4": ("sbuf", [128, 24], "uint16"),
    "OU": ("sbuf", [128, 24], "uint16"),
    "OR": ("sbuf", [128, 24], "uint16"),
    "CL": ("sbuf", [128, 24], "uint16"),
    "SL": ("sbuf", [128, 24], "uint16"),
    "BT": ("sbuf", [128, 64], "int32"), "VT": ("sbuf", [128, 64], "int32"), "MK": ("sbuf", [128, 256], "bfloat16"), "PX": ("sbuf", [128, 256], "bfloat16"),
    "CN": ("sbuf", [128, 512], "bfloat16"), "SC": ("sbuf", [128, 512], "bfloat16"), "VD": ("sbuf", [128, 128], "float32"), "VE": ("sbuf", [128, 128], "float32"),
    "VDB": ("sbuf", [128, 128], "bfloat16"), "VEB": ("sbuf", [128, 128], "bfloat16"),
    "MD": ("sbuf", [128, 256], "bfloat16"), "UD": ("sbuf", [128, 256], "bfloat16"), "FF": ("sbuf", [128, 256], "bfloat16"),
    "WW": ("sbuf", [128, 96], "float32"), "ND": ("sbuf", [128, 256], "float32"),
    "VA": ("sbuf", [128, 8], "float32"), "VR": ("sbuf", [128, 8], "float32"), "VP": ("sbuf", [128, 8], "float32"), "T8": ("sbuf", [128, 8], "float32"),
    "ZS": ("sbuf", [128, 512], "float32"), "T64": ("sbuf", [128, 64], "float32"),
    "RM": ("sbuf", [128, 72], "float32"),
    "XS": ("sbuf", [128, 512], "bfloat16"), "OF": ("sbuf", [128, 8], "float32"), "OG": ("sbuf", [128, 8], "float32"), "HT": ("sbuf", [128, 512], "bfloat16"),
    "DK": ("sbuf", [128, 2048], "float32"), "DQ": ("sbuf", [128, 256], "float32"), "GK": ("sbuf", [128, 256], "float32"),
    "XT": ("sbuf", [128, 512], "bfloat16"), "KT": ("sbuf", [128, 2048], "bfloat16"), "WT": ("sbuf", [128, 512], "bfloat16"),
    "ET": ("sbuf", [128, 2048], "bfloat16"), "ST": ("sbuf", [128, 512], "bfloat16"), "YS": ("sbuf", [128, 64], "float32"),
    "pv": ("psum", [128, 2048], "float32"), "pz": ("psum", [128, 1536], "float32"), "px": ("psum", [128, 512], "float32"),
}


def _codes(name, n):
    SCRATCH["c" + name] = ("sbuf", [128, n], "float8_e4m3fn_x4")
    SCRATCH["s" + name] = ("sbuf", [128, n], "uint8")


for _n, _w in (("KQ", 512), ("EQ", 512), ("SQ", 128), ("WQ", 128), ("XQ", 128), ("HQ3", 128), ("KC", 128)):
    _codes(_n, _w)
for _t in range(HOPS):
    for _n, _w in (("SD", 96), ("LA", 128), ("NW", 128), ("RW", 192 if _t else 256)):
        _codes(_n + str(_t), _w)
for _t in range(HOPS + 1):
    SCRATCH["NN%d" % _t] = ("sbuf", [128, 192], "int32")
SEMAPHORES = ["cv", "cs", "ct", "cg", "ls", "dst", "dx", "dno", "dnx", "dnd", "nxr", "dky", "dw", "dh3", "dout"]
for _t in range(HOPS):
    SEMAPHORES += ["aq%d" % _t, "av%d" % _t, "rq%d" % _t, "rc%d" % _t]


def rank_program(g, core, T, topo):
    me = T.rank_of(core)
    if me is None:
        return
    cores = list(T.cores)
    eng = {"v": g.vector, "s": g.scalar, "t": g.tensor, "g": g, "y": g.sync}
    count = {}
    known = {q: {} for q in eng}
    seen = {}

    def need(q, deps):
        for d in deps:
            if d is None:
                continue
            sem, val = d
            if known[q].get(sem, 0) >= val:
                continue
            eng[q].wait_ge(T.sem[sem], int(val))
            known[q][sem] = val
            for k, w in seen.get(d, {}).items():
                if known[q].get(k, 0) < w:
                    known[q][k] = w

    def done(q, ins, sem, n):
        count[sem] = count.get(sem, 0) + n
        ins.then_inc(T.sem[sem], n)
        tok = (sem, count[sem])
        seen[tok] = dict(known[q])
        return tok

    v = g.vector
    getv = {"copy": v.tensor_copy, "tt": v.tensor_tensor, "ts": v.tensor_scalar, "red": v.tensor_reduce, "scan": v.tensor_tensor_scan,
            "set": v.memset, "q": v.quantize_mx}

    def V(name, deps, *args):
        need("v", deps)
        return done("v", getv[name](*args), "cv", 1)

    def S(out, in_, deps, *scale):
        need("s", deps)
        return done("s", g.scalar.activation(out, in_, F.Copy, *scale), "cs", 1)

    def MM(out, lc, ls, rc, rs, start, stop, deps):
        need("t", deps)
        return done("t", g.tensor.matmul_mx(out, lc, ls, rc, rs, start, stop), "ct", 1)

    def DMA(q, sem, out, in_, deps=()):
        need(q, deps)
        return done(q, eng[q].dma_start(out, in_), sem, 16)

    def IOTA(out, pattern, base, cm, f32=False):
        if f32:
            return done("g", g.iota(out, pattern, base, cm, allow_small_or_imprecise_dtypes=True), "cg", 1)
        return done("g", g.iota(out, pattern, base, cm), "cg", 1)

    peers = [(me + 1 + b) % NR for b in range(NR - 1)]

    def part(s, r):
        others = sorted((o for o in range(NR) if o != s), key=lambda o: (topo.die(cores[o]) != topo.die(cores[s]), (o - s) % NR))
        e = topo.engines(cores[s], cores[r])
        q = len(e) // 4
        return (e[:q], e[q:2 * q], e[2 * q:])[others.index(r)]

    def bits(es):
        m = 0
        for i in es:
            m |= 1 << i
        return m

    def coreid(r):
        rid, pid, _ = topo.addr(cores[r])
        return DstId(rid=rid, pnc=pid)

    LIST = sum(len(part(r, me)) for r in peers)
    COLS = 15

    def fused(tr):
        g.remote_dma_fused(tr, local_sem=T.sem.ls)

    def one(r, m, sem, src, dst):
        return RemoteDMATransfer(dst_ids=[coreid(r)], dma_engine_mask=m, remote_sem=T.sem[sem], src=src, dst=dst)

    def send(sem, t, dst, src, deps):
        need("g", deps)
        fused([one(r, bits(part(me, r)), sem + str(t), L(src, t, 2 * b, 2 * b + 2), L(dst, t, 2 * ((me - r - 1) % NR), 2 * ((me - r - 1) % NR) + 2))
               for b, r in enumerate(peers)])
        count["ls"] = count.get("ls", 0) + sum(len(part(me, r)) for r in peers)

    def by(x, a, b):
        return x[:, a:b].bitcast(dt.uint8)

    def sendcols(sem, dst, src, deps):
        C, P, DC, DP = T["c" + src], T["s" + src], T["c" + dst], T["s" + dst]
        need("g", deps)
        tr = []
        for b, r in enumerate(peers):
            e = topo.engines(core, cores[r])[5 * b:5 * b + 5]
            o = 32 * ((me - r - 1) % NR)
            i = 32 * b
            for k in range(4):
                tr.append(one(r, 1 << e[k], sem, by(C, i + 8 * k, i + 8 * k + 8), by(DC, o + 8 * k, o + 8 * k + 8)))
            tr.append(one(r, 1 << e[4], sem, P[:, i:i + 32], DP[:, o:o + 32]))
        fused(tr)
        count["ls"] = count.get("ls", 0) + 15

    def wd(x, a, b):
        return x[:, a:b].bitcast(dt.uint32)

    def L(name, t, a, b, step=1):
        return T[name][:, 8 * t + a:8 * t + b:step]

    off = 128 * (NR - 1 - me)
    K = {}

    for k in range(8):
        d_st = DMA("y" if k % 2 == 0 else "s", "dst", T.STW[16 * k:16 * k + 16, 0:4], T.st[:, :])
    d_nd = DMA("s", "dnd", T.NXD[:, :], T.nx[:, :])
    d_x = DMA("y", "dx", T.XT[:, 0:256], T.x[:, :])
    d_ky = DMA("s", "dky", T.KT[:, 0:1024], T.ky[:, 0:1024])
    d_ky = DMA("y", "dky", T.KT[:, 1024:2048], T.ky[:, 1024:2048])
    for k in range(8):
        d_no = DMA("y", "dno", T.NXV[16 * k:16 * k + 16, 0:32], T.nx[:, :])
    d_w = DMA("y", "dw", T.WT[:, :], T.w[:, :])

    i_pi = IOTA(T.PI[:, 0:1], [[0, 1]], 0, 1)
    i_ni = IOTA(T.NODI[:, :], [[1, 512]], off, 0)
    i_jp = IOTA(T.JP[:, :], [[1, 128]], 0, -1)
    i_kp = IOTA(T.KP[:, :], [[-16, 8]], 0, 1)
    need("g", [d_nd])
    e16 = topo.engines(core, cores[peers[0]])
    fused([RemoteDMATransfer(dst_ids=[coreid(r) for r in peers], dma_engine_mask=bits(e16), remote_sem=T.sem.nxr, srcs=[T.NXD[:, :]],
                             dsts=[T["NXR%d" % ((me - r - 1) % NR)][:, :] for r in peers])])
    count["ls"] = len(e16)

    m_rs = V("set", [], T.RS64[:, :], 1.0)
    k_pj = V("ts", [i_pi], T.XI[:, 4:5], T.PI[:, 0:1], 15, None, A.bitwise_and)
    m_rs = V("set", [m_rs], T.RS64[:, 0:512:64], 0.0)
    k_t0 = V("ts", [k_pj], T.THR[:, 0:1], T.XI[:, 4:5], 0.0, None, A.add)
    k_t1 = V("ts", [k_pj], T.THR[:, 1:2], T.XI[:, 4:5], 16.0, None, A.add)
    k_th = [k_t0, k_t1]
    x_a = V("ts", [k_pj], T.XI[:, 0:1], T.XI[:, 4:5], 2, None, A.arith_shift_right)
    x_u = V("ts", [i_pi], T.XI[:, 3:4], T.PI[:, 0:1], 1.0, None, A.add)
    x_g = V("ts", [i_pi], T.XI[:, 2:3], T.PI[:, 0:1], 4, None, A.arith_shift_right)
    x_b = V("ts", [x_a], T.XI[:, 1:2], T.XI[:, 0:1], 4.0, None, A.add)
    x_u = V("ts", [x_u], T.XI[:, 5:6], T.XI[:, 3:4], 3, None, A.bitwise_and)
    x_g = V("copy", [x_g], T.XF[:, 0:1], T.XI[:, 2:3])
    x_m = V("set", [], T.RM[:, 0:8], BIG)
    x_u = V("ts", [x_u], T.XF[:, 1:2], T.XI[:, 5:6], 16.0, 7.0, A.mult, A.add)
    m_xt = V("set", [], T.XT[:, 256:512], 0.0)
    m_r16 = V("set", [], T.RS16B[:, :], 1.0)
    m_r16f = V("set", [], T.RS16[:, :], 1.0)
    x_e = V("ts", [x_b, x_g, x_u], T.XF[:, 2:4], T.XI[:, 0:2], T.XF[:, 0:1], T.XF[:, 1:2], A.is_equal, A.mult)

    def lists(t, bt, gap):
        gap(0)
        mk = []
        for b in range(4):
            mk.append(V("ts", [bt], T.MK[:, 64 * b:64 * b + 64], T.BT[:, :], float(b), None, A.is_equal))
        gap(1)
        px = [V("scan", [mk[2 * h + 1], m_rs], T.PX[:, 128 * h:128 * h + 128], T.RS64[:, 0:128], T.MK[:, 128 * h:128 * h + 128], 0.0, A.mult, A.add)
              for h in range(2)]
        gap(2)
        cn = [V("ts", [px[1], k_th[h]], T.CN[:, 256 * h:256 * h + 256], T.PX[:, :], T.THR[:, h:h + 1], None, A.is_le) for h in range(2)]
        gap(3)
        sc = [V("scan", [cn[h]], T.SC[:, 256 * h:256 * h + 256], T.RS64[:, 0:256], T.CN[:, 256 * h:256 * h + 256], 0.0, A.mult, A.add) for h in range(2)]
        gap(4)
        for h in range(2):
            al = V("ts", [sc[h]], L("AL", t, h, 8, 2), T.SC[:, 256 * h + 63:256 * h + 256:64], 63.0, None, A.min)
        gap(5)
        return al

    def diag(t, al):
        return V("tt", [K["vt"], al, K["d16"]], T.VDB[:, :], T.VT[:, 0:64].indirect(L("AL", t, 0, 8)), T.D16B[:, 0:128], A.mult)

    def run(vd):
        return V("scan", [vd, K["r16"]], T.VEB[:, :], T.RS16B[:, 0:128], T.VDB[:, :], 0.0, A.mult, A.add)

    def depart(t, al, held):
        c, s = T["cRW%d" % t], T["sRW%d" % t]
        p2 = S(T["sSD%d" % t][:, 0:96], s[:, 128:192].indirect(L("AL", t, 0, 6)), [al, held[-1]])
        p1 = V("copy", [al, held[0]], wd(T["cSD%d" % t], 0, 96), wd(c, 128, 192).indirect(L("AL", t, 0, 6)))
        sendcols("aq%d" % t, "LA%d" % t, "SD%d" % t, [p1, p2])
        return S(T["sLA%d" % t][:, 96:128], s[:, 128:192].indirect(L("AL", t, 6, 8)), [al, held[-1]])

    def mine32(t, al, held):
        return V("copy", [al, held[0]], wd(T["cLA%d" % t], 96, 128), wd(T["cRW%d" % t], 128, 192).indirect(L("AL", t, 6, 8)))

    def tell(t, ve):
        vs = V("ts", [ve], L("VS", t, 0, 8), T.VEB[:, 15:128:16], 4.0, None, A.mult)
        send("av", t, "VL", "VS", [vs])
        return vs

    def eq(b):
        return T.cEQ[:, 128 * b:128 * b + 128], T.sEQ[:, 128 * b:128 * b + 128]

    def server(t, own, vs, prev, aside, step):
        KQ, sKQ = T.cKQ, T.sKQ
        LA, sLA = T["cLA%d" % t], T["sLA%d" % t]
        land = [("aq%d" % t, COLS)] + own + [K["kq"]]
        z = []

        def zout(i):
            n = CUTS[i + 1] - CUTS[i]
            return T.pz[:, 512 * i:512 * i + n] if i < 3 else T.px[:, 0:n]

        for i in range(4):
            a, b = CUTS[i], CUTS[i + 1]
            z.append(MM(zout(i), LA[:, 0:128], sLA[:, 0:128], KQ[:, a:b], sKQ[:, a:b], True, True, land + [prev["z"][i]]))

        def zcopy(i):
            return T.ZS[:, CUTS[i]:CUTS[i + 1]], zout(i)

        def half(b):
            return MM(T.pv[:, 512 * b:512 * b + 128], *eq(b), LA[:, 0:128], sLA[:, 0:128], True, t > 0, [K["eq"], prev["pv"][b]])

        dq = [half(b) for b in range(2)]
        c0 = S(*zcopy(0), [z[0], prev["t64"]])
        c2 = S(*zcopy(2), [z[2]])
        if t > 0:
            d = [S(T.DQ[:, 128 * b:128 * b + 128], T.pv[:, 512 * b:512 * b + 128], [dq[b], prev["ht"]]) for b in range(2)]
        aside(3)
        V("tt", [vs, K["m8"]], T.T8[:, 6:8], L("VS", t, 6, 8), T.M8[:, 6:8], A.mult)
        V("copy", [vs], T.VA[:, 6:8], L("VS", t, 6, 8))
        b8 = V("tt", [("av%d" % t, LIST)], T.T8[:, 0:6], L("VL", t, 0, 6), T.M8[:, 0:6], A.mult)
        va = V("copy", [], T.VA[:, 0:6], L("VL", t, 0, 6))
        vr = V("tt", [i_tb], T.VR[:, 0:6], L("VL", t, 0, 6), T.TB[:, 0:6], A.add) if t > 0 else None
        vp = V("red", [b8], T.VP[:, 0:1], T.T8[:, :], AxisListType.X, A.add)
        c1 = V("copy", [z[1]], *zcopy(1))
        z4 = V("ts", [vp, i_io4], L("Z4", t, 0, 4), T.IO4[:, 0:4], T.VP[:, 0:1], None, A.add)
        c3 = V("copy", [z[3]], *zcopy(3))
        t64 = V("tt", [c0, c1, c2, c3, z4, K["nm"]], T.T64[:, :], T.ZS[:, 0:512].indirect(L("Z4", t, 0, 4)), T.NM64[:, :], A.add)
        step()
        rm = V("scan", [t64], T.RM[:, 8:72], T.T64[:, :], T.T64[:, :], -BIG, A.max, A.max)
        step()
        xs = V("ts", [rm, x_m, K["xs"], K["xl"]], T.XS[:, 0:32], T.RM[:, 0:56].indirect(T.XL[:, 0:2]), T.RM[:, 71:72], None, A.is_lt)
        step()
        xq = V("q", [xs, prev["xm"]], T.cXQ[:, 0:128], T.sXQ[:, 0:128], T.XS[:, :])
        xm = MM(T.px[:, 0:128], T.cSQ[:, 0:128], T.sSQ[:, 0:128], T.cXQ[:, 0:128], T.sXQ[:, 0:128], True, True, [xq, K["sq"], c3])
        dq += [half(b) for b in range(2, 4)]
        aside(0)
        step()
        step()
        if t > 0:
            og = V("tt", [xm, vr], T.OG[:, 0:6], T.px[:, 0:6], T.VR[:, 0:6], A.add)
            of = V("tt", [xm, va], T.OF[:, :], T.px[:, 0:8], T.VA[:, :], A.add)
            told = V("copy", [og], L("OR", t, 0, 6), T.OG[:, 0:6])
            send("rc", t, "CL", "OR", [told])
        else:
            of = V("tt", [xm, va], T.OF[:, :], T.px[:, 0:8], T.VA[:, :], A.add)
        ou = V("copy", [of], L("OU", t, 0, 8), T.OF[:, :])
        step()
        if t == 0:
            ks = S(T.sKC[:, 0:128], sKQ[:, 0:512].indirect(L("OU", t, 0, 8)), [ou, K["kq"]])
            nd = V("tt", [ou, K["t3"], K["db"]], T.VD[:, :], T.NXA[:, 1536:2048].indirect(L("OU", t, 0, 8)), T.D16[:, :], A.mult)
            kc = V("copy", [ou], wd(T.cKC, 0, 128), wd(KQ, 0, 512).indirect(L("OU", t, 0, 8)))
            ne = V("scan", [nd, K["r16f"]], T.VE[:, :], T.RS16[:, :], T.VD[:, :], 0.0, A.mult, A.add)
            told = V("ts", [ne], L("OR", t, 0, 8), T.VE[:, 15:128:16], float(-off), None, A.add)
            send("rc", t, "CL", "OR", [told])
            aside(1)
            h = []
            for b in range(4):
                km = MM(T.pv[:, 512 * b:512 * b + 128], *eq(b), T.cKC[:, 0:128], T.sKC[:, 0:128], False, True, [kc, ks])
                o, i = T.HT[:, b:512:4], T.pv[:, 512 * b:512 * b + 128]
                h.append(S(o, i, [km]) if b % 2 == 0 else V("copy", [km], o, i))
            ready = h
            ht = None
        else:
            def chosen(b):
                return T.DK[:, 512 * b:512 * b + 512].indirect(L("OU", t, 0, 8))

            gk = [S(T.GK[:, 128 * b:128 * b + 128], chosen(2 + b), [ou, prev["ht"]] + K["dk"]) for b in range(2)]
            aside(1)
            for b in range(2):
                V("tt", [ou, d[b], prev["nq"]] + K["dk"], T.HT[:, b:512:4], chosen(b), T.DQ[:, 128 * b:128 * b + 128], A.add)
            ready = [V("tt", [dq[2 + b], gk[b]], T.HT[:, 2 + b:512:4], T.pv[:, 512 * (2 + b):512 * (2 + b) + 128], T.GK[:, 128 * b:128 * b + 128], A.add)
                     for b in range(2)]
            h = d + ready
            ht = ready[1]
        step()
        C, P = T["cNW%d" % t], T["sNW%d" % t]
        nq = V("q", ready, C[:, 0:128], P[:, 0:128], T.HT[:, :])
        sendcols("rq%d" % t, "RW%d" % t, "NW%d" % t, [nq])
        prev.update({"z": [c0, c1, c2, of], "pv": h, "t64": t64, "ht": ht, "xm": xm, "of": of, "nq": nq})
        w1 = V("copy", [nq, K["idl"]], wd(T["cRW%d" % t], 96, 128), wd(C, 96, 128).indirect(T.IDL[:, 0:2]))
        w2 = S(T["sRW%d" % t][:, 96:128], P[:, 96:128].indirect(T.IDL[:, 0:2]), [nq, K["idl"]])
        aside(2)
        return [w1, w2], ou, told

    def where(t):
        md = V("scan", [K["db"]], T.MD[:, :], T.MK[:, :], T.D16B[:, :], 0.0, A.max, A.mult)
        yield None
        ud = V("scan", [md], T.UD[:, :], T.PX[:, :], T.MD[:, :], 0.0, A.max, A.mult)
        yield None
        ff = V("scan", [ud, K["r16"]], T.FF[:, :], T.RS16B[:, :], T.UD[:, :], 0.0, A.mult, A.add)
        yield None
        w = T.FF[:, 15:256:16]
        w1 = V("ts", [ff], T.WW[:, 0:16], w, float(CAP), None, A.is_le)
        w2 = V("ts", [ff], T.WW[:, 16:32], w, 0.0, None, A.is_gt)
        w3 = V("tt", [ff, K["c16"]], T.WW[:, 32:48], w, T.C16[:, :], A.add)
        yield None
        w4 = V("tt", [w1, w2], T.WW[:, 48:64], T.WW[:, 0:16], T.WW[:, 16:32], A.mult)
        yield None
        w5 = V("tt", [w4, w3], T.WW[:, 64:80], T.WW[:, 48:64], T.WW[:, 32:48], A.mult)
        yield None
        w6 = V("tt", [w5], T.WW[:, 80:88], T.WW[:, 64:72], T.WW[:, 72:80], A.add)
        yield None
        w7 = V("tt", [w6], T.WW[:, 88:92], T.WW[:, 80:84], T.WW[:, 84:88], A.add)
        yield None
        w8 = V("tt", [w7, K["aw"]], T.WW[:, 92:96], T.WW[:, 88:92], T.AW[:, :], A.add)
        yield None
        K["sl"] = V("copy", [w8], L("SL", t, 0, 4), T.WW[:, 92:96])
        while True:
            yield None

    def order(t, held, back, deps, c, s, o):
        h2 = S(s[:, o:o + 64], T["sRW%d" % t][:, 0:192].indirect(L("SL", t, 0, 4)), [held[-1], back[1]] + deps)
        h1 = V("copy", [held[0], back[0]] + deps, wd(c, o, o + 64), wd(T["cRW%d" % t], 0, 192).indirect(L("SL", t, 0, 4)))
        return [h1, h2]

    def table(b):
        return S(T.NXA[:, 512 * b:512 * b + 512], T.NODF[:, 0:512].indirect(T.NXU[:, 32 * b:32 * b + 32]), [K["no"] if b == 3 else K["nu"], K["nf"]])

    def dkc(b):
        K["dk"].append(S(T.DK[:, 512 * b:512 * b + 512], T.pv[:, 512 * b:512 * b + 512], [K["um"][b]]))

    for b in range(4):
        m_e = S(T.ET[:, 512 * b:512 * b + 512], T.RS64[:, :], [m_rs], 0.0, 0.0)

    k_st = V("copy", [d_st], T.STU[:, :], T.STW[:, :])
    start = T.NODI[:, 0:512].indirect(T.STU[:, 0:4])
    bt = V("ts", [k_st, i_ni], T.BT[:, :], start, 7, 3, A.logical_shift_right, A.bitwise_and)

    def gap0(k):
        if k == 0:
            K["node"] = V("copy", [], T.NN0[:, 128:192], start)
        if k == 1:
            K["r16"] = V("set", [m_r16], T.RS16B[:, 0:256:16], 0.0)
            K["jpa"] = V("ts", [i_jp], T.JPA[:, :], T.JP[:, :], 15, None, A.bitwise_and)
        if k == 2:
            K["r16f"] = V("set", [m_r16f], T.RS16[:, 0:128:16], 0.0)
            K["vt"] = V("ts", [K["node"]], T.VT[:, :], T.NN0[:, 128:192], 127, None, A.bitwise_and)
        if k == 3:
            K["held"] = [V("q", [d_x, m_xt], T.cRW0[:, 128:256], T.sRW0[:, 128:256], T.XT[:, :])]
        if k == 4:
            K["d16"] = V("ts", [K["jpa"]], T.D16B[:, 0:128], T.JPA[:, :], 0.0, None, A.is_equal)
        if k == 5:
            K["xl"] = V("copy", [x_e], T.XL[:, 0:2], T.XF[:, 2:4])
            K["id"] = V("ts", [i_jp], T.ID[:, :], T.JP[:, :], 0.0, 0.5, A.is_equal, A.mult)

    al = lists(0, bt, gap0)
    held, node = K["held"], K["node"]
    hq0 = held[0]
    o2 = depart(0, al, held)
    vd = diag(0, al)
    o1 = mine32(0, al, held)
    vs = tell(0, run(vd))
    own = [o1, o2]
    i_io4 = IOTA(T.IO4[:, 0:4], [[1, 4]], 0, 0)
    i_16 = IOTA(T.IO[:, :], [[32, 4], [-16, 4]], -129, 0, True)
    i_k16 = IOTA(T.IO4[:, 4:8], [[16, 4]], 0, 0)
    i_tb = IOTA(T.TB[:, 0:6], [[-512, 3], [0, 2]], 1024, 0, True)
    K["xs"] = IOTA(T.XS[:, :], [[0, 512]], 0, 0, True)
    K["nf"] = IOTA(T.NODF[:, :], [[1, 512]], off, 0, True)
    S(T.D16[:, :], T.D16B[:, 0:128], [K["d16"]])
    K["db"] = S(T.D16B[:, 128:256], T.D16B[:, 0:128], [K["d16"]])
    for b in range(4):
        k_e = S(T.ET[:, 512 * b + b:512 * b + 512:4], T.ID[:, :], [m_e, K["id"]])
    for b in range(4):
        k_s = S(T.ST[:, b:512:4], T.D16B[:, 0:128], [K["d16"]])
    K["kq"] = V("q", [d_ky], T.cKQ[:, 0:512], T.sKQ[:, 0:512], T.KT[:, :])
    find = where(0)
    next(find)
    k_kp = V("ts", [i_kp], T.KP2[:, :], T.KP[:, :], 4, None, A.arith_shift_right)
    K["nm"] = V("ts", [K["d16"]], T.NM64[:, :], T.D16B[:, 0:64], -1.0, BIG, A.add, A.mult)
    next(find)
    K["m8"] = V("ts", [k_kp], T.M8[:, :], T.KP2[:, :], 0.0, None, A.is_equal)
    K["c16"] = V("ts", [i_16, k_t0], T.C16[:, :], T.IO[:, :], T.THR[:, 0:1], None, A.subtract)
    next(find)
    K["no"] = V("copy", [d_no], T.NXU[:, 96:128], T.NXV[:, :])
    K["eq"] = V("q", [k_e], T.cEQ[:, 0:512], T.sEQ[:, 0:512], T.ET[:, :])
    K["sq"] = V("q", [k_s], T.cSQ[:, 0:128], T.sSQ[:, 0:128], T.ST[:, :])
    for b in range(3):
        for k in range(8):
            d_nx = DMA("y", "dnx", T.NXW[16 * k:16 * k + 16, 32 * b:32 * b + 32], T["NXR%d" % b][:, :], [("nxr", 3 * len(e16))])
    DMA("y", "dh3", by(T.cHQ3, 64, 128), by(T.cRW0, 192, 256), [hq0])
    d_h3 = DMA("y", "dh3", T.sHQ3[:, 64:128], T.sRW0[:, 192:256], [hq0])

    def aside0(k):
        if k == 3:
            K["t3"] = table(3)
        if k == 0:
            K["idl"] = V("ts", [k_t0, i_k16], T.IDL[:, :], T.IO4[:, 4:6], T.THR[:, 0:1], None, A.add)
            K["aw"] = V("ts", [k_t0, i_k16], T.AW[:, :], T.IO4[:, 4:8], T.THR[:, 0:1], 128.0, A.add, A.add)
        if k == 2:
            K["nu"] = V("copy", [d_nx], T.NXU[:, 0:96], T.NXW[:, :])
            K["dk"] = []
            K["um"] = [MM(T.pv[:, 512 * b:512 * b + 512], *eq(b), T.cKQ[:, 0:512], T.sKQ[:, 0:512], True, True, [prev["pv"][b]]) for b in range(4)]
            for b in range(2):
                dkc(b)
            K["nxa"] = [K["t3"], table(0)]

    def aside1(k):
        if k == 3:
            K["nxa"].append(table(2))
        if k == 2:
            K["wq"] = V("q", [d_w], T.cWQ[:, 0:128], T.sWQ[:, 0:128], T.WT[:, :])

    prev = {"z": [None] * 4, "pv": [None] * 4, "t64": None, "ht": None, "xm": None, "of": None, "nq": None}
    for t in range(HOPS):
        n = T["NN%d" % t]
        if t == 0:
            back, ou, told = server(0, own, vs, prev, aside0, lambda: next(find))
            mine, theirs, tabs = T.NODI[:, 0:512].indirect(L("OR", 0, 6, 8)), T.NODI[:, 0:512].indirect(L("CL", 0, 0, 6)), [told]
        else:
            find = where(t)
            next(find)
            if t == 1:
                dkc(2)
                K["dk"].append(V("copy", [K["um"][3]], T.DK[:, 1536:2048], T.pv[:, 1536:2048]))
                prev["pv"] = K["dk"]
                K["nxa"].append(table(1))
            next(find)
            next(find)
            back, ou, told = server(t, own, vs, prev, aside1 if t == 1 else lambda k: None, lambda: next(find))
            mine, theirs, tabs = T.NXA[:, 1536:2048].indirect(L("OU", t, 6, 8)), T.NXA[:, 0:1536].indirect(L("CL", t, 0, 6)), [ou] + K["nxa"]
        sl = K["sl"]
        V("copy", tabs, n[:, 96:128], mine)
        V("ts", [node], T.ND[:, 64 * t:64 * t + 64], n[:, 128:192], float(-off), None, A.add)
        g1 = V("copy", [("rc%d" % t, LIST)], n[:, 0:96], theirs)
        byq = n[:, 0:192].indirect(L("SL", t, 0, 4))
        got = [sl, ("rq%d" % t, COLS)]

        def nodes():
            return V("copy", [g1, sl, node], T["NN%d" % (t + 1)][:, 128:192], byq)

        if t + 1 == HOPS:
            node = nodes()
            nd = V("ts", [node], T.ND[:, 64 * HOPS:64 * HOPS + 64], T["NN%d" % HOPS][:, 128:192], float(-off), None, A.add)
            DMA("y", "dout", T.nd[:, :], T.ND[0:1, 0:256], [nd])
            hq = order(t, held, back, got, T.cHQ3, T.sHQ3, 0)
            break
        bt = V("ts", [g1, sl, node], T.BT[:, :], byq, 7, 3, A.logical_shift_right, A.bitwise_and)

        def gap(k):
            if k == 0:
                K["node"] = nodes()
            if k == 2:
                K["vt"] = V("ts", [K["node"]], T.VT[:, :], T["NN%d" % (t + 1)][:, 128:192], 127, None, A.bitwise_and)
            if k == 5:
                K["held"] = order(t, held, back, got, T["cRW%d" % (t + 1)], T["sRW%d" % (t + 1)], 128)

        al = lists(t + 1, bt, gap)
        held, node = K["held"], K["node"]
        o2 = depart(t + 1, al, held)
        vd = diag(t + 1, al)
        ve = run(vd)
        o1 = mine32(t + 1, al, held)
        vs = tell(t + 1, ve)
        own = [o1, o2]

    DMA("y", "dout", T.oc[:, :], by(T.cHQ3, 0, 64), [hq[0]])
    for k in range(4):
        DMA("s" if k < 2 else "y", "dout", T.osc[4 * k:4 * k + 4, 0:64], T.sHQ3[32 * k:32 * k + 4, 0:64], [hq[1]])
    ym = MM(T.px[:, 0:128], T.cWQ[:, 0:128], T.sWQ[:, 0:128], T.cHQ3[:, 0:128], T.sHQ3[:, 0:128], True, True, hq + [K["wq"], d_h3, prev["of"]])
    yc = V("copy", [ym], T.YS[:, :], T.px[:, 0:64])
    DMA("y", "dout", T.y[:, :], T.YS[:, :], [yc])
    for sem in ("dout", "ls", "cv", "cs", "ct", "cg", "dst", "dx", "dky", "dnx", "dno", "dnd", "dw", "dh3"):
        need("g", [(sem, count[sem])])
